import numpy as np, ml_dtypes
CORES = [2,3,42,43,82,83,122,123]
N = 8
BF = ml_dtypes.bfloat16
def gentries(a):
    return np.ascontiguousarray(a.reshape(8, 16, -1).transpose(0, 2, 1)).reshape(8, -1)
def gtable(e):
    e = np.asarray(e); return np.ascontiguousarray(e.reshape(8, -1, 16).transpose(0, 2, 1)).reshape(128, -1).astype(np.int32)
P, A, M, Q = 32768, 4, 8, 256
S = N * P
def letters(rng, w, n):
    a = np.add.accumulate(w); return np.searchsorted(a[:-1], rng.random(n) * a[-1], side="right")
def places(rng):
    p = rng.integers(0, S + 1, (N, 8, 2, Q)); u = P // 8
    v = rng.integers(0, 8 * N + 1, p.shape) * u + rng.integers(-1, 2, p.shape)
    p = np.sort(np.where(rng.random(p.shape) < 0.25, np.minimum(np.maximum(v, 0), S), p), axis=2)
    k = (8 * np.arange(N)[:, None] + np.arange(8)) * u
    p[:, :, 0, Q - 5] = k; p[:, :, 1, Q - 5] = k + u; p[:, :, :, Q - 4] = S; p[:, :, :, Q - 3] = 0
    p[:, :, 1, Q - 2] = p[:, :, 0, Q - 2]; p[:, :, 0, Q - 1] = 0; p[:, :, 1, Q - 1] = S
    return p
def pack(s, e, p):
    return {"bwt": np.ascontiguousarray(np.asarray(s).reshape(8, N, P).transpose(1, 0, 2)).astype(np.int32), "pats": np.stack([gtable(e[r].reshape(8, M * Q)) for r in range(N)]), "starts": np.stack([gtable(p[r].reshape(8, 2 * Q)) for r in range(N)])}
def bw(t):
    n = len(t); key = np.zeros(n, np.int64); k = 62 // (A - 1).bit_length()
    for i in range(k): key = key * A + np.roll(t, -i)
    while True:
        o = np.argsort(key); ks = key[o]
        v = np.zeros(n, np.int64); v[o[1:]] = np.add.accumulate((ks[1:] != ks[:-1]).astype(np.int64))
        if v.max() == n - 1 or k >= n: break
        key = (v * n + np.roll(v, -k)) * n + np.roll(v, -2 * k); k *= 3
    return t[o - 1]
def setup_inputs(rng):
    s = []; e = rng.integers(0, A, (N, 8, M, Q)); h = Q // 2
    for g in range(8):
        w = np.exp2(rng.integers(0, 4, A)); c = rng.integers(0, A); w[c] += 4 * A
        s.append(np.concatenate([letters(rng, w * np.exp2(rng.integers(0, 3, A)), P) for r in range(N)]))
        e[:, g, :, :h] = np.where(rng.random((N, M, h)) < 0.875, c, e[:, g, :, :h])
    return pack(np.stack(s), e, places(rng))
def setup_inputs_ends(rng):
    i = np.arange(S); s = np.zeros((8, S), np.int64)
    s[0] = i * A // S; s[1] = A - 1 - s[0]; s[2] = i % A; s[3] = rng.integers(0, A - 1, S); s[4] = rng.integers(1, A, S); s[5] = i // P % A
    s[6] = np.where((i % P == 0) | (i % P == P - 1), A - 1, rng.integers(0, A - 1, S)); s[7] = np.where(i == S - 1, A - 1, rng.integers(0, A - 1, S))
    e = rng.integers(0, A, (N, 8, M, Q)); e[..., 0] = 0; e[..., 1] = A - 1; e[..., 2] = 0; e[:, :, 0, 2] = A - 1; e[..., 3] = 0; e[:, :, M - 1, 3] = A - 1
    q = rng.integers(0, N); e[q] = rng.integers(0, A, (8, M, 1)); e[q, 0] = e[q, 0, 0, 0]
    p = places(rng); p[:, :, 0, :4] = 0; p[:, :, 1, :4] = S; p[q, :, 0] = 0; p[q, :, 1] = S
    return pack(s, e, p)
def setup_inputs_one(rng):
    k = (np.arange(8) + rng.integers(0, A)) % A; c = k[None, :, None, None]
    e = np.where(rng.random((N, 8, 1, Q)) < 0.5, c, rng.integers(0, A, (N, 8, M, Q))); e[..., 0] = k[None, :, None]
    return pack(np.repeat(k[:, None], S, axis=1), e, places(rng))
def setup_inputs_text(rng):
    s = []; e = np.zeros((N, 8, M, Q), np.int64); h = Q // 2
    for g in range(8):
        t = np.tile(letters(rng, np.exp2(rng.integers(0, 3, A)), S // 8), 8); t = np.where(rng.random(S) < 0.03125, rng.integers(0, A, S), t); s.append(bw(t))
        e[:, g] = t[(rng.integers(0, S, (N, 1, Q)) + (M - 1 - np.arange(M))[None, :, None]) % S]
    e[..., h:] = np.where(rng.random((N, 8, M, Q - h)) < 0.0625, rng.integers(0, A, (N, 8, M, Q - h)), e[..., h:])
    p = places(rng); p[:, :, 0, :h] = 0; p[:, :, 1, :h] = S
    return pack(np.stack(s), e, p)
def setup_inputs_spread(rng):
    s = np.stack([np.concatenate([letters(rng, np.exp2(-2.0 * rng.permutation(A)), P) for r in range(N)]) for g in range(8)])
    e = np.stack([s[g][rng.integers(0, S, (N, M, Q))] for g in range(8)], axis=1)
    p = places(rng); p[:, :, 1] = np.minimum(p[:, :, 0] + (rng.integers(0, S + 1, (N, 8, Q)) >> rng.integers(0, 20, (N, 8, Q))), S)
    return pack(s, np.where(rng.random((N, 8, 1, Q)) < 0.5, e, rng.integers(0, A, (N, 8, M, Q))), p)
def check_inputs(d):
    bad = [k + " out of range" for k in ("bwt", "pats") if not ((d[k] >= 0) & (d[k] < A)).all()]
    if not ((d["starts"] >= 0) & (d["starts"] <= S)).all(): bad.append("starts out of range")
    p = np.stack([gentries(a) for a in d["starts"]]).reshape(N, 8, 2, Q)
    if (p[:, :, 0] > p[:, :, 1]).any(): bad.append("lo over hi in starts")
    return bad
def reference(bwt, pats, starts):
    s = bwt.transpose(1, 0, 2).reshape(8, S)
    e = np.stack([gentries(pats[r]) for r in range(N)]).reshape(N, 8, M, Q)
    b = np.stack([gentries(starts[r]) for r in range(N)]).reshape(N, 8, 2, Q).astype(np.int64)
    ends = np.zeros((N, 8, 2, Q), np.int64)
    for g in range(8):
        C = np.array([np.count_nonzero(s[g] < c) for c in range(A)]); occ = np.zeros((A, S + 1), np.int64)
        for c in range(A): occ[c, 1:] = np.add.accumulate((s[g] == c).astype(np.int64))
        p = b[:, g]
        for t in range(M):
            c = e[:, g, t][:, None]; p = C[c] + occ[c, p]
        ends[:, g] = p
    return {"y": np.asarray(np.stack([gtable(ends[r].reshape(8, 2 * Q)) for r in range(N)]), np.float32)}

@@ -1,0 +1,440 @@
+import numpy as np
+from concourse.bass import DstId, RemoteDMATransfer
+from concourse.mybir import AluOpType as A, AxisListType, ActivationFunctionType as AF
+
+NPE = 4
+BIG = 2097152
+RND = 12582912.0
+B_T = (0.0, 638.5, 2552.5, 10208.5)
+P0 = "aA0 aA1 aB0 aA2 aB1 vA3 vB2"
+P1 = "aA0 aA1 aB0"
+P2 = "aA2 aB1 aA3 aB2"
+XCQ = "aava"
+XQ = "ava" + "avavavavavavavav" * 2
+
+SCRATCH = {
+    "PP": ("dram", [8, 128, 16], "int32"), "SS": ("dram", [8, 128, 4], "int32"),
+    "PL": ("dram", [8, 128, 16], "int32"), "SL": ("dram", [8, 128, 4], "int32"),
+    "RD": ("dram", [8, 128, 4], "float32"), "FL": ("dram", [8, 128, 4], "float32"),
+    "PSA": ("psum", [128, 2048], "float32"), "PSB": ("psum", [128, 2048], "float32"),
+}
+for _n, _w, _d in (
+        ("D32", 2048, "int32"), ("D", 2048, "bfloat16"), ("CE", 2048, "bfloat16"), ("SEND", 384, "float32"), ("LR", 384, "float32"),
+        ("H", 256, "float32"), ("HM", 256, "float32"), ("LXP", 512, "bfloat16"),
+        ("TA", 2048, "bfloat16"), ("TB", 2048, "bfloat16"), ("CI", 128, "int32"), ("CX", 512, "int32"), ("NS", 512, "float32"),
+        ("S1", 512, "bfloat16"), ("N15", 32, "bfloat16"), ("MK", 512, "float32"), ("BASE", 40, "float32"),
+        ("ONE32", 32, "float32"), ("F", 512, "float32"), ("NI", 512, "int32"), ("DI", 1024, "int32"),
+        ("DB", 2048, "bfloat16"), ("XC", 2048, "bfloat16"), ("X", 16400, "bfloat16"),
+        ("ONE1", 128, "bfloat16"), ("ONE2", 512, "bfloat16"), ("FOUR", 32, "bfloat16"), ("GA", 32, "bfloat16"), ("GB", 32, "bfloat16"),
+        ("ID", 128, "bfloat16"), ("IDP", 128, "bfloat16"), ("IDN", 128, "bfloat16"), ("INI", 128, "bfloat16"), ("CON", 64, "bfloat16"),
+        ("PK", 1024, "bfloat16"), ("TRI", 128, "bfloat16"), ("SEL", 128 * NPE, "bfloat16"),
+        ("SELY", 32, "bfloat16"), ("SELZ", 32, "bfloat16"), ("SELL", 16, "bfloat16"),
+        ("KI", 16, "int32"), ("KF", 48, "float32"), ("G1", 64, "float32"),
+        ("G2", 64, "float32"), ("G3", 64, "float32"), ("G4", 16, "float32"), ("G5", 32, "float32"), ("G6", 8, "float32"), ("IC4", 4, "float32"),
+        ("EM", 8, "float32"), ("EV", 8, "float32"), ("EI", 4, "int32"), ("W", 64, "bfloat16"), ("LW", 16, "bfloat16"),
+        ("OFX", 16, "uint16"), ("OFF", 32, "uint16"), ("OFC", 8, "uint16"), ("PT", 128, "int32"), ("ST", 32, "int32"), ("ST4", 32, "int32"),
+        ("OFP", 128, "uint16"), ("PTB", 128, "bfloat16"), ("LTR", 2048, "bfloat16"), ("AM", 512, "bfloat16"), ("QTB", 512, "bfloat16"),
+        ("RST", 64, "float32"), ("RES", 32, "float32"),
+        ("I0", 16, "int32"), ("J0", 16, "int32"), ("OA0", 16, "uint16"), ("OB0", 16, "uint16"), ("S0", 64, "float32"),
+        ("Z0", 256, "bfloat16"), ("ZL0", 256, "bfloat16"), ("E0", 256, "bfloat16"),
+        ("I1", 16, "int32"), ("J1", 16, "int32"), ("OA1", 16, "uint16"), ("OB1", 16, "uint16"), ("S1B", 64, "float32"),
+        ("Z1", 256, "bfloat16"), ("ZL1", 256, "bfloat16"), ("E1", 256, "bfloat16")):
+    SCRATCH[_n] = ("sbuf", [128, _w], _d)
+SEMAPHORES = (["vq", "aq", "pq", "gq", "dp", "ds", "dsp", "dss", "lpt", "lst", "rep", "yself", "yout", "rd",
+               "arrP", "arrS", "arrX", "arrF", "locP", "locS", "locX", "locF"] + ["b%d" % _i for _i in range(8)])
+
+
+def plan(T, topo, rank, kind):
+    core = T.cores[rank]
+    off = [d for d in range(8) if d != rank and topo.chip(T.cores[d]) != topo.chip(core)]
+    on = [d for d in range(8) if d != rank and topo.chip(T.cores[d]) == topo.chip(core)]
+    off.sort(key=lambda d: (topo.same_plane(topo.chip(core), topo.chip(T.cores[d])), (d - rank) % 8))
+    eo = topo.engines(core, T.cores[off[0]])
+    en = [e for e in topo.engines(core, T.cores[on[0]]) if e not in eo]
+    if kind == "X":
+        c1 = [(d, eo[2 * i:2 * i + 2]) for i, d in enumerate(off[:4])]
+        c2 = [(d, eo[4 * i:4 * i + 4]) for i, d in enumerate(off[4:])] + [(d, en[:2]) for d in on]
+        return [c1, c2]
+    sh = 2 if kind == "S" else 0
+    return [[(d, [eo[i + sh]]) for i, d in enumerate(off)] + [(d, [en[sh // 2]]) for d in on]]
+
+
+def rank_program(g, core, T, topo):
+    rank = T.rank_of(core)
+    if rank is None:
+        return
+    Q = {"v": g.vector, "a": g.scalar, "p": g.tensor, "g": g, "s": g.sync}
+    QS = {"v": "vq", "a": "aq", "p": "pq", "g": "gq"}
+    total, last, readers = {}, {}, {}
+    known = {q: {} for q in Q}
+
+    def wait(q, tok):
+        sem, val, know = tok
+        if val is None:
+            val = total[sem]
+        if known[q].get(sem, 0) >= val:
+            return
+        Q[q].wait_ge(T.sem[sem], int(val))
+        known[q][sem] = val
+        for s, v in know.items():
+            if known[q].get(s, 0) < v:
+                known[q][s] = v
+
+    def deps(q, rd, wr):
+        own = QS.get(q)
+        for k in rd:
+            if k in last:
+                wait(q, last[k])
+        for k in wr:
+            for tok in readers.get(k, []) + ([last[k]] if k in last else []):
+                if tok[0] != own:
+                    wait(q, tok)
+
+    def mark(tok, rd, wr):
+        for k in rd:
+            readers.setdefault(k, []).append(tok)
+        for k in wr:
+            last[k] = tok
+            readers[k] = []
+
+    def op(q, name, args, rd, wr, **kw):
+        deps(q, rd, wr)
+        o = Q[q]
+        fn = {"copy": lambda: o.tensor_copy(*args), "tt": lambda: o.tensor_tensor(*args), "ts": lambda: o.tensor_scalar(*args),
+              "memset": lambda: o.memset(*args), "red": lambda: o.tensor_reduce(*args), "scan": lambda: o.tensor_tensor_scan(*args),
+              "act": lambda: o.activation(*args, **kw), "iota": lambda: o.iota(*args, **kw), "asel": lambda: o.affine_select(*args)}[name]
+        s = QS[q]
+        fn().then_inc(T.sem[s], 1)
+        total[s] = total.get(s, 0) + 1
+        mark((s, total[s], dict(known[q])), rd, wr)
+
+    def mms(calls, rd, wr):
+        deps("p", rd, wr)
+        for i, a in enumerate(calls):
+            ins = g.tensor.matmul(*a)
+            if i == len(calls) - 1:
+                ins.then_inc(T.sem.pq, 1)
+        total["pq"] = total.get("pq", 0) + 1
+        mark(("pq", total["pq"], dict(known["p"])), rd, wr)
+
+    def dma(q, out, in_, sem, rd, wr):
+        deps(q, rd, wr)
+        Q[q].dma_start(out, in_).then_inc(T.sem[sem], 16)
+        total[sem] = total.get(sem, 0) + 16
+        mark((sem, None, dict(known[q])), rd, wr)
+
+    def send(kind, src, dst, arr, loc, rd):
+        deps("g", rd, [])
+        for call in plan(T, topo, rank, kind):
+            tr = []
+            for d, es in call:
+                rid, pid, _ = topo.addr(T.cores[d])
+                tr.append(RemoteDMATransfer(dst_ids=[DstId(rid=rid, pnc=pid)], dma_engine_mask=sum(1 << e for e in es),
+                                            remote_sem=T.sem[arr], srcs=[src(d)], dsts=[dst]))
+                total[loc] = total.get(loc, 0) + len(es)
+            g.remote_dma_fused(tr, local_sem=T.sem[loc])
+        total[arr] = arrive[arr]
+        mark((loc, total[loc], dict(known["g"])), rd, [])
+
+    arrive = {}
+    for kind, k, arr in (("P", "PL", "arrP"), ("S", "SL", "arrS"), ("X", "LR", "arrX"), ("F", "FL", "arrF")):
+        arrive[arr] = sum(len(es) for r in range(8) if r != rank for call in plan(T, topo, r, kind) for d, es in call if d == rank)
+        last[k] = (arr, arrive[arr], {})
+    V = lambda name, args, rd, wr: op("v", name, args, rd, wr)
+    S = lambda name, args, rd, wr, **kw: op("a", name, args, rd, wr, **kw)
+
+    def cp(q, out, in_, rd, wr):
+        if q == "v":
+            V("copy", (out, in_), rd, wr)
+        else:
+            S("act", (out, in_, AF.Copy), rd, wr)
+
+    dma("s", T.PP[:], T.pats[:], "dp", [], ["PP"])
+    dma("s", T.SS[:], T.starts[:], "ds", [], ["SS"])
+    for s in range(8):
+        dma("s" if s in (3, 5, 6, 7) else "a", T.D32[:, 256 * s:256 * s + 256], T.bwt[s:s + 1, :], "b%d" % s, [], ["D32%d" % s])
+    dma("s", T.PL[rank], T.pats[16 * rank:16 * rank + 16, :], "dsp", [], ["PLs"])
+    dma("s", T.SL[rank], T.starts[16 * rank:16 * rank + 16, :], "dss", [], ["SLs"])
+
+    fl = dict(allow_small_or_imprecise_dtypes=True)
+    V("memset", (T.ONE1[:], 1.0), [], ["ONE1"])
+    V("memset", (T.FOUR[:], 4.0), [], ["FOUR"])
+    op("g", "iota", (T.KI[:, 0:1], [[0, 1]], 0, 1), [], ["KI0"])
+    op("g", "asel", (T.ID[:], T.ONE1[:], [[-1, 128]], A.is_equal, 0.0, 0, 1), ["ONE1"], ["ID"])
+    op("g", "iota", (T.G4[:], [[2, 4], [8, 4]], 0, 0), [], ["G4"], **fl)
+    op("g", "iota", (T.G5[:], [[1, 4], [4, 4], [64, 2]], 0, 0), [], ["G5"], **fl)
+    op("g", "iota", (T.G6[:], [[48, 8]], 32, 0), [], ["G6"], **fl)
+    op("g", "iota", (T.IC4[:], [[1, 4]], 0, 0), [], ["IC4"], **fl)
+    send("P", lambda d: T.PP[d], T.PL[rank], "arrP", "locP", ["PP"])
+    send("S", lambda d: T.SS[d], T.SL[rank], "arrS", "locS", ["SS"])
+    op("g", "asel", (T.GA[:], T.FOUR[:], [[-16, 8], [0, 4]], A.is_ge, 0.0, 0, 1), ["FOUR"], ["GA"])
+    op("g", "asel", (T.GB[:], T.GA[:], [[16, 8], [0, 4]], A.is_ge, 0.0, 15, -1), ["GA"], ["GB"])
+    op("g", "asel", (T.TRI[:], T.ONE1[:], [[1, 128]], A.is_ge, 0.0, -1, -1), ["ONE1"], ["TRI"])
+    op("g", "iota", (T.G1[:], [[1, 16], [0, 4]], 0, 0), [], ["G1"], **fl)
+    op("g", "iota", (T.G2[:], [[0, 16], [64, 4]], 12288, 0), [], ["G2"], **fl)
+
+    col = lambda j: T.KF[:, j:j + 1]
+    for d, n, sh in ((2, 3, 0), (1, 15, 0), (3, 3, 2), (4, 1, 0), (5, 1, 1), (6, 7, 1), (7, 1, 0)):
+        V("ts", (T.KI[:, d:d + 1], T.KI[:, 0:1], sh, n, A.arith_shift_right, A.bitwise_and), ["KI0"], ["KI"])
+    V("copy", (T.KF[:, 0:8], T.KI[:, 0:8]), ["KI", "KI0"], ["KF"])
+    S("act", (col(8), col(2), AF.Exp), ["KF"], ["K8"], scale=float(np.log(64.0)))
+    for i in range(8):
+        V("ts", (T.PK[:, 128 * i:128 * i + 128], T.ID[:], float(4 ** i), None, A.mult), ["ID"], ["PK"])
+
+    def lin(j, src, k1, k2):
+        V("ts", (col(j), col(src), k1, k2, A.mult, A.add), ["KF"] if src < 8 else ["K%d" % src], ["K%d" % j])
+
+    CH = 5.0 * float(np.log(2.0))
+    for s in range(8):
+        c0 = 256 * s
+        V("copy", (T.D[:, c0:c0 + 256], T.D32[:, c0:c0 + 256]), ["D32%d" % s], ["D%d" % s])
+        S("act", (T.CE[:, c0:c0 + 256], T.D[:, c0:c0 + 256], AF.Exp), ["D%d" % s], ["CE%d" % s], scale=CH)
+    for f in range(4):
+        lo, hi = 512 * f, 512 * f + 512
+        mms([(T.PSA[:, lo:lo + 64], T.PK[:, 128 * i:128 * i + 128], T.D[:, lo + i:hi:8], i == 0, i == 7) for i in range(8)],
+            ["D%d" % (2 * f), "D%d" % (2 * f + 1), "PK"], ["A%d" % f])
+        if f % 2 == 1:
+            hh = f // 2
+            lo, hi, o = 1024 * hh, 1024 * hh + 1024, 512 * hh
+            mms([(T.PSB[:, o:o + 64], T.ID[:], T.CE[:, lo + q:hi:16], q == 0, q == 15) for q in range(16)],
+                ["CE%d" % s for s in range(4 * hh, 4 * hh + 4)] + ["ID"], ["B%d" % hh])
+    sk = []
+    for f in range(4):
+        for s in (2 * f, 2 * f + 1):
+            o = 512 * f + 32 * (s % 2)
+            V("ts", (T.SEND[:, 48 * s:48 * s + 32], T.PSA[:, o:o + 32], 128.0, None, A.add), ["A%d" % f], ["SX%d" % s])
+            sk.append("SX%d" % s)
+    for hh in range(2):
+        for s in (4 * hh, 4 * hh + 1, 4 * hh + 2, 4 * hh + 3):
+            o = 512 * hh + 16 * (s % 4)
+            cp("a" if hh == 0 else "v", T.SEND[:, 48 * s + 32:48 * s + 48], T.PSB[:, o:o + 16], ["B%d" % hh], ["SC%d" % s])
+            sk.append("SC%d" % s)
+    send("X", lambda d: T.SEND[:, 48 * d:48 * d + 48], T.LR[:, 48 * rank:48 * rank + 48], "arrX", "locX", sk)
+    V("copy", (T.LR[:, 48 * rank:48 * rank + 48], T.SEND[:, 48 * rank:48 * rank + 48]), ["SX%d" % rank, "SC%d" % rank], ["LRs"])
+
+    V("memset", (T.ONE2[:], 1.0), [], ["ONE2"])
+    op("g", "asel", (T.SEL[:], T.ONE2[:, 0:128 * NPE], [[-16, NPE], [0, 8], [-1, 16]], A.is_equal, 0.0, 0, 1), ["ONE2"], ["SEL"])
+    lin(28, 6, 48.0, 0.0)
+    lin(21, 2, 128.0, 0.0)
+    lin(22, 3, 16.0, 0.0)
+    lin(13, 4, -12800.0, 51200.0)
+    lin(16, 5, -13056.0, 0.0)
+    V("tt", (col(14), col(4), col(5), A.mult), ["KF"], ["K14"])
+    V("tt", (col(29), col(28), col(7), A.add), ["K28", "KF"], ["K29"])
+    V("tt", (col(23), col(21), col(22), A.add), ["K21", "K22"], ["K23"])
+    V("tt", (col(17), col(13), col(16), A.add), ["K13", "K16"], ["K17"])
+    lin(15, 14, -38144.0, 0.0)
+    lin(31, 14, -1.0, 1.0)
+    V("ts", (T.OFX[:], T.G4[:], col(29), None, A.add), ["G4", "K29"], ["OFX"])
+    V("ts", (T.OFC[:], T.G6[:], col(1), None, A.add), ["G6", "KF"], ["OFC"])
+    V("ts", (T.OFF[:], T.G5[:], col(23), None, A.add), ["G5", "K23"], ["OFF"])
+    V("tt", (col(18), col(17), col(15), A.add), ["K17", "K15"], ["K18"])
+    V("memset", (T.MK[:], 1.0), [], ["MK0"])
+    V("memset", (T.ONE32[:], 1.0), [], ["ONE32"])
+    V("memset", (T.BASE[:, 0:1], 0.0), [], ["BASE0"])
+    V("ts", (T.INI[:], T.ID[:], col(18), None, A.mult), ["ID", "K18"], ["INI"])
+    V("memset", (T.TB[:, 3:2048:4], 0.0), [], ["TB3"])
+    V("memset", (T.DB[:, 3:2048:4], 0.0), [], ["DB3"])
+    V("ts", (T.IDP[:], T.ID[:], 1.25, None, A.mult), ["ID"], ["IDP"])
+    V("ts", (T.IDN[:], T.ID[:], -1.25, None, A.mult), ["ID"], ["IDN"])
+    V("memset", (T.MK[:, 0:512:16], 0.0), ["MK0"], ["MK"])
+    V("copy", (T.LW[:, 0:4], T.IC4[:]), ["IC4"], ["LW"])
+    V("ts", (T.SELL[:, 0:8], T.GB[:, 0:32:4], 1.0 / 64, None, A.mult), ["GB"], ["SELL"])
+    L0 = 1536
+    V("memset", (T.PSB[:, L0 + 240:L0 + 256], 0.0), [], ["B3z"])
+    mms([(T.PSA[:, 512 * b:512 * b + 512], T.INI[:], T.ONE2[:, 0:512], True, False) for b in range(4)], ["INI", "ONE2"], ["A0", "A1", "A2", "A3"])
+
+    dma("s", T.PT[:], T.PL[:], "lpt", ["PL", "PLs"], ["PT"])
+    dma("s", T.ST[:], T.SL[:], "lst", ["SL", "SLs"], ["ST"])
+    V("copy", (T.OFP[:], T.PT[:]), ["PT"], ["OFP"])
+    V("copy", (T.PTB[:], T.PT[:]), ["PT"], ["PTB"])
+    S("act", (T.LTR[:, 0:1024], T.LW[:, 0:4].indirect(T.OFP[:, 0:64]), AF.Copy), ["LW", "OFP"], ["LTR0"])
+    V("copy", (T.LTR[:, 1024:2048], T.LW[:, 0:4].indirect(T.OFP[:, 64:128])), ["LW", "OFP"], ["LTR1"])
+    tau = lambda t: t // 2 + (4 if t % 2 else 0)
+    cs = []
+    for t in range(8):
+        o = L0 + 16 * (t // 2) + (128 if t % 2 else 0)
+        for blk in range(2):
+            cs.append((T.PSB[:, o + 8 * blk:o + 8 * blk + 8], T.LTR[:, 256 * t + 128 * blk:256 * t + 128 * blk + 128], T.SELL[:, 0:8], True, True))
+    for t in range(1, 8):
+        o = L0 + 64 + 16 * ((t - 1) // 2) + (0 if t % 2 else 128)
+        cs.append((T.PSB[:, o:o + 16], T.ID[:], T.PTB[:, 16 * t:16 * t + 16], True, True))
+    mms(cs, ["LTR0", "LTR1", "SELL", "PTB", "ID", "B3z"], ["B3"])
+
+    V("copy", (T.CI[:], T.LR[:, 0:384].indirect(T.OFC[:, 0:8])), ["LR", "LRs", "OFC"], ["CI"])
+    S("act", (T.H[:], T.LR[:, 0:384].indirect(T.OFX[:, 0:16]), AF.Copy), ["LR", "LRs", "OFX"], ["H"], scale=(1.0 + 2.0 ** -17) / 256, bias=RND)
+    S("act", (T.LXP[:, 1:512:2], T.H[:], AF.Copy), ["H"], ["LXP1"], bias=-RND - 129.0)
+    LXK = ["LXP0", "LXP1"]
+
+    def planes(e, lst):
+        for x in lst.split():
+            name, i = "T" + x[1], int(x[2])
+            k, sc = i + (x[1] == "B"), 64.0 / 4 ** i
+            args, wr = (T[name][:, 1024 * e + i:1024 * e + 1024:4], T.LXP[:, 256 * e:256 * e + 256]), ["%s%d%d" % (name, i, e)]
+            if x[0] == "v":
+                V("ts", args + (B_T[k] + 128.0, sc, A.add, A.mult), LXK, wr)
+            else:
+                S("act", args + (AF.Copy,), LXK, wr, scale=sc, bias=sc * (B_T[k] + 128.0))
+
+    def cx(c):
+        V("ts", (T.CX[:, 128 * c:128 * c + 128], T.CI[:], 5 * c, 31, A.arith_shift_right, A.bitwise_and), ["CI"], ["CX"])
+    cx(0)
+    cx(1)
+    V("ts", (T.HM[:], T.H[:], -RND, -256.0, A.add, A.mult), ["H"], ["HM"])
+    cx(2)
+    V("tt", (T.LXP[:, 0:512:2], T.LR[:, 0:384].indirect(T.OFX[:, 0:16]), T.HM[:], A.add), ["LR", "LRs", "OFX", "HM"], ["LXP0"])
+    cx(3)
+    V("copy", (T.NS[:, 1:512], T.CX[:, 0:511]), ["CX"], ["NS"])
+    V("copy", (T.N15[:], T.CX[:, 15:512:16]), ["CX"], ["N15"])
+    V("memset", (T.NS[:, 0:512:16], 0.0), ["NS"], ["NS"])
+    V("scan", (T.S1[:], T.MK[:], T.NS[:], 0.0, A.mult, A.add), ["MK", "NS"], ["S1"])
+    planes(0, P0)
+    for j, (m, k) in enumerate(((T.ONE1[:], "ONE1"), (T.TRI[:], "TRI"))):
+        o = T.PSB[:, 512 + 512 * j:544 + 512 * j]
+        mms([(o, m, T.S1[:, 15:512:16], True, False), (o, m, T.N15[:], False, True)], ["S1", "N15", k], ["B%d" % (1 + j)])
+    V("scan", (T.BASE[:, 1:33], T.ONE32[:], T.PSB[:, 512:544], 0.0, A.mult, A.add), ["B1", "ONE32"], ["B1", "BASE"])
+    V("tt", (T.NS[:, 0:512:16], T.PSB[:, 1024:1056], T.BASE[:, 0:32], A.add), ["B2", "BASE", "BASE0"], ["B2", "NS"])
+    V("scan", (T.F[:], T.MK[:], T.NS[:], 0.0, A.mult, A.add), ["MK", "NS"], ["F"])
+    planes(1, P1)
+    PO = lambda b, m: T.PSA[:, 512 * b + m:512 * b + 512:4]
+
+    def letters_turned(e):
+        for b in (2 * e, 2 * e + 1):
+            cs = []
+            for m in range(4):
+                x0 = 128 * (4 * b + m)
+                cs += [(PO(b, m), T.TA[:, x0:x0 + 128], T.IDP[:], False, False), (PO(b, m), T.TB[:, x0:x0 + 128], T.IDN[:], False, False)]
+            mms(cs, ["TA%d%d" % (i, e) for i in range(4)] + ["TB%d%d" % (i, e) for i in range(3)] + ["TB3", "IDP", "IDN"], ["A%d" % b])
+
+    def xc(b):
+        cp(XCQ[b], T.XC[:, b:2048:4], T.PSA[:, 512 * b:512 * b + 512], ["A%d" % b], ["A%d" % b, "XC%d" % b])
+
+    for e in range(2):
+        n0, n1, m0, m1 = 256 * e, 256 * e + 256, 1024 * e, 1024 * e + 1024
+        V("copy", (T.NI[:, n0:n1], T.F[:, 0:512].indirect(T.OFF[:, 16 * e:16 * e + 16])), ["F", "OFF"], ["NI%d" % e])
+        letters_turned(e)
+        S("act", (T.DB[:, m0 + 2:m1:4], T.F[:, 0:512].indirect(T.OFF[:, 16 * e:16 * e + 16]), AF.Copy), ["F", "OFF"], ["DB2%d" % e],
+          scale=2.0 ** -12, bias=191.5 + 2.0 ** -13)
+        if e == 0:
+            planes(1, P2)
+        for i in range(2):
+            V("ts", (T.DI[:, 512 * i + n0:512 * i + n1], T.NI[:, n0:n1], 6 * i, 63, A.arith_shift_right, A.bitwise_and), ["NI%d" % e], ["DI%d%d" % (i, e)])
+        for i in range(2):
+            V("ts", (T.DB[:, m0 + i:m1:4], T.DI[:, 512 * i + n0:512 * i + n1], -64.0, None, A.add), ["DI%d%d" % (i, e)], ["DB%d%d" % (i, e)])
+        for b in (2 * e, 2 * e + 1):
+            mms([(PO(b, m), T.DB[:, 128 * (4 * b + m):128 * (4 * b + m) + 128], T.ID[:], False, m == 3) for m in range(4)],
+                ["DB%d%d" % (i, e) for i in range(3)] + ["DB3", "ID"], ["A%d" % b])
+            xc(b)
+    for c in range(4):
+        V("ts", (T.AM[:, 128 * c:128 * c + 128], T.PSB[:, L0:L0 + 128], float(c), -float(BIG), A.not_equal, A.mult), ["B3"], ["AM%d" % c])
+    for c in range(4):
+        V("tt", (T.QTB[:, c:512:4], T.PSB[:, L0 + 128:L0 + 256], T.AM[:, 128 * c:128 * c + 128], A.add), ["B3", "B3z", "AM%d" % c], ["QTB%d" % c])
+
+    XK, XCK = ["XE"], ["XC%d" % b for b in range(4)]
+    for k in range(NPE, 8):
+        for y in range(8):
+            dma("s", T.X[16 * y:16 * y + 16, 2048 * k:2048 * k + 2048], T.XC[16 * k:16 * k + 16, :], "rep", XCK, ["XD%d%d" % (k, y)])
+            XK.append("XD%d%d" % (k, y))
+    small = [
+        lambda: V("memset", (T.RST[:], 1.0), [], ["RST0"]),
+        lambda: V("ts", (T.EM[:, 0:4], T.IC4[:], col(3), col(31), A.is_equal, A.mult), ["IC4", "KF", "K31"], ["EM"]),
+        lambda: V("ts", (T.G3[:], T.G1[:], col(1), None, A.is_gt), ["G1", "KF"], ["G3"]),
+        lambda: V("memset", (T.RST[:, 0:64:4], 0.0), ["RST0"], ["RST"]),
+        lambda: V("ts", (col(30), T.EM[:, 0:1], 7712.0, None, A.mult), ["EM"], ["K30"]),
+        lambda: V("tt", (T.EV[:, 0:4], T.EM[:, 0:4], T.BASE[:, 8:33:8], A.mult), ["EM", "BASE"], ["EV"]),
+        lambda: V("tt", (T.W[:], T.G3[:], T.G2[:], A.mult), ["G3", "G2"], ["W"]),
+        lambda: V("ts", (T.CON[:], T.ONE1[:, 0:64], col(8), col(30), A.mult, A.mult), ["ONE1", "K8", "K30"], ["CON"]),
+        lambda: V("ts", (T.ST4[:], T.ST[:], 4.0, None, A.mult), ["ST"], ["ST4"]),
+        lambda: V("red", (T.EV[:, 4:5], T.EV[:, 0:4], AxisListType.X, A.add), ["EV"], ["EV4"]),
+        lambda: lin(9, 4, -63.0 / 64, 1.0),
+        lambda: lin(10, 5, -4095.0 / 4096, 1.0),
+    ] + [
+        lambda c=c: V("ts", (T.SELY[:, c:32:4], T.GB[:, c:32:4], col(8), T.EM[:, c:c + 1], A.mult, A.mult), ["GB", "K8", "EM"], ["SELY"]) for c in range(4)
+    ] + [
+        lambda: V("tt", (col(11), col(9), col(10), A.mult), ["K9", "K10"], ["K11"]),
+    ] + [
+        lambda h=h: V("tt", (T["I%d" % h][:], T.ST4[:, 16 * h:16 * h + 16], T.PT[:, 0:16], A.add), ["ST4", "PT"], ["I%d" % h]) for h in range(2)
+    ] + [
+        lambda: lin(12, 11, 0.5, -0.5),
+        lambda: V("ts", (T.SELZ[:], T.SELY[:], -1.25, None, A.mult), ["SELY"], ["SELZ"]),
+        lambda: lin(26, 5, 64.0, -64.0),
+        lambda: lin(27, 14, 64.0, -64.0),
+        lambda: V("ts", (T.EI[:, 0:1], T.EV[:, 4:5], col(11), col(12), A.mult, A.add), ["EV4", "K11", "K12"], ["EI0"]),
+        lambda: V("ts", (T.EI[:, 1:2], T.EI[:, 0:1], 6, None, A.arith_shift_right), ["EI0"], ["EI1"]),
+        lambda: V("ts", (T.EV[:, 6:7], T.EI[:, 1:2], col(26), col(27), A.mult, A.add), ["EI1", "K26", "K27"], ["EV6"]),
+        lambda: V("tt", (T.X[:, 16384:16385], T.EI[:, 0:1], T.EV[:, 6:7], A.add), ["EI0", "EV6"], ["XE"]),
+    ]
+    n = 0
+    for b in range(4):
+        for k in range(NPE):
+            pb = n % 3
+            mms([(T.PSB[:, 512 * pb:512 * pb + 512], T.SEL[:, 128 * k:128 * k + 128], T.XC[:, b:2048:4], True, True)], ["XC%d" % b, "SEL"], ["B%d" % pb])
+            cp(XQ[n], T.X[:, 2048 * k + b:2048 * k + 2048:4], T.PSB[:, 512 * pb:512 * pb + 512], ["B%d" % pb], ["B%d" % pb, "X%d" % n])
+            XK.append("X%d" % n)
+            if XQ[n] == "v":
+                for f in small[:5]:
+                    f()
+                del small[:5]
+            n += 1
+    for f in small:
+        f()
+
+    B = lambda name, n: T[("S1B" if name == "S" and n % 2 else "%s%d" % (name, n % 2))]
+    key = lambda name, n: "%s:%d" % (name, n % 2)
+    for h in range(2):
+        last["I:%d" % h] = last["I%d" % h]
+    QK = ["QTB%d" % c for c in range(4)]
+
+    def state(n):
+        ps, pk = 512 * (n % 2), "A%d" % (n % 2)
+        V("scan", (B("S", n)[:], T.RST[:], T.PSA[:, ps:ps + 64], 0.0, A.mult, A.max), [pk, "RST"], [pk, key("S", n)])
+
+    def block(n):
+        ps, pk = 512 * (n % 2), "A%d" % (n % 2)
+        src, sk = (B("I", n)[:], key("I", n)) if n < 2 else (B("S", n)[:, 3:64:4], key("S", n))
+        V("ts", (B("OA", n)[:], src, 1.0 / 64, -0.5 + 0.5 / 64, A.mult, A.add), [sk], [key("OA", n)])
+        S("act", (B("Z", n)[:], T.X[:, 0:16385].indirect(B("OA", n)[:, 0:16]), AF.Copy), [key("OA", n)] + XK, [key("Z", n)])
+        S("act", (B("ZL", n)[:], B("Z", n)[:], AF.Copy), [key("Z", n)], [key("ZL", n)], scale=0.8, bias=12313.6)
+        mms([(T.PSA[:, ps:ps + 64], T.ONE1[:], T.CON[:], True, False)], ["ONE1", "CON"], [pk])
+
+    def table(n):
+        t, ps, pk, Z, ZL = n // 2, 512 * (n % 2), "A%d" % (n % 2), B("Z", n), B("ZL", n)
+        q0 = 64 * tau(t)
+        cs = [(T.PSA[:, ps + 32 * k:ps + 32 * k + 32], ZL[:, 128 * k:128 * k + 128], T.SELZ[:], False, False) for k in range(2)]
+        cs += [(T.PSA[:, ps:ps + 64], T.ID[:], T.QTB[:, q0:q0 + 64], False, False)]
+        cs += [(T.PSA[:, ps + 32 * k:ps + 32 * k + 32], Z[:, 128 * k:128 * k + 128], T.SELY[:], False, False) for k in range(2)]
+        mms(cs, [key("Z", n), key("ZL", n), "ID", "SELY", "SELZ"] + QK, [pk])
+
+    def count(n):
+        ps, pk, ZL, E = 512 * (n % 2), "A%d" % (n % 2), B("ZL", n), B("E", n)
+        V("tt", (E[:], T.W[:, 0:64].indirect(B("OB", n)[:, 0:16]), ZL[:], A.is_equal), [key("OB", n), "W", key("ZL", n)], [key("E", n)])
+        mms([(T.PSA[:, ps + 32 * k:ps + 32 * k + 32], E[:, 128 * k:128 * k + 128], T.GB[:], False, k == 1) for k in range(2)],
+            [key("E", n), "GB"], [pk])
+
+    for n in range(18):
+        if n >= 2:
+            state(n)
+        if 0 < n < 17:
+            V("copy", (B("OB", n - 1)[:], B("J", n - 1)[:]), [key("J", n - 1)], [key("OB", n - 1)])
+        if n < 16:
+            block(n)
+        else:
+            h = n % 2
+            V("ts", (T.RES[:, 16 * h:16 * h + 16], B("S", n)[:, 3:64:4], 0.25, None, A.mult), [key("S", n)], ["RES%d" % h])
+        if 0 < n < 17:
+            table(n - 1)
+            count(n - 1)
+        if n < 16:
+            if n >= 2:
+                V("copy", (B("I", n)[:], B("S", n)[:, 3:64:4]), [key("S", n)], [key("I", n)])
+            V("ts", (B("J", n)[:], B("I", n)[:], 63, None, A.bitwise_and), [key("I", n)], [key("J", n)])
+    dma("s", T.RD[:], T.RES[:], "rd", ["RES0", "RES1"], ["RD"])
+    send("F", lambda d: T.RD[d], T.FL[rank], "arrF", "locF", ["RD"])
+    r0, r1 = 16 * rank, 16 * rank + 16
+    dma("s", T.y[r0:r1, :], T.RES[r0:r1, :], "yself", ["RES0", "RES1"], ["y0"])
+    if rank > 0:
+        dma("s", T.y[0:r0, :], T.FL[0:rank], "yout", ["FL"], ["y1"])
+    if rank < 7:
+        dma("s", T.y[r1:128, :], T.FL[rank + 1:8], "yout", ["FL"], ["y2"])
+    for sem in sorted(total):
+        wait("g", (sem, total[sem], {}))

@@ -1,54 +1,54 @@
-import numpy as np
 from concourse.bass import DstId, RemoteDMATransfer
 from concourse.mybir import AluOpType as A, AxisListType, ActivationFunctionType as AF
 
-NPE = 4
-BIG = 2097152
-RND = 12582912.0
-B_T = (0.0, 638.5, 2552.5, 10208.5)
-P0 = "aA0 aA1 aB0 aA2 aB1 vA3 vB2"
-P1 = "aA0 aA1 aB0"
-P2 = "aA2 aB1 aA3 aB2"
-XCQ = "aava"
-XQ = "ava" + "avavavavavavavav" * 2
+NPE = 5
+BIG = 2097152.0
+TOFF = (0.0, -1.5, -7.5, -31.5)
+PLANES = "aA0 vU0 vB0 aA2 vB2 aA1 vB1 vA3"
+XCQ = "avav"
 
 SCRATCH = {
     "PP": ("dram", [8, 128, 16], "int32"), "SS": ("dram", [8, 128, 4], "int32"),
     "PL": ("dram", [8, 128, 16], "int32"), "SL": ("dram", [8, 128, 4], "int32"),
     "RD": ("dram", [8, 128, 4], "float32"), "FL": ("dram", [8, 128, 4], "float32"),
-    "PSA": ("psum", [128, 2048], "float32"), "PSB": ("psum", [128, 2048], "float32"),
+    "PV": ("psum", [128, 2048], "bfloat16"), "PSA": ("psum", [128, 2048], "float32"),
+    "PS0": ("psum", [128, 4, 2, 64], "float32"), "PS1": ("psum", [128, 4, 2, 64], "float32"),
 }
 for _n, _w, _d in (
-        ("D32", 2048, "int32"), ("D", 2048, "bfloat16"), ("CE", 2048, "bfloat16"), ("SEND", 384, "float32"), ("LR", 384, "float32"),
-        ("H", 256, "float32"), ("HM", 256, "float32"), ("LXP", 512, "bfloat16"),
-        ("TA", 2048, "bfloat16"), ("TB", 2048, "bfloat16"), ("CI", 128, "int32"), ("CX", 512, "int32"), ("NS", 512, "float32"),
-        ("S1", 512, "bfloat16"), ("N15", 32, "bfloat16"), ("MK", 512, "float32"), ("BASE", 40, "float32"),
-        ("ONE32", 32, "float32"), ("F", 512, "float32"), ("NI", 512, "int32"), ("DI", 1024, "int32"),
-        ("DB", 2048, "bfloat16"), ("XC", 2048, "bfloat16"), ("X", 16400, "bfloat16"),
-        ("ONE1", 128, "bfloat16"), ("ONE2", 512, "bfloat16"), ("FOUR", 32, "bfloat16"), ("GA", 32, "bfloat16"), ("GB", 32, "bfloat16"),
-        ("ID", 128, "bfloat16"), ("IDP", 128, "bfloat16"), ("IDN", 128, "bfloat16"), ("INI", 128, "bfloat16"), ("CON", 64, "bfloat16"),
-        ("PK", 1024, "bfloat16"), ("TRI", 128, "bfloat16"), ("SEL", 128 * NPE, "bfloat16"),
-        ("SELY", 32, "bfloat16"), ("SELZ", 32, "bfloat16"), ("SELL", 16, "bfloat16"),
-        ("KI", 16, "int32"), ("KF", 48, "float32"), ("G1", 64, "float32"),
-        ("G2", 64, "float32"), ("G3", 64, "float32"), ("G4", 16, "float32"), ("G5", 32, "float32"), ("G6", 8, "float32"), ("IC4", 4, "float32"),
-        ("EM", 8, "float32"), ("EV", 8, "float32"), ("EI", 4, "int32"), ("W", 64, "bfloat16"), ("LW", 16, "bfloat16"),
-        ("OFX", 16, "uint16"), ("OFF", 32, "uint16"), ("OFC", 8, "uint16"), ("PT", 128, "int32"), ("ST", 32, "int32"), ("ST4", 32, "int32"),
-        ("OFP", 128, "uint16"), ("PTB", 128, "bfloat16"), ("LTR", 2048, "bfloat16"), ("AM", 512, "bfloat16"), ("QTB", 512, "bfloat16"),
-        ("RST", 64, "float32"), ("RES", 32, "float32"),
-        ("I0", 16, "int32"), ("J0", 16, "int32"), ("OA0", 16, "uint16"), ("OB0", 16, "uint16"), ("S0", 64, "float32"),
+        ("D32", 2048, "int32"), ("D", 2048, "bfloat16"), ("G1", 512, "bfloat16"), ("G2", 512, "bfloat16"), ("G3", 512, "bfloat16"),
+        ("SEND", 960, "bfloat16"), ("LR", [8, 120], "bfloat16"), ("M", 180, "bfloat16"), ("MC", 120, "bfloat16"),
+        ("DPI", 16, "bfloat16"), ("DP", 16, "bfloat16"),
+        ("TA", [32, 4, 16], "bfloat16"), ("TB", [32, 4, 16], "bfloat16"), ("AD", [32, 4, 2], "bfloat16"),
+        ("NI", 64, "int32"), ("DI", [32, 3, 2], "int32"), ("UI", 64, "float32"), ("MASK", 128, "float32"), ("MS", 128, "float32"),
+        ("BX", 8, "float32"), ("BI", 4, "int32"), ("XC", 2048, "bfloat16"), ("X", 16400, "bfloat16"),
+        ("ONE1", 128, "bfloat16"), ("ONE2", 128 * NPE, "bfloat16"), ("FOUR", 64, "bfloat16"), ("GA", 64, "bfloat16"), ("GB", 64, "bfloat16"),
+        ("ID", [8, 4, 4], "bfloat16"), ("CON", 128, "bfloat16"), ("TRI", 128, "bfloat16"), ("SEL", 128 * NPE, "bfloat16"),
+        ("SELY", 64, "bfloat16"), ("SELZ", 64, "bfloat16"), ("SELQ", 64, "bfloat16"), ("EQ", 32, "bfloat16"), ("CQ", 32, "float32"),
+        ("KI", 8, "int32"), ("KF", 32, "float32"), ("RI", 64, "float32"), ("CI", 64, "float32"), ("W0", 64, "float32"),
+        ("VA", 16, "float32"), ("VB", 16, "float32"), ("L0", 16, "float32"),
+        ("W", 1088, "bfloat16"), ("LW", 16, "bfloat16"), ("PT", [4, 2, 16], "int32"), ("ST", 32, "int32"), ("ST4", 32, "int32"),
+        ("P4", 64, "int32"), ("PI", 64, "int32"), ("OFP", 64, "uint16"), ("LTR", 1024, "bfloat16"), ("AM", 256, "float32"), ("NX", 64, "float32"),
+        ("QTB", [4, 2, 16, 4], "bfloat16"), ("RST", 64, "float32"), ("RES", 32, "float32"), ("I", 32, "int32"), ("J", 32, "int32"),
+        ("OA0", 16, "uint16"), ("OB0", 16, "uint16"), ("S0", 64, "float32"), ("L0S", 64, "float32"),
         ("Z0", 256, "bfloat16"), ("ZL0", 256, "bfloat16"), ("E0", 256, "bfloat16"),
-        ("I1", 16, "int32"), ("J1", 16, "int32"), ("OA1", 16, "uint16"), ("OB1", 16, "uint16"), ("S1B", 64, "float32"),
+        ("OA1", 16, "uint16"), ("OB1", 16, "uint16"), ("S1", 64, "float32"), ("L1S", 64, "float32"),
         ("Z1", 256, "bfloat16"), ("ZL1", 256, "bfloat16"), ("E1", 256, "bfloat16")):
-    SCRATCH[_n] = ("sbuf", [128, _w], _d)
+    SCRATCH[_n] = ("sbuf", [128] + (_w if isinstance(_w, list) else [_w]), _d)
 SEMAPHORES = (["vq", "aq", "pq", "gq", "dp", "ds", "dsp", "dss", "lpt", "lst", "rep", "yself", "yout", "rd",
                "arrP", "arrS", "arrX", "arrF", "locP", "locS", "locX", "locF"] + ["b%d" % _i for _i in range(8)])
 
 
-def plan(T, topo, rank, kind):
+def others(T, topo, rank):
     core = T.cores[rank]
     off = [d for d in range(8) if d != rank and topo.chip(T.cores[d]) != topo.chip(core)]
     on = [d for d in range(8) if d != rank and topo.chip(T.cores[d]) == topo.chip(core)]
     off.sort(key=lambda d: (topo.same_plane(topo.chip(core), topo.chip(T.cores[d])), (d - rank) % 8))
+    return off, on
+
+
+def plan(T, topo, rank, kind):
+    core = T.cores[rank]
+    off, on = others(T, topo, rank)
     eo = topo.engines(core, T.cores[off[0]])
     en = [e for e in topo.engines(core, T.cores[on[0]]) if e not in eo]
     if kind == "X":
@@ -111,7 +111,7 @@ def rank_program(g, core, T, topo):
     def mms(calls, rd, wr):
         deps("p", rd, wr)
         for i, a in enumerate(calls):
-            ins = g.tensor.matmul(*a)
+            ins = g.tensor.matmul(*a) if len(a) == 5 else g.tensor.transpose(*a)
             if i == len(calls) - 1:
                 ins.then_inc(T.sem.pq, 1)
         total["pq"] = total.get("pq", 0) + 1
@@ -123,18 +123,16 @@ def rank_program(g, core, T, topo):
         total[sem] = total.get(sem, 0) + 16
         mark((sem, None, dict(known[q])), rd, wr)
 
-    def send(kind, src, dst, arr, loc, rd):
+    def send(call, src, dst, arr, loc, rd):
         deps("g", rd, [])
-        for call in plan(T, topo, rank, kind):
-            tr = []
-            for d, es in call:
-                rid, pid, _ = topo.addr(T.cores[d])
-                tr.append(RemoteDMATransfer(dst_ids=[DstId(rid=rid, pnc=pid)], dma_engine_mask=sum(1 << e for e in es),
-                                            remote_sem=T.sem[arr], srcs=[src(d)], dsts=[dst]))
-                total[loc] = total.get(loc, 0) + len(es)
-            g.remote_dma_fused(tr, local_sem=T.sem[loc])
+        tr = []
+        for d, es in call:
+            rid, pid, _ = topo.addr(T.cores[d])
+            tr.append(RemoteDMATransfer(dst_ids=[DstId(rid=rid, pnc=pid)], dma_engine_mask=sum(1 << e for e in es),
+                                        remote_sem=T.sem[arr], srcs=[src(d)], dsts=[dst]))
+            total[loc] = total.get(loc, 0) + len(es)
+        g.remote_dma_fused(tr, local_sem=T.sem[loc])
         total[arr] = arrive[arr]
-        mark((loc, total[loc], dict(known["g"])), rd, [])
 
     arrive = {}
     for kind, k, arr in (("P", "PL", "arrP"), ("S", "SL", "arrS"), ("X", "LR", "arrX"), ("F", "FL", "arrF")):
@@ -142,6 +140,9 @@ def rank_program(g, core, T, topo):
         last[k] = (arr, arrive[arr], {})
     V = lambda name, args, rd, wr: op("v", name, args, rd, wr)
     S = lambda name, args, rd, wr, **kw: op("a", name, args, rd, wr, **kw)
+    G = lambda name, args, rd, wr, **kw: op("g", name, args, rd, wr, **kw)
+    PS = (T.PS0, T.PS1)
+    col = lambda j: T.KF[:, j:j + 1]
 
     def cp(q, out, in_, rd, wr):
         if q == "v":
@@ -149,273 +150,274 @@ def rank_program(g, core, T, topo):
         else:
             S("act", (out, in_, AF.Copy), rd, wr)
 
+    off, on = others(T, topo, rank)
+    order = off + on + [rank]
     dma("s", T.PP[:], T.pats[:], "dp", [], ["PP"])
     dma("s", T.SS[:], T.starts[:], "ds", [], ["SS"])
-    for s in range(8):
-        dma("s" if s in (3, 5, 6, 7) else "a", T.D32[:, 256 * s:256 * s + 256], T.bwt[s:s + 1, :], "b%d" % s, [], ["D32%d" % s])
+    for n, s in enumerate(order):
+        dma("s" if n in (3, 5, 6, 7) else "a", T.D32[:, 256 * n:256 * n + 256], T.bwt[s:s + 1, :], "b%d" % n, [], ["D32%d" % n])
     dma("s", T.PL[rank], T.pats[16 * rank:16 * rank + 16, :], "dsp", [], ["PLs"])
     dma("s", T.SL[rank], T.starts[16 * rank:16 * rank + 16, :], "dss", [], ["SLs"])
 
     fl = dict(allow_small_or_imprecise_dtypes=True)
     V("memset", (T.ONE1[:], 1.0), [], ["ONE1"])
+    V("memset", (T.DPI[:, 0:8], -1.0), [], ["DPI0"])
+    V("memset", (T.DPI[:, 8:16], 1.0), [], ["DPI1"])
+    G("asel", (T.ID[:], T.ONE1[:], [[-1, 128]], A.is_equal, 0.0, 0, 1), ["ONE1"], ["ID"])
+    G("asel", (T.DP[:], T.DPI[:], [[15, 2], [16, 8]], A.is_ge, 0.0, -1, -1), ["DPI0", "DPI1"], ["DP"])
+    G("iota", (T.MC[:, 0:16], [[16, 8], [0, 2]], -241, 0), [], ["MC0"], **fl)
+    G("iota", (T.KI[:, 0:1], [[0, 1]], 0, 1), [], ["KI0"])
+    V("memset", (T.MC[:, 16:64], -256.0), [], ["MC1"])
+    V("memset", (T.MC[:, 64:120], 0.0), [], ["MC2"])
+    V("memset", (T.M[:], 0.0), [], ["M"])
     V("memset", (T.FOUR[:], 4.0), [], ["FOUR"])
-    op("g", "iota", (T.KI[:, 0:1], [[0, 1]], 0, 1), [], ["KI0"])
-    op("g", "asel", (T.ID[:], T.ONE1[:], [[-1, 128]], A.is_equal, 0.0, 0, 1), ["ONE1"], ["ID"])
-    op("g", "iota", (T.G4[:], [[2, 4], [8, 4]], 0, 0), [], ["G4"], **fl)
-    op("g", "iota", (T.G5[:], [[1, 4], [4, 4], [64, 2]], 0, 0), [], ["G5"], **fl)
-    op("g", "iota", (T.G6[:], [[48, 8]], 32, 0), [], ["G6"], **fl)
-    op("g", "iota", (T.IC4[:], [[1, 4]], 0, 0), [], ["IC4"], **fl)
-    send("P", lambda d: T.PP[d], T.PL[rank], "arrP", "locP", ["PP"])
-    send("S", lambda d: T.SS[d], T.SL[rank], "arrS", "locS", ["SS"])
-    op("g", "asel", (T.GA[:], T.FOUR[:], [[-16, 8], [0, 4]], A.is_ge, 0.0, 0, 1), ["FOUR"], ["GA"])
-    op("g", "asel", (T.GB[:], T.GA[:], [[16, 8], [0, 4]], A.is_ge, 0.0, 15, -1), ["GA"], ["GB"])
-    op("g", "asel", (T.TRI[:], T.ONE1[:], [[1, 128]], A.is_ge, 0.0, -1, -1), ["ONE1"], ["TRI"])
-    op("g", "iota", (T.G1[:], [[1, 16], [0, 4]], 0, 0), [], ["G1"], **fl)
-    op("g", "iota", (T.G2[:], [[0, 16], [64, 4]], 12288, 0), [], ["G2"], **fl)
+    V("memset", (T.MC[:, 112:114], 128.0), ["MC2"], ["MC2"])
+    V("memset", (T.M[:, 56:180:61], -1.0), ["M"], ["Mt"])
+    V("memset", (T.M[:, 57:180:61], 1.0), [], ["Mt"])
+    for c in range(4):
+        V("ts", (T.M[:, 8 * c:8 * c + 8], T.ID[:, :, c, 0], 128.0, None, A.mult), ["ID"], ["M0"])
+    for j in range(4):
+        for h in range(2):
+            V("ts", (T.M[32 * j:32 * j + 32, 32 + h:56:2], T.ID[32 * j:32 * j + 32, 2 * j + h, :, 1:4], float(4 ** j), None, A.mult), ["ID"], ["M0"])
+    for t in (1, 2):
+        V("copy", (T.M[:, 60 * t:60 * t + 56], T.M[:, 0:56]), ["M0"], ["M%d" % t])
+    for t in (2, 1, 0):
+        o = 68 * t
+        V("tt", (T.M[:, o:o + 16], T.M[:, o:o + 16], T.DP[:], A.add), ["M%d" % t, "DP"], ["M%d" % t])
+    G("iota", (T.UI[:], [[1, 8], [8, 4], [0, 2]], 0, 0), [], ["UI"], **fl)
+    G("iota", (T.RI[:], [[1, 16], [0, 4]], 0, 0), [], ["RI"], **fl)
+    G("iota", (T.CI[:], [[0, 16], [128, 4]], -256, 0), [], ["CI"], **fl)
+    G("iota", (T.CQ[:], [[4, 8], [1, 4]], 0, 0), [], ["CQ"], **fl)
+    G("iota", (T.VA[:], [[1, 4], [0, 4]], 0, 0), [], ["VA"], **fl)
+    G("iota", (T.VB[:], [[0, 4], [1, 4]], -60, 0), [], ["VB"], **fl)
+    send(plan(T, topo, rank, "P")[0], lambda d: T.PP[d], T.PL[rank], "arrP", "locP", ["PP"])
+    send(plan(T, topo, rank, "S")[0], lambda d: T.SS[d], T.SL[rank], "arrS", "locS", ["SS"])
 
-    col = lambda j: T.KF[:, j:j + 1]
-    for d, n, sh in ((2, 3, 0), (1, 15, 0), (3, 3, 2), (4, 1, 0), (5, 1, 1), (6, 7, 1), (7, 1, 0)):
-        V("ts", (T.KI[:, d:d + 1], T.KI[:, 0:1], sh, n, A.arith_shift_right, A.bitwise_and), ["KI0"], ["KI"])
-    V("copy", (T.KF[:, 0:8], T.KI[:, 0:8]), ["KI", "KI0"], ["KF"])
-    S("act", (col(8), col(2), AF.Exp), ["KF"], ["K8"], scale=float(np.log(64.0)))
-    for i in range(8):
-        V("ts", (T.PK[:, 128 * i:128 * i + 128], T.ID[:], float(4 ** i), None, A.mult), ["ID"], ["PK"])
+    def turn(n):
+        c0, b = 256 * n, n % 2
+        V("copy", (T.D[:, c0:c0 + 256], T.D32[:, c0:c0 + 256]), ["D32%d" % n], ["D%d" % n])
+        tile = lambda h: T.D[:, c0 + 128 * h:c0 + 128 * h + 128]
+        mms([(T.PV[:, 1024 * b + 128 * h:1024 * b + 128 * h + 128], tile(h), T.ID[:]) for h in range(2)], ["D%d" % n, "ID"], ["PV%d" % b])
+        mms([(PS[b][:, h], tile(h), T.ID[:], True, True) for h in range(2)], ["D%d" % n, "ID"], ["P%d" % b])
+        S("act", (T.G3[:, 256 * b:256 * b + 256], PS[b][:, 0:2], AF.Relu), ["P%d" % b], ["P%d" % b, "G3%d" % b], bias=-2.0)
 
-    def lin(j, src, k1, k2):
-        V("ts", (col(j), col(src), k1, k2, A.mult, A.add), ["KF"] if src < 8 else ["K%d" % src], ["K%d" % j])
+    def mix(n):
+        b, o = n % 2, 512 * (n % 4)
+        for t, F in ((1, T.G1), (2, T.G2)):
+            V("ts", (F[:, 256 * b:256 * b + 256], T.PV[:, 1024 * b:1024 * b + 256], float(t), None, A.is_ge), ["PV%d" % b] * (t == 1), ["PV%d" % b, "G%d%d" % (t, b)])
+        cs = [(T.PSA[:, o:o + 120], T.ONE1[0:1, :], T.MC[0:1, :], True, False)]
+        for t, F in ((2, T.G3), (0, T.G1), (1, T.G2)):
+            for h in range(2):
+                cs.append((T.PSA[:, o + h:o + 120:2], F[:, 256 * b + 128 * h:256 * b + 128 * h + 128], T.M[:, 60 * t:60 * t + 60], False, t == 1 and h == 1))
+        mms(cs, ["G1%d" % b, "G2%d" % b, "G3%d" % b, "M0", "M1", "M2", "Mt", "MC0", "MC1", "MC2", "ONE1"], ["A%d" % (n % 4)])
+        out, k = (T.SEND[:, 120 * n:120 * n + 120], "SX%d" % n) if n < 7 else (T.LR[:, rank, :], "LRs")
+        cp("a", out, T.PSA[:, o:o + 120], ["A%d" % (n % 4)], ["A%d" % (n % 4), k])
 
-    CH = 5.0 * float(np.log(2.0))
-    for s in range(8):
-        c0 = 256 * s
-        V("copy", (T.D[:, c0:c0 + 256], T.D32[:, c0:c0 + 256]), ["D32%d" % s], ["D%d" % s])
-        S("act", (T.CE[:, c0:c0 + 256], T.D[:, c0:c0 + 256], AF.Exp), ["D%d" % s], ["CE%d" % s], scale=CH)
-    for f in range(4):
-        lo, hi = 512 * f, 512 * f + 512
-        mms([(T.PSA[:, lo:lo + 64], T.PK[:, 128 * i:128 * i + 128], T.D[:, lo + i:hi:8], i == 0, i == 7) for i in range(8)],
-            ["D%d" % (2 * f), "D%d" % (2 * f + 1), "PK"], ["A%d" % f])
-        if f % 2 == 1:
-            hh = f // 2
-            lo, hi, o = 1024 * hh, 1024 * hh + 1024, 512 * hh
-            mms([(T.PSB[:, o:o + 64], T.ID[:], T.CE[:, lo + q:hi:16], q == 0, q == 15) for q in range(16)],
-                ["CE%d" % s for s in range(4 * hh, 4 * hh + 4)] + ["ID"], ["B%d" % hh])
-    sk = []
-    for f in range(4):
-        for s in (2 * f, 2 * f + 1):
-            o = 512 * f + 32 * (s % 2)
-            V("ts", (T.SEND[:, 48 * s:48 * s + 32], T.PSA[:, o:o + 32], 128.0, None, A.add), ["A%d" % f], ["SX%d" % s])
-            sk.append("SX%d" % s)
-    for hh in range(2):
-        for s in (4 * hh, 4 * hh + 1, 4 * hh + 2, 4 * hh + 3):
-            o = 512 * hh + 16 * (s % 4)
-            cp("a" if hh == 0 else "v", T.SEND[:, 48 * s + 32:48 * s + 48], T.PSB[:, o:o + 16], ["B%d" % hh], ["SC%d" % s])
-            sk.append("SC%d" % s)
-    send("X", lambda d: T.SEND[:, 48 * d:48 * d + 48], T.LR[:, 48 * rank:48 * rank + 48], "arrX", "locX", sk)
-    V("copy", (T.LR[:, 48 * rank:48 * rank + 48], T.SEND[:, 48 * rank:48 * rank + 48]), ["SX%d" % rank, "SC%d" % rank], ["LRs"])
+    src = lambda d: T.SEND[:, 120 * order.index(d):120 * order.index(d) + 120]
+    calls = plan(T, topo, rank, "X")
+    for n in range(9):
+        if n < 8:
+            turn(n)
+        if n > 0:
+            mix(n - 1)
+        if n in (4, 7):
+            send(calls[n // 7], src, T.LR[:, rank, :], "arrX", "locX", ["SX%d" % order.index(d) for d, _ in calls[n // 7]])
 
     V("memset", (T.ONE2[:], 1.0), [], ["ONE2"])
-    op("g", "asel", (T.SEL[:], T.ONE2[:, 0:128 * NPE], [[-16, NPE], [0, 8], [-1, 16]], A.is_equal, 0.0, 0, 1), ["ONE2"], ["SEL"])
-    lin(28, 6, 48.0, 0.0)
-    lin(21, 2, 128.0, 0.0)
-    lin(22, 3, 16.0, 0.0)
-    lin(13, 4, -12800.0, 51200.0)
-    lin(16, 5, -13056.0, 0.0)
-    V("tt", (col(14), col(4), col(5), A.mult), ["KF"], ["K14"])
-    V("tt", (col(29), col(28), col(7), A.add), ["K28", "KF"], ["K29"])
-    V("tt", (col(23), col(21), col(22), A.add), ["K21", "K22"], ["K23"])
-    V("tt", (col(17), col(13), col(16), A.add), ["K13", "K16"], ["K17"])
-    lin(15, 14, -38144.0, 0.0)
-    lin(31, 14, -1.0, 1.0)
-    V("ts", (T.OFX[:], T.G4[:], col(29), None, A.add), ["G4", "K29"], ["OFX"])
-    V("ts", (T.OFC[:], T.G6[:], col(1), None, A.add), ["G6", "KF"], ["OFC"])
-    V("ts", (T.OFF[:], T.G5[:], col(23), None, A.add), ["G5", "K23"], ["OFF"])
-    V("tt", (col(18), col(17), col(15), A.add), ["K17", "K15"], ["K18"])
-    V("memset", (T.MK[:], 1.0), [], ["MK0"])
-    V("memset", (T.ONE32[:], 1.0), [], ["ONE32"])
-    V("memset", (T.BASE[:, 0:1], 0.0), [], ["BASE0"])
-    V("ts", (T.INI[:], T.ID[:], col(18), None, A.mult), ["ID", "K18"], ["INI"])
-    V("memset", (T.TB[:, 3:2048:4], 0.0), [], ["TB3"])
-    V("memset", (T.DB[:, 3:2048:4], 0.0), [], ["DB3"])
-    V("ts", (T.IDP[:], T.ID[:], 1.25, None, A.mult), ["ID"], ["IDP"])
-    V("ts", (T.IDN[:], T.ID[:], -1.25, None, A.mult), ["ID"], ["IDN"])
-    V("memset", (T.MK[:, 0:512:16], 0.0), ["MK0"], ["MK"])
-    V("copy", (T.LW[:, 0:4], T.IC4[:]), ["IC4"], ["LW"])
-    V("ts", (T.SELL[:, 0:8], T.GB[:, 0:32:4], 1.0 / 64, None, A.mult), ["GB"], ["SELL"])
-    L0 = 1536
-    V("memset", (T.PSB[:, L0 + 240:L0 + 256], 0.0), [], ["B3z"])
-    mms([(T.PSA[:, 512 * b:512 * b + 512], T.INI[:], T.ONE2[:, 0:512], True, False) for b in range(4)], ["INI", "ONE2"], ["A0", "A1", "A2", "A3"])
+    G("asel", (T.TRI[:], T.ONE1[:], [[1, 128]], A.is_ge, 0.0, -1, -1), ["ONE1"], ["TRI"])
+    G("asel", (T.GA[:], T.FOUR[:], [[0, 2], [-16, 8], [0, 4]], A.is_ge, 0.0, 0, 1), ["FOUR"], ["GA"])
+    G("asel", (T.GB[:], T.GA[:], [[0, 2], [16, 8], [0, 4]], A.is_ge, 0.0, 14, -1), ["GA"], ["GB"])
+    G("asel", (T.SEL[:], T.ONE2[:], [[-16, NPE], [0, 8], [-1, 16]], A.is_equal, 0.0, 0, 1), ["ONE2"], ["SEL"])
+    for d, n, sh in ((1, 15, 0), (2, 3, 2), (3, 7, 4), (4, 1, 0), (5, 1, 1), (6, 31, 2)):
+        V("ts", (T.KI[:, d:d + 1], T.KI[:, 0:1], sh, n, A.arith_shift_right, A.bitwise_and), ["KI0"], ["KI"])
+    V("memset", (T.TB[:, :, 0, :], 0.0), [], ["TB0"])
+    V("copy", (T.KF[:, 0:7], T.KI[:, 0:7]), ["KI", "KI0"], ["KF"])
+    V("memset", (T.TB[:, :, 1:4, 12:16], -102400.0), [], ["TB3"])
+
+    def lin(j, src, k1, k2):
+        V("ts", (col(j), col(src), k1, k2, A.mult, A.add), ["KF"] if src < 7 else ["K%d" % src], ["K%d" % j])
+
+    def two(j, a, b, o):
+        V("tt", (col(j), col(a), col(b), o), ["KF" if a < 7 else "K%d" % a, "KF" if b < 7 else "K%d" % b], ["K%d" % j])
+
+    two(8, 4, 5, A.mult)
+    two(9, 4, 5, A.max)
+    lin(10, 2, 8.0, 8.0)
+    lin(11, 5, 63.0, 1.0)
+    lin(12, 5, -63.0 / 64, 1.0)
+    lin(13, 5, -4.0, 4.0)
+    V("ts", (T.W0[:], T.RI[:], col(1), 128.0, A.is_gt, A.mult), ["RI", "KF"], ["W0"])
+    V("ts", (T.L0[:], T.VA[:], col(1), -BIG, A.not_equal, A.mult), ["VA", "KF"], ["L0"])
+    V("ts", (T.EQ[:], T.CQ[:], col(6), None, A.is_equal), ["CQ", "KF"], ["EQ"])
+    lin(14, 8, 252.0, 4.0)
+    lin(15, 8, -63.0 / 64, 1.0)
+    two(16, 9, 8, A.subtract)
+    V("ts", (col(17), col(10), col(3), -8.0, A.add, A.add), ["K10", "KF"], ["K17"])
+    lin(24, 9, -81679.0, 143.0)
+    V("tt", (T.W[:, 0:64], T.W0[:], T.CI[:], A.add), ["W0", "CI"], ["W"])
+    V("tt", (T.LW[:], T.L0[:], T.VB[:], A.add), ["L0", "VB"], ["LW"])
+    two(18, 11, 14, A.mult)
+    V("ts", (col(19), col(12), col(15), col(9), A.mult, A.mult), ["K12", "K15", "K9"], ["K19"])
+    lin(20, 16, -64.0, 0.0)
+    lin(21, 16, 32.0, 0.0)
+    V("ts", (T.MASK[:, 0:64], T.UI[:], col(17), None, A.is_lt), ["UI", "K17"], ["MASK0"])
+    V("ts", (T.MASK[:, 64:128], T.UI[:], col(10), None, A.is_lt), ["UI", "K10"], ["MASK1"])
+    V("memset", (T.AD[:, :, 0, :], 0.0), [], ["AD0"])
+    lin(22, 19, 1.0 / 64, 0.0)
+    V("ts", (col(23), col(9), 81664.0, col(21), A.mult, A.add), ["K9", "K21"], ["K23"])
+    V("ts", (T.SELY[:, 0:32], T.EQ[:], col(18), None, A.mult), ["EQ", "K18"], ["SELY0"])
+    V("ts", (T.SELY[:, 32:64], T.EQ[:], col(13), None, A.mult), ["EQ", "K13"], ["SELY1"])
+    V("memset", (T.CON[:], 0.0), [], ["CON0"])
+    V("memset", (T.RST[:], 1.0), [], ["RST0"])
+    V("memset", (T.NX[:, 48:64], -60.0), [], ["NX1"])
+    V("ts", (T.SELZ[:], T.SELY[:], -1.0, None, A.mult), ["SELY0", "SELY1"], ["SELZ"])
+    for p0, x, y in ((0, 0xC30000, 6144), (32, 0x1600, 2), (64, 0xFC, 0)):
+        V("memset", (T.CON[p0:p0 + 32, 0:64], float(x)), ["CON0"], ["CON"])
+        if y:
+            V("memset", (T.CON[p0:p0 + 32, 64:128], float(y)), [], ["CON"])
+    V("memset", (T.RST[:, 0:64:4], 0.0), ["RST0"], ["RST"])
+    for h in range(2):
+        cp("a", T.SELQ[:, 32 * h:32 * h + 32], T.ID[:, :, 0, :], ["ID"], ["SELQ%d" % h])
+    for w in (64, 128, 256, 512):
+        cp("a", T.W[:, w:2 * w], T.W[:, 0:w], ["W"], ["W"])
+    cp("a", T.W[:, 1024:1088], T.W[:, 0:64], ["W"], ["W"])
 
     dma("s", T.PT[:], T.PL[:], "lpt", ["PL", "PLs"], ["PT"])
     dma("s", T.ST[:], T.SL[:], "lst", ["SL", "SLs"], ["ST"])
-    V("copy", (T.OFP[:], T.PT[:]), ["PT"], ["OFP"])
-    V("copy", (T.PTB[:], T.PT[:]), ["PT"], ["PTB"])
-    S("act", (T.LTR[:, 0:1024], T.LW[:, 0:4].indirect(T.OFP[:, 0:64]), AF.Copy), ["LW", "OFP"], ["LTR0"])
-    V("copy", (T.LTR[:, 1024:2048], T.LW[:, 0:4].indirect(T.OFP[:, 64:128])), ["LW", "OFP"], ["LTR1"])
-    tau = lambda t: t // 2 + (4 if t % 2 else 0)
-    cs = []
-    for t in range(8):
-        o = L0 + 16 * (t // 2) + (128 if t % 2 else 0)
-        for blk in range(2):
-            cs.append((T.PSB[:, o + 8 * blk:o + 8 * blk + 8], T.LTR[:, 256 * t + 128 * blk:256 * t + 128 * blk + 128], T.SELL[:, 0:8], True, True))
-    for t in range(1, 8):
-        o = L0 + 64 + 16 * ((t - 1) // 2) + (0 if t % 2 else 128)
-        cs.append((T.PSB[:, o:o + 16], T.ID[:], T.PTB[:, 16 * t:16 * t + 16], True, True))
-    mms(cs, ["LTR0", "LTR1", "SELL", "PTB", "ID", "B3z"], ["B3"])
+    V("ts", (T.P4[:], T.PT[:, :, 0, :], 4.0, None, A.mult), ["PT"], ["P4"])
+    for c in range(4):
+        V("ts", (T.AM[:, 64 * c:64 * c + 64], T.PT[:, :, 1, :], float(c), -BIG, A.not_equal, A.mult), ["PT"], ["AM%d" % c])
+    V("tt", (T.PI[:], T.P4[:], T.PT[:, :, 1, :], A.add), ["P4", "PT"], ["PI"])
+    V("ts", (T.NX[:, 0:48], T.PT[:, 1:4, 0, :], -60.0, None, A.add), ["PT"], ["NX0"])
+    V("copy", (T.OFP[:], T.PI[:]), ["PI"], ["OFP"])
+    S("act", (T.LTR[:], T.LW[:, 0:16].indirect(T.OFP[:, 0:64]), AF.Copy), ["LW", "OFP"], ["LTR"])
+    for c in range(4):
+        V("tt", (T.QTB[:, :, 0, :, c], T.AM[:, 64 * c:64 * c + 64], T.NX[:], A.add), ["AM%d" % c, "NX0", "NX1"], ["QTB0"])
+    V("ts", (T.ST4[:], T.ST[:], 4.0, None, A.mult), ["ST"], ["ST4"])
+    V("copy", (T.QTB[:, :, 1], T.QTB[:, :, 0]), ["QTB0"], ["QTB1"])
+    for h in range(2):
+        V("tt", (T.I[:, 16 * h:16 * h + 16], T.ST4[:, 16 * h:16 * h + 16], T.PT[:, 0, 0, :], A.add), ["ST4", "PT"], ["I"])
+    V("ts", (T.J[:], T.I[:], 63, None, A.bitwise_and), ["I"], ["J"])
+    for h in range(2):
+        V("ts", (T["OA%d" % h][:], T.I[:, 16 * h:16 * h + 16], 1.0 / 64, -0.5 + 0.5 / 64, A.mult, A.add), ["I"], ["OA:%d" % h])
+    for h in range(2):
+        V("copy", (T["OB%d" % h][:], T.J[:, 16 * h:16 * h + 16]), ["J"], ["OB:%d" % h])
 
-    V("copy", (T.CI[:], T.LR[:, 0:384].indirect(T.OFC[:, 0:8])), ["LR", "LRs", "OFC"], ["CI"])
-    S("act", (T.H[:], T.LR[:, 0:384].indirect(T.OFX[:, 0:16]), AF.Copy), ["LR", "LRs", "OFX"], ["H"], scale=(1.0 + 2.0 ** -17) / 256, bias=RND)
-    S("act", (T.LXP[:, 1:512:2], T.H[:], AF.Copy), ["H"], ["LXP1"], bias=-RND - 129.0)
-    LXK = ["LXP0", "LXP1"]
+    LK = ["LR", "LRs"]
+    tot = lambda h: T.LR[:, :, 112 + h:120:2]
+    before = lambda h: T.PS0[:, 0, 0, h:64:2]
+    mms([(before(0), T.TRI[:], tot(0), True, False), (before(0), T.TRI[:], tot(1), False, True),
+         (before(1), T.TRI[:], tot(0), True, False), (before(1), T.TRI[:], tot(1), False, False),
+         (before(1), T.ID[:], tot(0), False, True)], LK + ["TRI", "ID"], ["P0"])
+    mms([(T.PS1[:, 0, h], T.ONE1[:], T.LR[:, :, 112:120], True, True) for h in range(2)], LK + ["ONE1"], ["P1"])
 
-    def planes(e, lst):
-        for x in lst.split():
-            name, i = "T" + x[1], int(x[2])
-            k, sc = i + (x[1] == "B"), 64.0 / 4 ** i
-            args, wr = (T[name][:, 1024 * e + i:1024 * e + 1024:4], T.LXP[:, 256 * e:256 * e + 256]), ["%s%d%d" % (name, i, e)]
-            if x[0] == "v":
-                V("ts", args + (B_T[k] + 128.0, sc, A.add, A.mult), LXK, wr)
-            else:
-                S("act", args + (AF.Copy,), LXK, wr, scale=sc, bias=sc * (B_T[k] + 128.0))
+    def plane(x):
+        j = int(x[2])
+        if x[1] == "U":
+            cp(x[0], T.TA[:, :, 0, :], T.LR[:, :, 0:64], LK, ["TAU"])
+            return
+        k = j + (x[1] == "B")
+        add = TOFF[k] + (((160.0 if j else 0.0) if x[1] == "A" else (800.0 if j else 640.0)) * 4 ** j)
+        sc = (128.0 if x[1] == "A" else -128.0) / 4 ** j
+        args, wr = (T["T" + x[1]][:, :, 1:4, 4 * j:4 * j + 4], T.LR[:, :, 64:112]), ["T" + x[1:]]
+        if x[0] == "v":
+            V("ts", args + (add, sc, A.add, A.mult), LK, wr)
+        else:
+            S("act", args + (AF.Copy,), LK, wr, scale=sc, bias=sc * add)
 
-    def cx(c):
-        V("ts", (T.CX[:, 128 * c:128 * c + 128], T.CI[:], 5 * c, 31, A.arith_shift_right, A.bitwise_and), ["CI"], ["CX"])
-    cx(0)
-    cx(1)
-    V("ts", (T.HM[:], T.H[:], -RND, -256.0, A.add, A.mult), ["H"], ["HM"])
-    cx(2)
-    V("tt", (T.LXP[:, 0:512:2], T.LR[:, 0:384].indirect(T.OFX[:, 0:16]), T.HM[:], A.add), ["LR", "LRs", "OFX", "HM"], ["LXP0"])
-    cx(3)
-    V("copy", (T.NS[:, 1:512], T.CX[:, 0:511]), ["CX"], ["NS"])
-    V("copy", (T.N15[:], T.CX[:, 15:512:16]), ["CX"], ["N15"])
-    V("memset", (T.NS[:, 0:512:16], 0.0), ["NS"], ["NS"])
-    V("scan", (T.S1[:], T.MK[:], T.NS[:], 0.0, A.mult, A.add), ["MK", "NS"], ["S1"])
-    planes(0, P0)
-    for j, (m, k) in enumerate(((T.ONE1[:], "ONE1"), (T.TRI[:], "TRI"))):
-        o = T.PSB[:, 512 + 512 * j:544 + 512 * j]
-        mms([(o, m, T.S1[:, 15:512:16], True, False), (o, m, T.N15[:], False, True)], ["S1", "N15", k], ["B%d" % (1 + j)])
-    V("scan", (T.BASE[:, 1:33], T.ONE32[:], T.PSB[:, 512:544], 0.0, A.mult, A.add), ["B1", "ONE32"], ["B1", "BASE"])
-    V("tt", (T.NS[:, 0:512:16], T.PSB[:, 1024:1056], T.BASE[:, 0:32], A.add), ["B2", "BASE", "BASE0"], ["B2", "NS"])
-    V("scan", (T.F[:], T.MK[:], T.NS[:], 0.0, A.mult, A.add), ["MK", "NS"], ["F"])
-    planes(1, P1)
+    pl = PLANES.split()
+    for x in pl:
+        if x[0] == "a":
+            plane(x)
+    pl = [x for x in pl if x[0] == "v"]
+    plane(pl[0])
+    V("copy", (T.NI[:], T.PS0[:, 0, 0]), ["P0"], ["P0", "NI"])
+    V("tt", (T.MS[:], T.PS1[:, 0], T.MASK[:], A.mult), ["P1", "MASK0", "MASK1"], ["P1", "MS"])
+    plane(pl[1])
+    for i, (sh, n) in enumerate(((0, 63), (6, 63), (12, 63))):
+        V("ts", (T.DI[:, :, i, :], T.NI[:], sh, n, A.arith_shift_right, A.bitwise_and), ["NI"], ["DI"])
+    for h in range(2):
+        V("red", (T.BX[:, h:h + 1], T.MS[:, 64 * h:64 * h + 64], AxisListType.X, A.add), ["MS"], ["BX0"])
+    V("copy", (T.AD[:, :, 1:4, :], T.DI[:]), ["DI"], ["AD"])
+    V("ts", (T.BI[:, 2:4], T.BX[:, 0:2], 0.25, col(22), A.add, A.mult), ["BX0", "K22"], ["BI1"])
+    V("ts", (T.BI[:, 0:2], T.BX[:, 0:2], 0.25, col(19), A.add, A.mult), ["BX0", "K19"], ["BI0"])
+    plane(pl[2])
+    V("ts", (T.BX[:, 2:4], T.BI[:, 2:4], col(20), col(23), A.mult, A.add), ["BI1", "K20", "K23"], ["BX1"])
+    plane(pl[3])
+    V("tt", (T.BX[:, 4:6], T.BI[:, 0:2], T.BX[:, 2:4], A.add), ["BI0", "BX1"], ["BX2"])
+    for x in pl[4:]:
+        plane(x)
     PO = lambda b, m: T.PSA[:, 512 * b + m:512 * b + 512:4]
-
-    def letters_turned(e):
-        for b in (2 * e, 2 * e + 1):
-            cs = []
-            for m in range(4):
-                x0 = 128 * (4 * b + m)
-                cs += [(PO(b, m), T.TA[:, x0:x0 + 128], T.IDP[:], False, False), (PO(b, m), T.TB[:, x0:x0 + 128], T.IDN[:], False, False)]
-            mms(cs, ["TA%d%d" % (i, e) for i in range(4)] + ["TB%d%d" % (i, e) for i in range(3)] + ["TB3", "IDP", "IDN"], ["A%d" % b])
-
-    def xc(b):
-        cp(XCQ[b], T.XC[:, b:2048:4], T.PSA[:, 512 * b:512 * b + 512], ["A%d" % b], ["A%d" % b, "XC%d" % b])
-
+    slot = lambda b, m: 2 * (b + 4 * (m % 2)) + m // 2
     for e in range(2):
-        n0, n1, m0, m1 = 256 * e, 256 * e + 256, 1024 * e, 1024 * e + 1024
-        V("copy", (T.NI[:, n0:n1], T.F[:, 0:512].indirect(T.OFF[:, 16 * e:16 * e + 16])), ["F", "OFF"], ["NI%d" % e])
-        letters_turned(e)
-        S("act", (T.DB[:, m0 + 2:m1:4], T.F[:, 0:512].indirect(T.OFF[:, 16 * e:16 * e + 16]), AF.Copy), ["F", "OFF"], ["DB2%d" % e],
-          scale=2.0 ** -12, bias=191.5 + 2.0 ** -13)
-        if e == 0:
-            planes(1, P2)
-        for i in range(2):
-            V("ts", (T.DI[:, 512 * i + n0:512 * i + n1], T.NI[:, n0:n1], 6 * i, 63, A.arith_shift_right, A.bitwise_and), ["NI%d" % e], ["DI%d%d" % (i, e)])
-        for i in range(2):
-            V("ts", (T.DB[:, m0 + i:m1:4], T.DI[:, 512 * i + n0:512 * i + n1], -64.0, None, A.add), ["DI%d%d" % (i, e)], ["DB%d%d" % (i, e)])
+        for x, j in (("A", e), ("B", e), ("A", e + 2), ("B", e + 2)):
+            for b in (2 * e, 2 * e + 1):
+                mms([(PO(b, m), T["T" + x][:, :, :, slot(b, m)], T.ID[:], (x, j, m) == ("A", e, 0), False) for m in (j // 2, j // 2 + 2)],
+                    ["TAU" if x == "A" else "TB0", "T%s%d" % (x, j), "ID"], ["A%d" % b])
         for b in (2 * e, 2 * e + 1):
-            mms([(PO(b, m), T.DB[:, 128 * (4 * b + m):128 * (4 * b + m) + 128], T.ID[:], False, m == 3) for m in range(4)],
-                ["DB%d%d" % (i, e) for i in range(3)] + ["DB3", "ID"], ["A%d" % b])
-            xc(b)
-    for c in range(4):
-        V("ts", (T.AM[:, 128 * c:128 * c + 128], T.PSB[:, L0:L0 + 128], float(c), -float(BIG), A.not_equal, A.mult), ["B3"], ["AM%d" % c])
-    for c in range(4):
-        V("tt", (T.QTB[:, c:512:4], T.PSB[:, L0 + 128:L0 + 256], T.AM[:, 128 * c:128 * c + 128], A.add), ["B3", "B3z", "AM%d" % c], ["QTB%d" % c])
+            mms([(PO(b, m), T.AD[:, :, :, m // 2], T.ID[:], False, m == 3) for m in range(4)], ["AD", "AD0", "ID"], ["A%d" % b])
+    for b in range(4):
+        args, rd, wr = (T.XC[:, b:2048:4], T.PSA[:, 512 * b:512 * b + 512]), ["A%d" % b, "BX2"], ["A%d" % b, "XC%d" % b]
+        if XCQ[b] == "v":
+            V("ts", args + (T.BX[:, 4:5], None, A.add), rd, wr)
+        else:
+            S("act", args + (AF.Identity,), rd, wr, bias=T.BX[:, 4:5])
+    V("ts", (T.X[:, 16384:16385], T.BX[:, 5:6], col(24), None, A.add), ["BX2", "K24"], ["XE"])
 
     XK, XCK = ["XE"], ["XC%d" % b for b in range(4)]
     for k in range(NPE, 8):
         for y in range(8):
             dma("s", T.X[16 * y:16 * y + 16, 2048 * k:2048 * k + 2048], T.XC[16 * k:16 * k + 16, :], "rep", XCK, ["XD%d%d" % (k, y)])
             XK.append("XD%d%d" % (k, y))
-    small = [
-        lambda: V("memset", (T.RST[:], 1.0), [], ["RST0"]),
-        lambda: V("ts", (T.EM[:, 0:4], T.IC4[:], col(3), col(31), A.is_equal, A.mult), ["IC4", "KF", "K31"], ["EM"]),
-        lambda: V("ts", (T.G3[:], T.G1[:], col(1), None, A.is_gt), ["G1", "KF"], ["G3"]),
-        lambda: V("memset", (T.RST[:, 0:64:4], 0.0), ["RST0"], ["RST"]),
-        lambda: V("ts", (col(30), T.EM[:, 0:1], 7712.0, None, A.mult), ["EM"], ["K30"]),
-        lambda: V("tt", (T.EV[:, 0:4], T.EM[:, 0:4], T.BASE[:, 8:33:8], A.mult), ["EM", "BASE"], ["EV"]),
-        lambda: V("tt", (T.W[:], T.G3[:], T.G2[:], A.mult), ["G3", "G2"], ["W"]),
-        lambda: V("ts", (T.CON[:], T.ONE1[:, 0:64], col(8), col(30), A.mult, A.mult), ["ONE1", "K8", "K30"], ["CON"]),
-        lambda: V("ts", (T.ST4[:], T.ST[:], 4.0, None, A.mult), ["ST"], ["ST4"]),
-        lambda: V("red", (T.EV[:, 4:5], T.EV[:, 0:4], AxisListType.X, A.add), ["EV"], ["EV4"]),
-        lambda: lin(9, 4, -63.0 / 64, 1.0),
-        lambda: lin(10, 5, -4095.0 / 4096, 1.0),
-    ] + [
-        lambda c=c: V("ts", (T.SELY[:, c:32:4], T.GB[:, c:32:4], col(8), T.EM[:, c:c + 1], A.mult, A.mult), ["GB", "K8", "EM"], ["SELY"]) for c in range(4)
-    ] + [
-        lambda: V("tt", (col(11), col(9), col(10), A.mult), ["K9", "K10"], ["K11"]),
-    ] + [
-        lambda h=h: V("tt", (T["I%d" % h][:], T.ST4[:, 16 * h:16 * h + 16], T.PT[:, 0:16], A.add), ["ST4", "PT"], ["I%d" % h]) for h in range(2)
-    ] + [
-        lambda: lin(12, 11, 0.5, -0.5),
-        lambda: V("ts", (T.SELZ[:], T.SELY[:], -1.25, None, A.mult), ["SELY"], ["SELZ"]),
-        lambda: lin(26, 5, 64.0, -64.0),
-        lambda: lin(27, 14, 64.0, -64.0),
-        lambda: V("ts", (T.EI[:, 0:1], T.EV[:, 4:5], col(11), col(12), A.mult, A.add), ["EV4", "K11", "K12"], ["EI0"]),
-        lambda: V("ts", (T.EI[:, 1:2], T.EI[:, 0:1], 6, None, A.arith_shift_right), ["EI0"], ["EI1"]),
-        lambda: V("ts", (T.EV[:, 6:7], T.EI[:, 1:2], col(26), col(27), A.mult, A.add), ["EI1", "K26", "K27"], ["EV6"]),
-        lambda: V("tt", (T.X[:, 16384:16385], T.EI[:, 0:1], T.EV[:, 6:7], A.add), ["EI0", "EV6"], ["XE"]),
-    ]
+    ring = [(T.PS0[:], "P0"), (T.PS1[:], "P1")] + [(T.PSA[:, 512 * b:512 * b + 512], "A%d" % b) for b in range(2)]
     n = 0
     for b in range(4):
         for k in range(NPE):
-            pb = n % 3
-            mms([(T.PSB[:, 512 * pb:512 * pb + 512], T.SEL[:, 128 * k:128 * k + 128], T.XC[:, b:2048:4], True, True)], ["XC%d" % b, "SEL"], ["B%d" % pb])
-            cp(XQ[n], T.X[:, 2048 * k + b:2048 * k + 2048:4], T.PSB[:, 512 * pb:512 * pb + 512], ["B%d" % pb], ["B%d" % pb, "X%d" % n])
+            ps, pk = ring[n % 4]
+            mms([(ps, T.SEL[:, 128 * k:128 * k + 128], T.XC[:, b:2048:4], True, True)], ["XC%d" % b, "SEL"], [pk])
+            cp("av"[n % 2], T.X[:, 2048 * k + b:2048 * k + 2048:4], ps, [pk], [pk, "X%d" % n])
             XK.append("X%d" % n)
-            if XQ[n] == "v":
-                for f in small[:5]:
-                    f()
-                del small[:5]
             n += 1
-    for f in small:
-        f()
 
-    B = lambda name, n: T[("S1B" if name == "S" and n % 2 else "%s%d" % (name, n % 2))]
+    B = lambda name, n: T["L%dS" % (n % 2) if name == "L" else "%s%d" % (name, n % 2)]
     key = lambda name, n: "%s:%d" % (name, n % 2)
-    for h in range(2):
-        last["I:%d" % h] = last["I%d" % h]
-    QK = ["QTB%d" % c for c in range(4)]
+    out = lambda n, k: PS[n % 2][:, 0, :, 32 * k:32 * k + 32]
 
     def state(n):
-        ps, pk = 512 * (n % 2), "A%d" % (n % 2)
-        V("scan", (B("S", n)[:], T.RST[:], T.PSA[:, ps:ps + 64], 0.0, A.mult, A.max), [pk, "RST"], [pk, key("S", n)])
+        pk = "P%d" % (n % 2)
+        V("scan", (B("S", n)[:], T.RST[:], PS[n % 2][:, 0, 0], 0.0, A.mult, A.max), [pk, "RST"], [pk, key("S", n)])
+
+    def low(n):
+        pk = "P%d" % (n % 2)
+        V("scan", (B("L", n)[:], T.RST[:], PS[n % 2][:, 0, 1], 0.0, A.mult, A.max), [pk, "RST"], [pk, key("L", n)])
 
     def block(n):
-        ps, pk = 512 * (n % 2), "A%d" % (n % 2)
-        src, sk = (B("I", n)[:], key("I", n)) if n < 2 else (B("S", n)[:, 3:64:4], key("S", n))
-        V("ts", (B("OA", n)[:], src, 1.0 / 64, -0.5 + 0.5 / 64, A.mult, A.add), [sk], [key("OA", n)])
+        if n >= 2:
+            V("ts", (B("OA", n)[:], B("S", n)[:, 3:64:4], 1.0 / 64, -0.5 + 0.5 / 64, A.mult, A.add), [key("S", n)], [key("OA", n)])
         S("act", (B("Z", n)[:], T.X[:, 0:16385].indirect(B("OA", n)[:, 0:16]), AF.Copy), [key("OA", n)] + XK, [key("Z", n)])
-        S("act", (B("ZL", n)[:], B("Z", n)[:], AF.Copy), [key("Z", n)], [key("ZL", n)], scale=0.8, bias=12313.6)
-        mms([(T.PSA[:, ps:ps + 64], T.ONE1[:], T.CON[:], True, False)], ["ONE1", "CON"], [pk])
+        S("act", (B("ZL", n)[:], B("Z", n)[:], AF.Copy), [key("Z", n)], [key("ZL", n)], bias=24512.5)
 
     def table(n):
-        t, ps, pk, Z, ZL = n // 2, 512 * (n % 2), "A%d" % (n % 2), B("Z", n), B("ZL", n)
-        q0 = 64 * tau(t)
-        cs = [(T.PSA[:, ps + 32 * k:ps + 32 * k + 32], ZL[:, 128 * k:128 * k + 128], T.SELZ[:], False, False) for k in range(2)]
-        cs += [(T.PSA[:, ps:ps + 64], T.ID[:], T.QTB[:, q0:q0 + 64], False, False)]
-        cs += [(T.PSA[:, ps + 32 * k:ps + 32 * k + 32], Z[:, 128 * k:128 * k + 128], T.SELY[:], False, False) for k in range(2)]
-        mms(cs, [key("Z", n), key("ZL", n), "ID", "SELY", "SELZ"] + QK, [pk])
+        t, pk, Z, ZL = n // 2, "P%d" % (n % 2), B("Z", n), B("ZL", n)
+        mms([(PS[n % 2][:, 0], T.ONE1[:], T.CON[:], True, False)], ["ONE1", "CON"], [pk])
+        cs = [(out(n, k), ZL[:, 128 * k:128 * k + 128], T.SELZ[:], False, False) for k in range(2)]
+        if t % 2:
+            cs += [(PS[n % 2][:, 0], T.ID[:], T.QTB[:, t // 2], False, False)]
+        else:
+            cs += [(out(n, k), T.LTR[:, 128 * (t + k):128 * (t + k) + 128], T.SELQ[:], False, False) for k in range(2)]
+        cs += [(out(n, k), Z[:, 128 * k:128 * k + 128], T.SELY[:], False, False) for k in range(2)]
+        mms(cs, [key("Z", n), key("ZL", n), "ID", "SELY0", "SELY1", "SELZ", "SELQ0", "SELQ1", "LTR", "QTB0", "QTB1"], [pk])
 
     def count(n):
-        ps, pk, ZL, E = 512 * (n % 2), "A%d" % (n % 2), B("ZL", n), B("E", n)
-        V("tt", (E[:], T.W[:, 0:64].indirect(B("OB", n)[:, 0:16]), ZL[:], A.is_equal), [key("OB", n), "W", key("ZL", n)], [key("E", n)])
-        mms([(T.PSA[:, ps + 32 * k:ps + 32 * k + 32], E[:, 128 * k:128 * k + 128], T.GB[:], False, k == 1) for k in range(2)],
-            [key("E", n), "GB"], [pk])
+        pk, E = "P%d" % (n % 2), B("E", n)
+        V("tt", (E[:], T.W[:, 0:1088].indirect(B("OB", n)[:, 0:16]), B("Z", n)[:], A.is_gt), [key("OB", n), "W", key("Z", n)], [key("E", n)])
+        mms([(out(n, k), E[:, 128 * k:128 * k + 128], T.GB[:], False, k == 1) for k in range(2)], [key("E", n), "GB"], [pk])
 
     for n in range(18):
         if n >= 2:
             state(n)
-        if 0 < n < 17:
-            V("copy", (B("OB", n - 1)[:], B("J", n - 1)[:]), [key("J", n - 1)], [key("OB", n - 1)])
+        if 2 < n < 17:
+            V("copy", (B("OB", n - 1)[:], B("L", n - 1)[:, 3:64:4]), [key("L", n - 1)], [key("OB", n - 1)])
         if n < 16:
             block(n)
         else:
@@ -424,12 +426,10 @@ def rank_program(g, core, T, topo):
         if 0 < n < 17:
             table(n - 1)
             count(n - 1)
-        if n < 16:
-            if n >= 2:
-                V("copy", (B("I", n)[:], B("S", n)[:, 3:64:4]), [key("S", n)], [key("I", n)])
-            V("ts", (B("J", n)[:], B("I", n)[:], 63, None, A.bitwise_and), [key("I", n)], [key("J", n)])
+        if 2 <= n < 16:
+            low(n)
     dma("s", T.RD[:], T.RES[:], "rd", ["RES0", "RES1"], ["RD"])
-    send("F", lambda d: T.RD[d], T.FL[rank], "arrF", "locF", ["RD"])
+    send(plan(T, topo, rank, "F")[0], lambda d: T.RD[d], T.FL[rank], "arrF", "locF", ["RD"])
     r0, r1 = 16 * rank, 16 * rank + 16
     dma("s", T.y[r0:r1, :], T.RES[r0:r1, :], "yself", ["RES0", "RES1"], ["y0"])
     if rank > 0:

@@ -1,3 +1,4 @@
+import math
 from concourse.bass import DstId, RemoteDMATransfer
 from concourse.mybir import AluOpType as A, AxisListType, ActivationFunctionType as AF
 
@@ -24,7 +25,7 @@ for _n, _w, _d in (
         ("ONE1", 128, "bfloat16"), ("ONE2", 128 * NPE, "bfloat16"), ("FOUR", 64, "bfloat16"), ("GA", 64, "bfloat16"), ("GB", 64, "bfloat16"),
         ("ID", [8, 4, 4], "bfloat16"), ("CON", 128, "bfloat16"), ("TRI", 128, "bfloat16"), ("SEL", 128 * NPE, "bfloat16"),
         ("SELY", 64, "bfloat16"), ("SELZ", 64, "bfloat16"), ("SELQ", 64, "bfloat16"), ("EQ", 32, "bfloat16"), ("CQ", 32, "float32"),
-        ("KI", 8, "int32"), ("KF", 32, "float32"), ("RI", 64, "float32"), ("CI", 64, "float32"), ("W0", 64, "float32"),
+        ("KI", 8, "int32"), ("KF", 16, "float32"), ("KB", 8, "bfloat16"), ("UC", 64, "float32"), ("RI", 64, "float32"), ("CI", 64, "float32"), ("W0", 64, "float32"),
         ("VA", 16, "float32"), ("VB", 16, "float32"), ("L0", 16, "float32"),
         ("W", 1088, "bfloat16"), ("LW", 16, "bfloat16"), ("PT", [4, 2, 16], "int32"), ("ST", 32, "int32"), ("ST4", 32, "int32"),
         ("P4", 64, "int32"), ("PI", 64, "int32"), ("OFP", 64, "uint16"), ("LTR", 1024, "bfloat16"), ("AM", 256, "float32"), ("NX", 64, "float32"),
@@ -163,14 +164,19 @@ def rank_program(g, core, T, topo):
     V("memset", (T.ONE1[:], 1.0), [], ["ONE1"])
     V("memset", (T.DPI[:, 0:8], -1.0), [], ["DPI0"])
     V("memset", (T.DPI[:, 8:16], 1.0), [], ["DPI1"])
+    G("iota", (T.KI[:, 0:1], [[0, 1]], 0, 1), [], ["KI0"])
     G("asel", (T.ID[:], T.ONE1[:], [[-1, 128]], A.is_equal, 0.0, 0, 1), ["ONE1"], ["ID"])
     G("asel", (T.DP[:], T.DPI[:], [[15, 2], [16, 8]], A.is_ge, 0.0, -1, -1), ["DPI0", "DPI1"], ["DP"])
     G("iota", (T.MC[:, 0:16], [[16, 8], [0, 2]], -241, 0), [], ["MC0"], **fl)
-    G("iota", (T.KI[:, 0:1], [[0, 1]], 0, 1), [], ["KI0"])
     V("memset", (T.MC[:, 16:64], -256.0), [], ["MC1"])
     V("memset", (T.MC[:, 64:120], 0.0), [], ["MC2"])
+    V("ts", (T.KI[:, 1:2], T.KI[:, 0:1], 3, None, A.bitwise_and), ["KI0"], ["KI1"])
     V("memset", (T.M[:], 0.0), [], ["M"])
     V("memset", (T.FOUR[:], 4.0), [], ["FOUR"])
+    V("copy", (col(1), T.KI[:, 1:2]), ["KI1"], ["K1"])
+    S("act", (col(0), col(1), AF.Relu), ["K1"], ["K0"], bias=-1.0)
+    S("act", (T.KB[:, 0:1], col(1), AF.Exp), ["K1"], ["KB0"], scale=-math.log(64.0), bias=math.log(64.0))
+    S("act", (T.KB[:, 1:2], col(0), AF.Exp), ["K0"], ["KB1"], scale=math.log(64.0), bias=math.log(4.0))
     V("memset", (T.MC[:, 112:114], 128.0), ["MC2"], ["MC2"])
     V("memset", (T.M[:, 56:180:61], -1.0), ["M"], ["Mt"])
     V("memset", (T.M[:, 57:180:61], 1.0), [], ["Mt"])
@@ -185,6 +191,7 @@ def rank_program(g, core, T, topo):
         o = 68 * t
         V("tt", (T.M[:, o:o + 16], T.M[:, o:o + 16], T.DP[:], A.add), ["M%d" % t, "DP"], ["M%d" % t])
     G("iota", (T.UI[:], [[1, 8], [8, 4], [0, 2]], 0, 0), [], ["UI"], **fl)
+    G("iota", (T.UC[:], [[0, 8], [1, 4], [0, 2]], 0, 0), [], ["UC"], **fl)
     G("iota", (T.RI[:], [[1, 16], [0, 4]], 0, 0), [], ["RI"], **fl)
     G("iota", (T.CI[:], [[0, 16], [128, 4]], -256, 0), [], ["CI"], **fl)
     G("iota", (T.CQ[:], [[4, 8], [1, 4]], 0, 0), [], ["CQ"], **fl)
@@ -223,55 +230,35 @@ def rank_program(g, core, T, topo):
         if n in (4, 7):
             send(calls[n // 7], src, T.LR[:, rank, :], "arrX", "locX", ["SX%d" % order.index(d) for d, _ in calls[n // 7]])
 
+    for out, n, x, k in ((T.TB[:, :, 0, :], 512, -81920.0, "TB0"), (T.TB[:, :, 1:4, 12:16], 384, -102400.0, "TB3")):
+        S("act", (out, T.D[:, 0:n], AF.Copy), ["D0", "D1"], [k], scale=0.0, bias=x)
     V("memset", (T.ONE2[:], 1.0), [], ["ONE2"])
     G("asel", (T.TRI[:], T.ONE1[:], [[1, 128]], A.is_ge, 0.0, -1, -1), ["ONE1"], ["TRI"])
     G("asel", (T.GA[:], T.FOUR[:], [[0, 2], [-16, 8], [0, 4]], A.is_ge, 0.0, 0, 1), ["FOUR"], ["GA"])
     G("asel", (T.GB[:], T.GA[:], [[0, 2], [16, 8], [0, 4]], A.is_ge, 0.0, 14, -1), ["GA"], ["GB"])
     G("asel", (T.SEL[:], T.ONE2[:], [[-16, NPE], [0, 8], [-1, 16]], A.is_equal, 0.0, 0, 1), ["ONE2"], ["SEL"])
-    for d, n, sh in ((1, 15, 0), (2, 3, 2), (3, 7, 4), (4, 1, 0), (5, 1, 1), (6, 31, 2)):
+    for d, n, sh in ((2, 15, 0), (3, 3, 2), (4, 7, 4), (5, 31, 2)):
         V("ts", (T.KI[:, d:d + 1], T.KI[:, 0:1], sh, n, A.arith_shift_right, A.bitwise_and), ["KI0"], ["KI"])
-    V("memset", (T.TB[:, :, 0, :], 0.0), [], ["TB0"])
-    V("copy", (T.KF[:, 0:7], T.KI[:, 0:7]), ["KI", "KI0"], ["KF"])
-    V("memset", (T.TB[:, :, 1:4, 12:16], -102400.0), [], ["TB3"])
-
-    def lin(j, src, k1, k2):
-        V("ts", (col(j), col(src), k1, k2, A.mult, A.add), ["KF"] if src < 7 else ["K%d" % src], ["K%d" % j])
-
-    def two(j, a, b, o):
-        V("tt", (col(j), col(a), col(b), o), ["KF" if a < 7 else "K%d" % a, "KF" if b < 7 else "K%d" % b], ["K%d" % j])
-
-    two(8, 4, 5, A.mult)
-    two(9, 4, 5, A.max)
-    lin(10, 2, 8.0, 8.0)
-    lin(11, 5, 63.0, 1.0)
-    lin(12, 5, -63.0 / 64, 1.0)
-    lin(13, 5, -4.0, 4.0)
-    V("ts", (T.W0[:], T.RI[:], col(1), 128.0, A.is_gt, A.mult), ["RI", "KF"], ["W0"])
-    V("ts", (T.L0[:], T.VA[:], col(1), -BIG, A.not_equal, A.mult), ["VA", "KF"], ["L0"])
-    V("ts", (T.EQ[:], T.CQ[:], col(6), None, A.is_equal), ["CQ", "KF"], ["EQ"])
-    lin(14, 8, 252.0, 4.0)
-    lin(15, 8, -63.0 / 64, 1.0)
-    two(16, 9, 8, A.subtract)
-    V("ts", (col(17), col(10), col(3), -8.0, A.add, A.add), ["K10", "KF"], ["K17"])
-    lin(24, 9, -81679.0, 143.0)
+    V("memset", (T.AD[:, :, 0, :], 224.0), [], ["AD0"])
+    V("ts", (col(6), col(1), 3.0, -64.0, A.not_equal, A.mult), ["K1"], ["K6"])
+    V("copy", (T.KF[:, 2:6], T.KI[:, 2:6]), ["KI"], ["KF"])
+    V("ts", (col(7), col(1), 2.0, 4.0, A.is_lt, A.mult), ["K1"], ["K7"])
+    V("ts", (col(8), col(1), 0.0, -17.0, A.is_equal, A.mult), ["K1"], ["K8"])
+    V("ts", (col(9), col(3), 8.0, col(4), A.mult, A.add), ["KF"], ["K9"])
+    V("ts", (T.MASK[:, 64:128], T.UC[:], col(3), None, A.is_le), ["UC", "KF"], ["MASK1"])
+    V("ts", (T.W0[:], T.RI[:], col(2), 128.0, A.is_gt, A.mult), ["RI", "KF"], ["W0"])
+    V("ts", (T.MASK[:, 0:64], T.UI[:], col(9), None, A.is_lt), ["UI", "K9"], ["MASK0"])
+    V("ts", (T.L0[:], T.VA[:], col(2), -BIG, A.not_equal, A.mult), ["VA", "KF"], ["L0"])
+    V("ts", (T.EQ[:], T.CQ[:], col(5), None, A.is_equal), ["CQ", "KF"], ["EQ"])
     V("tt", (T.W[:, 0:64], T.W0[:], T.CI[:], A.add), ["W0", "CI"], ["W"])
     V("tt", (T.LW[:], T.L0[:], T.VB[:], A.add), ["L0", "VB"], ["LW"])
-    two(18, 11, 14, A.mult)
-    V("ts", (col(19), col(12), col(15), col(9), A.mult, A.mult), ["K12", "K15", "K9"], ["K19"])
-    lin(20, 16, -64.0, 0.0)
-    lin(21, 16, 32.0, 0.0)
-    V("ts", (T.MASK[:, 0:64], T.UI[:], col(17), None, A.is_lt), ["UI", "K17"], ["MASK0"])
-    V("ts", (T.MASK[:, 64:128], T.UI[:], col(10), None, A.is_lt), ["UI", "K10"], ["MASK1"])
-    V("memset", (T.AD[:, :, 0, :], 0.0), [], ["AD0"])
-    lin(22, 19, 1.0 / 64, 0.0)
-    V("ts", (col(23), col(9), 81664.0, col(21), A.mult, A.add), ["K9", "K21"], ["K23"])
-    V("ts", (T.SELY[:, 0:32], T.EQ[:], col(18), None, A.mult), ["EQ", "K18"], ["SELY0"])
-    V("ts", (T.SELY[:, 32:64], T.EQ[:], col(13), None, A.mult), ["EQ", "K13"], ["SELY1"])
+    V("ts", (T.SELY[:, 0:32], T.EQ[:], T.KB[:, 1:2], None, A.mult), ["EQ", "KB1"], ["SELY0"])
+    V("ts", (T.SELY[:, 32:64], T.EQ[:], col(7), None, A.mult), ["EQ", "K7"], ["SELY1"])
     V("memset", (T.CON[:], 0.0), [], ["CON0"])
     V("memset", (T.RST[:], 1.0), [], ["RST0"])
     V("memset", (T.NX[:, 48:64], -60.0), [], ["NX1"])
     V("ts", (T.SELZ[:], T.SELY[:], -1.0, None, A.mult), ["SELY0", "SELY1"], ["SELZ"])
-    for p0, x, y in ((0, 0xC30000, 6144), (32, 0x1600, 2), (64, 0xFC, 0)):
+    for p0, x, y in ((0, 0xC20000, 6144), (32, 0xD600, 2), (64, 0xFC, 0)):
         V("memset", (T.CON[p0:p0 + 32, 0:64], float(x)), ["CON0"], ["CON"])
         if y:
             V("memset", (T.CON[p0:p0 + 32, 64:128], float(y)), [], ["CON"])
@@ -279,29 +266,37 @@ def rank_program(g, core, T, topo):
     for h in range(2):
         cp("a", T.SELQ[:, 32 * h:32 * h + 32], T.ID[:, :, 0, :], ["ID"], ["SELQ%d" % h])
     for w in (64, 128, 256, 512):
-        cp("a", T.W[:, w:2 * w], T.W[:, 0:w], ["W"], ["W"])
-    cp("a", T.W[:, 1024:1088], T.W[:, 0:64], ["W"], ["W"])
+        cp("v", T.W[:, w:2 * w], T.W[:, 0:w], ["W"], ["W"])
+    cp("v", T.W[:, 1024:1088], T.W[:, 0:64], [], ["W"])
 
     dma("s", T.PT[:], T.PL[:], "lpt", ["PL", "PLs"], ["PT"])
     dma("s", T.ST[:], T.SL[:], "lst", ["SL", "SLs"], ["ST"])
-    V("ts", (T.P4[:], T.PT[:, :, 0, :], 4.0, None, A.mult), ["PT"], ["P4"])
-    for c in range(4):
-        V("ts", (T.AM[:, 64 * c:64 * c + 64], T.PT[:, :, 1, :], float(c), -BIG, A.not_equal, A.mult), ["PT"], ["AM%d" % c])
-    V("tt", (T.PI[:], T.P4[:], T.PT[:, :, 1, :], A.add), ["P4", "PT"], ["PI"])
-    V("ts", (T.NX[:, 0:48], T.PT[:, 1:4, 0, :], -60.0, None, A.add), ["PT"], ["NX0"])
-    V("copy", (T.OFP[:], T.PI[:]), ["PI"], ["OFP"])
-    S("act", (T.LTR[:], T.LW[:, 0:16].indirect(T.OFP[:, 0:64]), AF.Copy), ["LW", "OFP"], ["LTR"])
-    for c in range(4):
-        V("tt", (T.QTB[:, :, 0, :, c], T.AM[:, 64 * c:64 * c + 64], T.NX[:], A.add), ["AM%d" % c, "NX0", "NX1"], ["QTB0"])
-    V("ts", (T.ST4[:], T.ST[:], 4.0, None, A.mult), ["ST"], ["ST4"])
-    V("copy", (T.QTB[:, :, 1], T.QTB[:, :, 0]), ["QTB0"], ["QTB1"])
-    for h in range(2):
-        V("tt", (T.I[:, 16 * h:16 * h + 16], T.ST4[:, 16 * h:16 * h + 16], T.PT[:, 0, 0, :], A.add), ["ST4", "PT"], ["I"])
-    V("ts", (T.J[:], T.I[:], 63, None, A.bitwise_and), ["I"], ["J"])
-    for h in range(2):
-        V("ts", (T["OA%d" % h][:], T.I[:, 16 * h:16 * h + 16], 1.0 / 64, -0.5 + 0.5 / 64, A.mult, A.add), ["I"], ["OA:%d" % h])
-    for h in range(2):
-        V("copy", (T["OB%d" % h][:], T.J[:, 16 * h:16 * h + 16]), ["J"], ["OB:%d" % h])
+
+    def pairs():
+        V("ts", (T.P4[:], T.PT[:, :, 0, :], 4.0, None, A.mult), ["PT"], ["P4"])
+        V("ts", (T.NX[:, 0:48], T.PT[:, 1:4, 0, :], -60.0, None, A.add), ["PT"], ["NX0"])
+        V("tt", (T.PI[:], T.P4[:], T.PT[:, :, 1, :], A.add), ["P4", "PT"], ["PI"])
+        for c in range(2):
+            V("ts", (T.AM[:, 64 * c:64 * c + 64], T.PT[:, :, 1, :], float(c), -BIG, A.not_equal, A.mult), ["PT"], ["AM%d" % c])
+        V("copy", (T.OFP[:], T.PI[:]), ["PI"], ["OFP"])
+        for c in range(2, 4):
+            V("ts", (T.AM[:, 64 * c:64 * c + 64], T.PT[:, :, 1, :], float(c), -BIG, A.not_equal, A.mult), ["PT"], ["AM%d" % c])
+
+    def spread(u):
+        S("act", (T.LTR[:, 512 * u:512 * u + 512], T.LW[:, 0:16].indirect(T.OFP[:, 32 * u:32 * u + 32]), AF.Copy), ["LW", "OFP"], ["LTR%d" % u])
+
+    def starts():
+        V("ts", (T.ST4[:], T.ST[:], 4.0, None, A.mult), ["ST"], ["ST4"])
+        for c in range(4):
+            V("tt", (T.QTB[:, :, 0, :, c], T.AM[:, 64 * c:64 * c + 64], T.NX[:], A.add), ["AM%d" % c, "NX0", "NX1"], ["QTB0"])
+        for h in range(2):
+            V("tt", (T.I[:, 16 * h:16 * h + 16], T.ST4[:, 16 * h:16 * h + 16], T.PT[:, 0, 0, :], A.add), ["ST4", "PT"], ["I"])
+        V("copy", (T.QTB[:, :, 1], T.QTB[:, :, 0]), ["QTB0"], ["QTB1"])
+        V("ts", (T.J[:], T.I[:], 63, None, A.bitwise_and), ["I"], ["J"])
+        for h in range(2):
+            V("ts", (T["OA%d" % h][:], T.I[:, 16 * h:16 * h + 16], 1.0 / 64, -0.5 + 0.5 / 64, A.mult, A.add), ["I"], ["OA:%d" % h])
+        for h in range(2):
+            V("copy", (T["OB%d" % h][:], T.J[:, 16 * h:16 * h + 16]), ["J"], ["OB:%d" % h])
 
     LK = ["LR", "LRs"]
     tot = lambda h: T.LR[:, :, 112 + h:120:2]
@@ -339,10 +334,10 @@ def rank_program(g, core, T, topo):
     for h in range(2):
         V("red", (T.BX[:, h:h + 1], T.MS[:, 64 * h:64 * h + 64], AxisListType.X, A.add), ["MS"], ["BX0"])
     V("copy", (T.AD[:, :, 1:4, :], T.DI[:]), ["DI"], ["AD"])
-    V("ts", (T.BI[:, 2:4], T.BX[:, 0:2], 0.25, col(22), A.add, A.mult), ["BX0", "K22"], ["BI1"])
-    V("ts", (T.BI[:, 0:2], T.BX[:, 0:2], 0.25, col(19), A.add, A.mult), ["BX0", "K19"], ["BI0"])
+    V("ts", (T.BI[:, 2:4], T.BX[:, 0:2], T.KB[:, 0:1], 1.0 / 64, A.mult, A.mult), ["BX0", "KB0"], ["BI1"])
+    V("ts", (T.BI[:, 0:2], T.BX[:, 0:2], T.KB[:, 0:1], None, A.mult), ["BX0", "KB0"], ["BI0"])
     plane(pl[2])
-    V("ts", (T.BX[:, 2:4], T.BI[:, 2:4], col(20), col(23), A.mult, A.add), ["BI1", "K20", "K23"], ["BX1"])
+    V("ts", (T.BX[:, 2:4], T.BI[:, 2:4], col(6), 81696.0, A.mult, A.add), ["BI1", "K6"], ["BX1"])
     plane(pl[3])
     V("tt", (T.BX[:, 4:6], T.BI[:, 0:2], T.BX[:, 2:4], A.add), ["BI0", "BX1"], ["BX2"])
     for x in pl[4:]:
@@ -356,13 +351,18 @@ def rank_program(g, core, T, topo):
                     ["TAU" if x == "A" else "TB0", "T%s%d" % (x, j), "ID"], ["A%d" % b])
         for b in (2 * e, 2 * e + 1):
             mms([(PO(b, m), T.AD[:, :, :, m // 2], T.ID[:], False, m == 3) for m in range(4)], ["AD", "AD0", "ID"], ["A%d" % b])
+    pairs()
     for b in range(4):
         args, rd, wr = (T.XC[:, b:2048:4], T.PSA[:, 512 * b:512 * b + 512]), ["A%d" % b, "BX2"], ["A%d" % b, "XC%d" % b]
         if XCQ[b] == "v":
             V("ts", args + (T.BX[:, 4:5], None, A.add), rd, wr)
         else:
             S("act", args + (AF.Identity,), rd, wr, bias=T.BX[:, 4:5])
-    V("ts", (T.X[:, 16384:16385], T.BX[:, 5:6], col(24), None, A.add), ["BX2", "K24"], ["XE"])
+        if b == 0:
+            spread(0)
+        if b == 1:
+            V("ts", (T.X[:, 16384:16385], T.BX[:, 5:6], col(8), -81536.0, A.add, A.add), ["BX2", "K8"], ["XE"])
+            starts()
 
     XK, XCK = ["XE"], ["XC%d" % b for b in range(4)]
     for k in range(NPE, 8):
@@ -378,6 +378,7 @@ def rank_program(g, core, T, topo):
             cp("av"[n % 2], T.X[:, 2048 * k + b:2048 * k + 2048:4], ps, [pk], [pk, "X%d" % n])
             XK.append("X%d" % n)
             n += 1
+    spread(1)
 
     B = lambda name, n: T["L%dS" % (n % 2) if name == "L" else "%s%d" % (name, n % 2)]
     key = lambda name, n: "%s:%d" % (name, n % 2)
@@ -391,43 +392,42 @@ def rank_program(g, core, T, topo):
         pk = "P%d" % (n % 2)
         V("scan", (B("L", n)[:], T.RST[:], PS[n % 2][:, 0, 1], 0.0, A.mult, A.max), [pk, "RST"], [pk, key("L", n)])
 
+    half = lambda name, n, k: B(name, n)[:, 128 * k:128 * k + 128]
+    hkey = lambda name, n, k: key(name, n) + str(k)
+
     def block(n):
         if n >= 2:
             V("ts", (B("OA", n)[:], B("S", n)[:, 3:64:4], 1.0 / 64, -0.5 + 0.5 / 64, A.mult, A.add), [key("S", n)], [key("OA", n)])
-        S("act", (B("Z", n)[:], T.X[:, 0:16385].indirect(B("OA", n)[:, 0:16]), AF.Copy), [key("OA", n)] + XK, [key("Z", n)])
-        S("act", (B("ZL", n)[:], B("Z", n)[:], AF.Copy), [key("Z", n)], [key("ZL", n)], bias=24512.5)
+        for k in range(2):
+            S("act", (half("Z", n, k), T.X[:, 0:16385].indirect(B("OA", n)[:, 8 * k:8 * k + 8]), AF.Copy), [key("OA", n)] + XK, [hkey("Z", n, k)])
+        for k in range(2):
+            S("act", (half("ZL", n, k), half("Z", n, k), AF.Copy), [hkey("Z", n, k)], [hkey("ZL", n, k)], bias=24512.5)
 
-    def table(n):
-        t, pk, Z, ZL = n // 2, "P%d" % (n % 2), B("Z", n), B("ZL", n)
-        mms([(PS[n % 2][:, 0], T.ONE1[:], T.CON[:], True, False)], ["ONE1", "CON"], [pk])
-        cs = [(out(n, k), ZL[:, 128 * k:128 * k + 128], T.SELZ[:], False, False) for k in range(2)]
-        if t % 2:
-            cs += [(PS[n % 2][:, 0], T.ID[:], T.QTB[:, t // 2], False, False)]
-        else:
-            cs += [(out(n, k), T.LTR[:, 128 * (t + k):128 * (t + k) + 128], T.SELQ[:], False, False) for k in range(2)]
-        cs += [(out(n, k), Z[:, 128 * k:128 * k + 128], T.SELY[:], False, False) for k in range(2)]
-        mms(cs, [key("Z", n), key("ZL", n), "ID", "SELY0", "SELY1", "SELZ", "SELQ0", "SELQ1", "LTR", "QTB0", "QTB1"], [pk])
-
-    def count(n):
-        pk, E = "P%d" % (n % 2), B("E", n)
-        V("tt", (E[:], T.W[:, 0:1088].indirect(B("OB", n)[:, 0:16]), B("Z", n)[:], A.is_gt), [key("OB", n), "W", key("Z", n)], [key("E", n)])
-        mms([(out(n, k), E[:, 128 * k:128 * k + 128], T.GB[:], False, k == 1) for k in range(2)], [key("E", n), "GB"], [pk])
+    def count(n, k):
+        t, pk = n // 2, "P%d" % (n % 2)
+        if k == 0:
+            mms([(PS[n % 2][:, 0], T.ONE1[:], T.CON[:], True, False)], ["ONE1", "CON"], [pk])
+        nxt = (T.ID[:], T.QTB[:, t // 2, :, 8 * k:8 * k + 8, :]) if t % 2 else (T.LTR[:, 128 * (t + k):128 * (t + k) + 128], T.SELQ[:])
+        mms([(out(n, k),) + x + (False, False) for x in ((half("ZL", n, k), T.SELZ[:]), nxt, (half("Z", n, k), T.SELY[:]))],
+            [hkey("Z", n, k), hkey("ZL", n, k), "ID", "SELY0", "SELY1", "SELZ", "SELQ0", "SELQ1", "LTR%d" % (t // 4), "QTB0", "QTB1"], [pk])
+        V("tt", (half("E", n, k), T.W[:, 0:1088].indirect(B("OB", n)[:, 8 * k:8 * k + 8]), half("Z", n, k), A.is_gt),
+          [key("OB", n), "W", hkey("Z", n, k)], [hkey("E", n, k)])
+        mms([(out(n, k), half("E", n, k), T.GB[:], False, k == 1)], [hkey("E", n, k), "GB"], [pk])
 
     for n in range(18):
         if n >= 2:
             state(n)
-        if 2 < n < 17:
-            V("copy", (B("OB", n - 1)[:], B("L", n - 1)[:, 3:64:4]), [key("L", n - 1)], [key("OB", n - 1)])
+        if 0 < n < 17:
+            count(n - 1, 0)
         if n < 16:
             block(n)
         else:
-            h = n % 2
-            V("ts", (T.RES[:, 16 * h:16 * h + 16], B("S", n)[:, 3:64:4], 0.25, None, A.mult), [key("S", n)], ["RES%d" % h])
+            V("ts", (T.RES[:, 16 * (n % 2):16 * (n % 2) + 16], B("S", n)[:, 3:64:4], 0.25, None, A.mult), [key("S", n)], ["RES%d" % (n % 2)])
         if 0 < n < 17:
-            table(n - 1)
-            count(n - 1)
+            count(n - 1, 1)
         if 2 <= n < 16:
             low(n)
+            V("copy", (B("OB", n)[:], B("L", n)[:, 3:64:4]), [key("L", n)], [key("OB", n)])
     dma("s", T.RD[:], T.RES[:], "rd", ["RES0", "RES1"], ["RD"])
     send(plan(T, topo, rank, "F")[0], lambda d: T.RD[d], T.FL[rank], "arrF", "locF", ["RD"])
     r0, r1 = 16 * rank, 16 * rank + 16

@@ -2,10 +2,17 @@ import math
 from concourse.bass import DstId, RemoteDMATransfer
 from concourse.mybir import AluOpType as A, AxisListType, ActivationFunctionType as AF
 
-NPE = 5
+NON = 4
+CPE = 9216
+NPE = -(-CPE // 2048)
+XQ = "av"
+RW = 120
+LQ = "asssssss"
+SENDS = (1, 3, 5, 6)
 BIG = 2097152.0
 TOFF = (0.0, -1.5, -7.5, -31.5)
-PLANES = "aA0 vU0 vB0 aA2 vB2 aA1 vB1 vA3"
+PLANES = "aA0 vB0 vU0 aA2 vB2 aA1 vB1 vA3"
+TURNS = "B3 B0 A0 A2 B2 A1 D0 B1 A3 D1"
 XCQ = "avav"
 
 SCRATCH = {
@@ -16,48 +23,46 @@ SCRATCH = {
     "PS0": ("psum", [128, 4, 2, 64], "float32"), "PS1": ("psum", [128, 4, 2, 64], "float32"),
 }
 for _n, _w, _d in (
-        ("D32", 2048, "int32"), ("D", 2048, "bfloat16"), ("G1", 512, "bfloat16"), ("G2", 512, "bfloat16"), ("G3", 512, "bfloat16"),
-        ("SEND", 960, "bfloat16"), ("LR", [8, 120], "bfloat16"), ("M", 180, "bfloat16"), ("MC", 120, "bfloat16"),
+        ("D32", 2048, "int32"), ("D", 2048, "bfloat16"), ("G1", 2048, "bfloat16"), ("G2", 2048, "bfloat16"), ("G3", 2048, "bfloat16"),
+        ("SEND", [8, RW], "bfloat16"), ("LR", [8, RW], "bfloat16"), ("M", 180, "bfloat16"), ("MC", RW, "bfloat16"),
         ("DPI", 16, "bfloat16"), ("DP", 16, "bfloat16"),
         ("TA", [32, 4, 16], "bfloat16"), ("TB", [32, 4, 16], "bfloat16"), ("AD", [32, 4, 2], "bfloat16"),
         ("NI", 64, "int32"), ("DI", [32, 3, 2], "int32"), ("UI", 64, "float32"), ("MASK", 128, "float32"), ("MS", 128, "float32"),
         ("BX", 8, "float32"), ("BI", 4, "int32"), ("XC", 2048, "bfloat16"), ("X", 16400, "bfloat16"),
         ("ONE1", 128, "bfloat16"), ("ONE2", 128 * NPE, "bfloat16"), ("FOUR", 64, "bfloat16"), ("GA", 64, "bfloat16"), ("GB", 64, "bfloat16"),
-        ("ID", [8, 4, 4], "bfloat16"), ("CON", 128, "bfloat16"), ("TRI", 128, "bfloat16"), ("SEL", 128 * NPE, "bfloat16"),
+        ("ID", [8, 4, 4], "bfloat16"), ("CON", 64, "bfloat16"), ("TRI", 128, "bfloat16"), ("SEL", 128 * NPE, "bfloat16"),
         ("SELY", 64, "bfloat16"), ("SELZ", 64, "bfloat16"), ("SELQ", 64, "bfloat16"), ("EQ", 32, "bfloat16"), ("CQ", 32, "float32"),
         ("KI", 8, "int32"), ("KF", 16, "float32"), ("KB", 8, "bfloat16"), ("UC", 64, "float32"), ("RI", 64, "float32"), ("CI", 64, "float32"), ("W0", 64, "float32"),
         ("VA", 16, "float32"), ("VB", 16, "float32"), ("L0", 16, "float32"),
         ("W", 1088, "bfloat16"), ("LW", 16, "bfloat16"), ("PT", [4, 2, 16], "int32"), ("ST", 32, "int32"), ("ST4", 32, "int32"),
         ("P4", 64, "int32"), ("PI", 64, "int32"), ("OFP", 64, "uint16"), ("LTR", 1024, "bfloat16"), ("AM", 256, "float32"), ("NX", 64, "float32"),
         ("QTB", [4, 2, 16, 4], "bfloat16"), ("RST", 64, "float32"), ("RES", 32, "float32"), ("I", 32, "int32"), ("J", 32, "int32"),
-        ("OA0", 16, "uint16"), ("OB0", 16, "uint16"), ("S0", 64, "float32"), ("L0S", 64, "float32"),
-        ("Z0", 256, "bfloat16"), ("ZL0", 256, "bfloat16"), ("E0", 256, "bfloat16"),
-        ("OA1", 16, "uint16"), ("OB1", 16, "uint16"), ("S1", 64, "float32"), ("L1S", 64, "float32"),
-        ("Z1", 256, "bfloat16"), ("ZL1", 256, "bfloat16"), ("E1", 256, "bfloat16")):
+        ("O", [4, 16], "uint16"), ("SC", 256, "float32"), ("Z", 512, "bfloat16"), ("ZL", 512, "bfloat16"), ("E", 512, "bfloat16")):
     SCRATCH[_n] = ("sbuf", [128] + (_w if isinstance(_w, list) else [_w]), _d)
 SEMAPHORES = (["vq", "aq", "pq", "gq", "dp", "ds", "dsp", "dss", "lpt", "lst", "rep", "yself", "yout", "rd",
                "arrP", "arrS", "arrX", "arrF", "locP", "locS", "locX", "locF"] + ["b%d" % _i for _i in range(8)])
 
 
-def others(T, topo, rank):
-    core = T.cores[rank]
-    off = [d for d in range(8) if d != rank and topo.chip(T.cores[d]) != topo.chip(core)]
-    on = [d for d in range(8) if d != rank and topo.chip(T.cores[d]) == topo.chip(core)]
-    off.sort(key=lambda d: (topo.same_plane(topo.chip(core), topo.chip(T.cores[d])), (d - rank) % 8))
-    return off, on
+def far_first(T, topo, rank):
+    chip = lambda d: topo.chip(T.cores[d])
+    return sorted((d for d in range(8) if d != rank), key=lambda d: (chip(d) == chip(rank), topo.same_plane(chip(rank), chip(d)), (d - rank) % 8))
 
 
 def plan(T, topo, rank, kind):
     core = T.cores[rank]
-    off, on = others(T, topo, rank)
+    order = far_first(T, topo, rank)
+    off, on = order[:6], order[6]
     eo = topo.engines(core, T.cores[off[0]])
-    en = [e for e in topo.engines(core, T.cores[on[0]]) if e not in eo]
+    en = [e for e in topo.engines(core, T.cores[on]) if e not in eo][:NON]
     if kind == "X":
-        c1 = [(d, eo[2 * i:2 * i + 2]) for i, d in enumerate(off[:4])]
-        c2 = [(d, eo[4 * i:4 * i + 4]) for i, d in enumerate(off[4:])] + [(d, en[:2]) for d in on]
-        return [c1, c2]
-    sh = 2 if kind == "S" else 0
-    return [[(d, [eo[i + sh]]) for i, d in enumerate(off)] + [(d, [en[sh // 2]]) for d in on]]
+        calls = []
+        for a, b in zip((0,) + tuple(n + 1 for n in SENDS), SENDS):
+            w = len(eo) // max(len(off[a:b + 1]), 1)
+            calls.append([(d, eo[w * i:w * i + w]) for i, d in enumerate(off[a:b + 1])] + [(on, en)] * (b == 6))
+        return calls
+    if kind == "P":
+        return [[(off[0], eo[0:2]), (off[1], eo[2:4])] + [(d, [eo[4 + i]]) for i, d in enumerate(off[2:])] + [(on, en[:1])]]
+    return [[(d, [eo[i]]) for i, d in enumerate(off)] + [(on, en[:1])]]
 
 
 def rank_program(g, core, T, topo):
@@ -151,12 +156,11 @@ def rank_program(g, core, T, topo):
         else:
             S("act", (out, in_, AF.Copy), rd, wr)
 
-    off, on = others(T, topo, rank)
-    order = off + on + [rank]
+    order = far_first(T, topo, rank) + [rank]
     dma("s", T.PP[:], T.pats[:], "dp", [], ["PP"])
-    dma("s", T.SS[:], T.starts[:], "ds", [], ["SS"])
     for n, s in enumerate(order):
-        dma("s" if n in (3, 5, 6, 7) else "a", T.D32[:, 256 * n:256 * n + 256], T.bwt[s:s + 1, :], "b%d" % n, [], ["D32%d" % n])
+        dma(LQ[n], T.D32[:, 256 * n:256 * n + 256], T.bwt[s:s + 1, :], "b%d" % n, [], ["D32%d" % n])
+    dma("s", T.SS[:], T.starts[:], "ds", [], ["SS"])
     dma("s", T.PL[rank], T.pats[16 * rank:16 * rank + 16, :], "dsp", [], ["PLs"])
     dma("s", T.SL[rank], T.starts[16 * rank:16 * rank + 16, :], "dss", [], ["SLs"])
 
@@ -169,14 +173,15 @@ def rank_program(g, core, T, topo):
     G("asel", (T.DP[:], T.DPI[:], [[15, 2], [16, 8]], A.is_ge, 0.0, -1, -1), ["DPI0", "DPI1"], ["DP"])
     G("iota", (T.MC[:, 0:16], [[16, 8], [0, 2]], -241, 0), [], ["MC0"], **fl)
     V("memset", (T.MC[:, 16:64], -256.0), [], ["MC1"])
-    V("memset", (T.MC[:, 64:120], 0.0), [], ["MC2"])
+    V("memset", (T.MC[:, 64:RW], 0.0), [], ["MC2"])
     V("ts", (T.KI[:, 1:2], T.KI[:, 0:1], 3, None, A.bitwise_and), ["KI0"], ["KI1"])
     V("memset", (T.M[:], 0.0), [], ["M"])
-    V("memset", (T.FOUR[:], 4.0), [], ["FOUR"])
+    V("memset", (T.FOUR[:, 0:32], 4.0), [], ["FOUR"])
+    V("memset", (T.FOUR[:, 32:64], 256.0), [], ["FOUR"])
     V("copy", (col(1), T.KI[:, 1:2]), ["KI1"], ["K1"])
     S("act", (col(0), col(1), AF.Relu), ["K1"], ["K0"], bias=-1.0)
     S("act", (T.KB[:, 0:1], col(1), AF.Exp), ["K1"], ["KB0"], scale=-math.log(64.0), bias=math.log(64.0))
-    S("act", (T.KB[:, 1:2], col(0), AF.Exp), ["K0"], ["KB1"], scale=math.log(64.0), bias=math.log(4.0))
+    S("act", (col(10), col(0), AF.Exp), ["K0"], ["K10"], scale=math.log(64.0), bias=math.log(4.0))
     V("memset", (T.MC[:, 112:114], 128.0), ["MC2"], ["MC2"])
     V("memset", (T.M[:, 56:180:61], -1.0), ["M"], ["Mt"])
     V("memset", (T.M[:, 57:180:61], 1.0), [], ["Mt"])
@@ -198,73 +203,70 @@ def rank_program(g, core, T, topo):
     G("iota", (T.VA[:], [[1, 4], [0, 4]], 0, 0), [], ["VA"], **fl)
     G("iota", (T.VB[:], [[0, 4], [1, 4]], -60, 0), [], ["VB"], **fl)
     send(plan(T, topo, rank, "P")[0], lambda d: T.PP[d], T.PL[rank], "arrP", "locP", ["PP"])
-    send(plan(T, topo, rank, "S")[0], lambda d: T.SS[d], T.SL[rank], "arrS", "locS", ["SS"])
 
     def turn(n):
         c0, b = 256 * n, n % 2
         V("copy", (T.D[:, c0:c0 + 256], T.D32[:, c0:c0 + 256]), ["D32%d" % n], ["D%d" % n])
         tile = lambda h: T.D[:, c0 + 128 * h:c0 + 128 * h + 128]
-        mms([(T.PV[:, 1024 * b + 128 * h:1024 * b + 128 * h + 128], tile(h), T.ID[:]) for h in range(2)], ["D%d" % n, "ID"], ["PV%d" % b])
         mms([(PS[b][:, h], tile(h), T.ID[:], True, True) for h in range(2)], ["D%d" % n, "ID"], ["P%d" % b])
-        S("act", (T.G3[:, 256 * b:256 * b + 256], PS[b][:, 0:2], AF.Relu), ["P%d" % b], ["P%d" % b, "G3%d" % b], bias=-2.0)
+        mms([(T.PV[:, 1024 * b + 128 * h:1024 * b + 128 * h + 128], tile(h), T.ID[:]) for h in range(2)], ["D%d" % n, "ID"], ["PV%d" % b])
+        S("act", (T.G3[:, c0:c0 + 256], PS[b][:, 0:2], AF.Relu), ["P%d" % b], ["P%d" % b, "G3%d" % n], bias=-2.0)
 
     def mix(n):
-        b, o = n % 2, 512 * (n % 4)
+        c0, b, d, o, pk = 256 * n, n % 2, order[n], 512 * (n % 4), "A%d" % (n % 4)
         for t, F in ((1, T.G1), (2, T.G2)):
-            V("ts", (F[:, 256 * b:256 * b + 256], T.PV[:, 1024 * b:1024 * b + 256], float(t), None, A.is_ge), ["PV%d" % b] * (t == 1), ["PV%d" % b, "G%d%d" % (t, b)])
-        cs = [(T.PSA[:, o:o + 120], T.ONE1[0:1, :], T.MC[0:1, :], True, False)]
-        for t, F in ((2, T.G3), (0, T.G1), (1, T.G2)):
-            for h in range(2):
-                cs.append((T.PSA[:, o + h:o + 120:2], F[:, 256 * b + 128 * h:256 * b + 128 * h + 128], T.M[:, 60 * t:60 * t + 60], False, t == 1 and h == 1))
-        mms(cs, ["G1%d" % b, "G2%d" % b, "G3%d" % b, "M0", "M1", "M2", "Mt", "MC0", "MC1", "MC2", "ONE1"], ["A%d" % (n % 4)])
-        out, k = (T.SEND[:, 120 * n:120 * n + 120], "SX%d" % n) if n < 7 else (T.LR[:, rank, :], "LRs")
-        cp("a", out, T.PSA[:, o:o + 120], ["A%d" % (n % 4)], ["A%d" % (n % 4), k])
+            V("ts", (F[:, c0:c0 + 256], T.PV[:, 1024 * b:1024 * b + 256], float(t), None, A.is_ge), ["PV%d" % b] * (t == 1), ["PV%d" % b, "G%d%d" % (t, n)])
+        mms([(T.PSA[:, o:o + RW], T.ONE1[0:1, :], T.MC[0:1, :], True, False)], ["MC0", "MC1", "MC2", "ONE1"], [pk])
+        mms([(T.PSA[:, o + h:o + 120:2], F[:, c0 + 128 * h:c0 + 128 * h + 128], T.M[:, 60 * t:60 * t + 60], False, t == 1 and h == 1)
+             for t, F in ((2, T.G3), (0, T.G1), (1, T.G2)) for h in range(2)], ["G1%d" % n, "G2%d" % n, "G3%d" % n, "M0", "M1", "M2", "Mt"], [pk])
+        out, k = (T.SEND[:, d, :], "SX%d" % d) if d != rank else (T.LR[:, rank, :], "LRs")
+        cp("a", out, T.PSA[:, o:o + RW], [pk], [pk, k])
+        if n in SENDS:
+            call = plan(T, topo, rank, "X")[SENDS.index(n)]
+            send(call, lambda d: T.SEND[:, d, :], T.LR[:, rank, :], "arrX", "locX", ["SX%d" % d for d, _ in call])
 
-    src = lambda d: T.SEND[:, 120 * order.index(d):120 * order.index(d) + 120]
-    calls = plan(T, topo, rank, "X")
     for n in range(9):
         if n < 8:
             turn(n)
         if n > 0:
             mix(n - 1)
-        if n in (4, 7):
-            send(calls[n // 7], src, T.LR[:, rank, :], "arrX", "locX", ["SX%d" % order.index(d) for d, _ in calls[n // 7]])
 
-    for out, n, x, k in ((T.TB[:, :, 0, :], 512, -81920.0, "TB0"), (T.TB[:, :, 1:4, 12:16], 384, -102400.0, "TB3")):
-        S("act", (out, T.D[:, 0:n], AF.Copy), ["D0", "D1"], [k], scale=0.0, bias=x)
+    def fill(out, n, x, wr, p0=0, p1=128):
+        S("act", (out, T.G3[p0:p1, 0:n], AF.Copy), ["G30", "G31", "G32"], wr, scale=0.0, bias=float(x))
+
+    fill(T.TB[:, :, 0, :], 512, -81920, ["TBU"])
+    fill(T.TB[:, :, 1:4, 12:16], 384, -102400, ["TB3"])
+    fill(T.AD[:, :, 0, :], 64, 224, ["AD0"])
     V("memset", (T.ONE2[:], 1.0), [], ["ONE2"])
     G("asel", (T.TRI[:], T.ONE1[:], [[1, 128]], A.is_ge, 0.0, -1, -1), ["ONE1"], ["TRI"])
+    send(plan(T, topo, rank, "S")[0], lambda d: T.SS[d], T.SL[rank], "arrS", "locS", ["SS"])
+    G("asel", (T.SEL[:], T.ONE2[:], [[-16, NPE], [0, 8], [-1, 16]], A.is_equal, 0.0, 0, 1), ["ONE2"], ["SEL"])
     G("asel", (T.GA[:], T.FOUR[:], [[0, 2], [-16, 8], [0, 4]], A.is_ge, 0.0, 0, 1), ["FOUR"], ["GA"])
     G("asel", (T.GB[:], T.GA[:], [[0, 2], [16, 8], [0, 4]], A.is_ge, 0.0, 14, -1), ["GA"], ["GB"])
-    G("asel", (T.SEL[:], T.ONE2[:], [[-16, NPE], [0, 8], [-1, 16]], A.is_equal, 0.0, 0, 1), ["ONE2"], ["SEL"])
     for d, n, sh in ((2, 15, 0), (3, 3, 2), (4, 7, 4), (5, 31, 2)):
         V("ts", (T.KI[:, d:d + 1], T.KI[:, 0:1], sh, n, A.arith_shift_right, A.bitwise_and), ["KI0"], ["KI"])
-    V("memset", (T.AD[:, :, 0, :], 224.0), [], ["AD0"])
     V("ts", (col(6), col(1), 3.0, -64.0, A.not_equal, A.mult), ["K1"], ["K6"])
     V("copy", (T.KF[:, 2:6], T.KI[:, 2:6]), ["KI"], ["KF"])
-    V("ts", (col(7), col(1), 2.0, 4.0, A.is_lt, A.mult), ["K1"], ["K7"])
+    V("ts", (col(7), col(1), 2.0, 256.0, A.is_lt, A.mult), ["K1"], ["K7"])
     V("ts", (col(8), col(1), 0.0, -17.0, A.is_equal, A.mult), ["K1"], ["K8"])
     V("ts", (col(9), col(3), 8.0, col(4), A.mult, A.add), ["KF"], ["K9"])
     V("ts", (T.MASK[:, 64:128], T.UC[:], col(3), None, A.is_le), ["UC", "KF"], ["MASK1"])
-    V("ts", (T.W0[:], T.RI[:], col(2), 128.0, A.is_gt, A.mult), ["RI", "KF"], ["W0"])
-    V("ts", (T.MASK[:, 0:64], T.UI[:], col(9), None, A.is_lt), ["UI", "K9"], ["MASK0"])
     V("ts", (T.L0[:], T.VA[:], col(2), -BIG, A.not_equal, A.mult), ["VA", "KF"], ["L0"])
-    V("ts", (T.EQ[:], T.CQ[:], col(5), None, A.is_equal), ["CQ", "KF"], ["EQ"])
-    V("tt", (T.W[:, 0:64], T.W0[:], T.CI[:], A.add), ["W0", "CI"], ["W"])
+    V("ts", (T.MASK[:, 0:64], T.UI[:], col(9), None, A.is_lt), ["UI", "K9"], ["MASK0"])
+    V("ts", (T.W0[:], T.RI[:], col(2), 128.0, A.is_gt, A.mult), ["RI", "KF"], ["W0"])
     V("tt", (T.LW[:], T.L0[:], T.VB[:], A.add), ["L0", "VB"], ["LW"])
-    V("ts", (T.SELY[:, 0:32], T.EQ[:], T.KB[:, 1:2], None, A.mult), ["EQ", "KB1"], ["SELY0"])
-    V("ts", (T.SELY[:, 32:64], T.EQ[:], col(7), None, A.mult), ["EQ", "K7"], ["SELY1"])
-    V("memset", (T.CON[:], 0.0), [], ["CON0"])
-    V("memset", (T.RST[:], 1.0), [], ["RST0"])
+    V("tt", (T.W[:, 0:64], T.W0[:], T.CI[:], A.add), ["W0", "CI"], ["W"])
+    V("ts", (T.EQ[:], T.CQ[:], col(5), None, A.is_equal), ["CQ", "KF"], ["EQ"])
+    G("asel", (T.RST[:], T.ONE1[:, 0:64], [[0, 16], [1, 4]], A.is_gt, 0.0, 0, 0), ["ONE1"], ["RST"])
+    for p0, x, y in ((0, 0xC20000, 0x60000), (32, 0xD600, 0x80), (64, 0xFC, 0)):
+        for o, z in ((0, x), (32, y)):
+            G("iota", (T.CON[p0:p0 + 32, o:o + 32], [[0, 32]], z, 0), ["RST", "CON"], ["CON"], **fl)
     V("memset", (T.NX[:, 48:64], -60.0), [], ["NX1"])
-    V("ts", (T.SELZ[:], T.SELY[:], -1.0, None, A.mult), ["SELY0", "SELY1"], ["SELZ"])
-    for p0, x, y in ((0, 0xC20000, 6144), (32, 0xD600, 2), (64, 0xFC, 0)):
-        V("memset", (T.CON[p0:p0 + 32, 0:64], float(x)), ["CON0"], ["CON"])
-        if y:
-            V("memset", (T.CON[p0:p0 + 32, 64:128], float(y)), [], ["CON"])
-    V("memset", (T.RST[:, 0:64:4], 0.0), ["RST0"], ["RST"])
+    S("act", (T.SELY[:, 0:32], T.EQ[:], AF.Copy), ["EQ", "K10"], ["SELY0"], scale=col(10))
+    S("act", (T.SELY[:, 32:64], T.EQ[:], AF.Copy), ["EQ", "K7"], ["SELY1"], scale=col(7))
     for h in range(2):
-        cp("a", T.SELQ[:, 32 * h:32 * h + 32], T.ID[:, :, 0, :], ["ID"], ["SELQ%d" % h])
+        S("act", (T.SELQ[:, 32 * h:32 * h + 32], T.ID[:, :, 0, :], AF.Copy), ["ID"], ["SELQ%d" % h], scale=64.0 ** h)
+    S("act", (T.SELZ[:], T.SELY[:], AF.Copy), ["SELY0", "SELY1"], ["SELZ"], scale=-1.0)
     for w in (64, 128, 256, 512):
         cp("v", T.W[:, w:2 * w], T.W[:, 0:w], ["W"], ["W"])
     cp("v", T.W[:, 1024:1088], T.W[:, 0:64], [], ["W"])
@@ -273,31 +275,43 @@ def rank_program(g, core, T, topo):
     dma("s", T.ST[:], T.SL[:], "lst", ["SL", "SLs"], ["ST"])
 
     def pairs():
-        V("ts", (T.P4[:], T.PT[:, :, 0, :], 4.0, None, A.mult), ["PT"], ["P4"])
-        V("ts", (T.NX[:, 0:48], T.PT[:, 1:4, 0, :], -60.0, None, A.add), ["PT"], ["NX0"])
-        V("tt", (T.PI[:], T.P4[:], T.PT[:, :, 1, :], A.add), ["P4", "PT"], ["PI"])
-        for c in range(2):
-            V("ts", (T.AM[:, 64 * c:64 * c + 64], T.PT[:, :, 1, :], float(c), -BIG, A.not_equal, A.mult), ["PT"], ["AM%d" % c])
-        V("copy", (T.OFP[:], T.PI[:]), ["PI"], ["OFP"])
-        for c in range(2, 4):
-            V("ts", (T.AM[:, 64 * c:64 * c + 64], T.PT[:, :, 1, :], float(c), -BIG, A.not_equal, A.mult), ["PT"], ["AM%d" % c])
+        return [lambda: V("ts", (T.P4[:], T.PT[:, :, 0, :], 4.0, None, A.mult), ["PT"], ["P4"]),
+                lambda: V("tt", (T.PI[:], T.P4[:], T.PT[:, :, 1, :], A.add), ["P4", "PT"], ["PI"]),
+                lambda: V("copy", (T.OFP[:], T.PI[:]), ["PI"], ["OFP"])]
 
     def spread(u):
         S("act", (T.LTR[:, 512 * u:512 * u + 512], T.LW[:, 0:16].indirect(T.OFP[:, 32 * u:32 * u + 32]), AF.Copy), ["LW", "OFP"], ["LTR%d" % u])
 
-    def starts():
-        V("ts", (T.ST4[:], T.ST[:], 4.0, None, A.mult), ["ST"], ["ST4"])
+    def odd():
+        V("ts", (T.NX[:, 0:48], T.PT[:, 1:4, 0, :], -60.0, None, A.add), ["PT"], ["NX0"])
+        for c in range(4):
+            V("ts", (T.AM[:, 64 * c:64 * c + 64], T.PT[:, :, 1, :], float(c), -BIG, A.not_equal, A.mult), ["PT"], ["AM%d" % c])
         for c in range(4):
             V("tt", (T.QTB[:, :, 0, :, c], T.AM[:, 64 * c:64 * c + 64], T.NX[:], A.add), ["AM%d" % c, "NX0", "NX1"], ["QTB0"])
-        for h in range(2):
-            V("tt", (T.I[:, 16 * h:16 * h + 16], T.ST4[:, 16 * h:16 * h + 16], T.PT[:, 0, 0, :], A.add), ["ST4", "PT"], ["I"])
-        V("copy", (T.QTB[:, :, 1], T.QTB[:, :, 0]), ["QTB0"], ["QTB1"])
-        V("ts", (T.J[:], T.I[:], 63, None, A.bitwise_and), ["I"], ["J"])
-        for h in range(2):
-            V("ts", (T["OA%d" % h][:], T.I[:, 16 * h:16 * h + 16], 1.0 / 64, -0.5 + 0.5 / 64, A.mult, A.add), ["I"], ["OA:%d" % h])
-        for h in range(2):
-            V("copy", (T["OB%d" % h][:], T.J[:, 16 * h:16 * h + 16]), ["J"], ["OB:%d" % h])
 
+    def starts():
+        OK = ["O:%d" % u for u in range(4)]
+        return [[lambda: V("ts", (T.QTB[:, :, 1], T.QTB[:, :, 0], 64.0, None, A.mult), ["QTB0"], ["QTB1"]),
+                 lambda: V("ts", (T.X[:, 16384:16385], T.BX[:, 5:6], col(8), -81536.0, A.add, A.add), ["BX2", "K8"], ["XE"])],
+                [lambda: V("ts", (T.ST4[:], T.ST[:], 4.0, None, A.mult), ["ST"], ["ST4"]),
+                 lambda: V("ts", (T.O[:, :, 0:8], T.ST[:], 1.0 / 16, -0.5 + 0.5 / 16, A.mult, A.add), ["ST"], OK)],
+                [lambda h=h: V("tt", (T.I[:, 16 * h:16 * h + 16], T.ST4[:, 16 * h:16 * h + 16], T.PT[:, 0, 0, :], A.add), ["ST4", "PT"], ["I"]) for h in range(2)],
+                [lambda: V("ts", (T.J[:], T.I[:], 63, None, A.bitwise_and), ["I"], ["J"])],
+                [lambda: V("copy", (T.O[:, :, 8:16], T.J[:]), ["J"], OK)]]
+
+    PO = lambda b, m: T.PSA[:, 512 * b + m:512 * b + 512:4]
+    slot = lambda b, m: 2 * (b + 4 * (m % 2)) + m // 2
+    turns = TURNS.split()
+
+    def turned(n):
+        x, j = turns[n], int(turns[n][1])
+        first, final = (all(int(y[1]) % 2 != j % 2 for y in part) for part in (turns[:n], turns[n + 1:]))
+        for b in (2 * (j % 2), 2 * (j % 2) + 1):
+            ms = range(4) if x[0] == "D" else (j // 2, j // 2 + 2)
+            mms([(PO(b, m), T.AD[:, :, :, m // 2] if x[0] == "D" else T["T" + x[0]][:, :, :, slot(b, m)], T.ID[:], first and m == ms[0], final and m == ms[-1]) for m in ms],
+                {"A": ["TAU", "T" + x], "B": ["TBU", "T" + x], "D": ["AD0", "AD"]}[x[0]] + ["ID"], ["A%d" % b])
+
+    turned(0)
     LK = ["LR", "LRs"]
     tot = lambda h: T.LR[:, :, 112 + h:120:2]
     before = lambda h: T.PS0[:, 0, 0, h:64:2]
@@ -320,15 +334,20 @@ def rank_program(g, core, T, topo):
         else:
             S("act", args + (AF.Copy,), LK, wr, scale=sc, bias=sc * add)
 
-    pl = PLANES.split()
+    pl, pr = PLANES.split(), pairs()
     for x in pl:
         if x[0] == "a":
             plane(x)
     pl = [x for x in pl if x[0] == "v"]
     plane(pl[0])
+    pr[0]()
+    plane(pl[1])
+    pr[1]()
+    plane(pl[2])
     V("copy", (T.NI[:], T.PS0[:, 0, 0]), ["P0"], ["P0", "NI"])
     V("tt", (T.MS[:], T.PS1[:, 0], T.MASK[:], A.mult), ["P1", "MASK0", "MASK1"], ["P1", "MS"])
-    plane(pl[1])
+    pr[2]()
+    spread(0)
     for i, (sh, n) in enumerate(((0, 63), (6, 63), (12, 63))):
         V("ts", (T.DI[:, :, i, :], T.NI[:], sh, n, A.arith_shift_right, A.bitwise_and), ["NI"], ["DI"])
     for h in range(2):
@@ -336,102 +355,87 @@ def rank_program(g, core, T, topo):
     V("copy", (T.AD[:, :, 1:4, :], T.DI[:]), ["DI"], ["AD"])
     V("ts", (T.BI[:, 2:4], T.BX[:, 0:2], T.KB[:, 0:1], 1.0 / 64, A.mult, A.mult), ["BX0", "KB0"], ["BI1"])
     V("ts", (T.BI[:, 0:2], T.BX[:, 0:2], T.KB[:, 0:1], None, A.mult), ["BX0", "KB0"], ["BI0"])
-    plane(pl[2])
-    V("ts", (T.BX[:, 2:4], T.BI[:, 2:4], col(6), 81696.0, A.mult, A.add), ["BI1", "K6"], ["BX1"])
     plane(pl[3])
+    V("ts", (T.BX[:, 2:4], T.BI[:, 2:4], col(6), 81696.0, A.mult, A.add), ["BI1", "K6"], ["BX1"])
+    plane(pl[4])
     V("tt", (T.BX[:, 4:6], T.BI[:, 0:2], T.BX[:, 2:4], A.add), ["BI0", "BX1"], ["BX2"])
-    for x in pl[4:]:
-        plane(x)
-    PO = lambda b, m: T.PSA[:, 512 * b + m:512 * b + 512:4]
-    slot = lambda b, m: 2 * (b + 4 * (m % 2)) + m // 2
-    for e in range(2):
-        for x, j in (("A", e), ("B", e), ("A", e + 2), ("B", e + 2)):
-            for b in (2 * e, 2 * e + 1):
-                mms([(PO(b, m), T["T" + x][:, :, :, slot(b, m)], T.ID[:], (x, j, m) == ("A", e, 0), False) for m in (j // 2, j // 2 + 2)],
-                    ["TAU" if x == "A" else "TB0", "T%s%d" % (x, j), "ID"], ["A%d" % b])
-        for b in (2 * e, 2 * e + 1):
-            mms([(PO(b, m), T.AD[:, :, :, m // 2], T.ID[:], False, m == 3) for m in range(4)], ["AD", "AD0", "ID"], ["A%d" % b])
-    pairs()
+    for n in range(1, len(turns)):
+        turned(n)
+    odd()
+    small = starts()
     for b in range(4):
         args, rd, wr = (T.XC[:, b:2048:4], T.PSA[:, 512 * b:512 * b + 512]), ["A%d" % b, "BX2"], ["A%d" % b, "XC%d" % b]
         if XCQ[b] == "v":
             V("ts", args + (T.BX[:, 4:5], None, A.add), rd, wr)
         else:
             S("act", args + (AF.Identity,), rd, wr, bias=T.BX[:, 4:5])
-        if b == 0:
-            spread(0)
         if b == 1:
-            V("ts", (T.X[:, 16384:16385], T.BX[:, 5:6], col(8), -81536.0, A.add, A.add), ["BX2", "K8"], ["XE"])
-            starts()
+            spread(1)
+        if XCQ[b] == "v":
+            for f in small.pop(0):
+                f()
 
     XK, XCK = ["XE"], ["XC%d" % b for b in range(4)]
-    for k in range(NPE, 8):
-        for y in range(8):
-            dma("s", T.X[16 * y:16 * y + 16, 2048 * k:2048 * k + 2048], T.XC[16 * k:16 * k + 16, :], "rep", XCK, ["XD%d%d" % (k, y)])
+    share = [min(max(CPE - 2048 * k, 0), 2048) for k in range(8)]
+    for k in range(7, -1, -1):
+        for y in range(8 if share[k] < 2048 else 0):
+            dma("s", T.X[16 * y:16 * y + 16, 2048 * k + share[k]:2048 * k + 2048], T.XC[16 * k:16 * k + 16, share[k]:2048], "rep", XCK, ["XD%d%d" % (k, y)])
             XK.append("XD%d%d" % (k, y))
-    ring = [(T.PS0[:], "P0"), (T.PS1[:], "P1")] + [(T.PSA[:, 512 * b:512 * b + 512], "A%d" % b) for b in range(2)]
-    n = 0
-    for b in range(4):
-        for k in range(NPE):
-            ps, pk = ring[n % 4]
-            mms([(ps, T.SEL[:, 128 * k:128 * k + 128], T.XC[:, b:2048:4], True, True)], ["XC%d" % b, "SEL"], [pk])
-            cp("av"[n % 2], T.X[:, 2048 * k + b:2048 * k + 2048:4], ps, [pk], [pk, "X%d" % n])
-            XK.append("X%d" % n)
-            n += 1
-    spread(1)
+    ring = [(lambda w, b=b: PS[b][:, 0:w // 128], "P%d" % b) for b in range(2)] + [(lambda w, b=b: T.PSA[:, 512 * b:512 * b + w], "A%d" % b) for b in range(4)]
+    for n, (b, k) in enumerate((b, k) for b in range(4) for k in range(NPE)):
+        ps, pk = ring[n % 6]
+        ps = ps(share[k] // 4)
+        mms([(ps, T.SEL[:, 128 * k:128 * k + 128], T.XC[:, b:share[k]:4], True, True)], ["XC%d" % b, "SEL"], [pk])
+        cp(XQ[n % len(XQ)], T.X[:, 2048 * k + b:2048 * k + share[k]:4], ps, [pk], [pk, "X%d" % n])
+        XK.append("X%d" % n)
+        if XQ[n % len(XQ)] == "v" and small:
+            for f in small.pop(0):
+                f()
 
-    B = lambda name, n: T["L%dS" % (n % 2) if name == "L" else "%s%d" % (name, n % 2)]
-    key = lambda name, n: "%s:%d" % (name, n % 2)
-    out = lambda n, k: PS[n % 2][:, 0, :, 32 * k:32 * k + 32]
+    key = lambda name, n: "%s:%d" % (name, n % 4)
+    tile = lambda name, n: T[name][:, 128 * (n % 4):128 * (n % 4) + 128]
+    bank = lambda n: T.PSA[:, 512 * (n % 4):512 * (n % 4) + 64]
+    st = lambda n, a, b, s: T.SC[:, 64 * (n % 4) + a:64 * (n % 4) + b:s]
 
-    def state(n):
-        pk = "P%d" % (n % 2)
-        V("scan", (B("S", n)[:], T.RST[:], PS[n % 2][:, 0, 0], 0.0, A.mult, A.max), [pk, "RST"], [pk, key("S", n)])
-
-    def low(n):
-        pk = "P%d" % (n % 2)
-        V("scan", (B("L", n)[:], T.RST[:], PS[n % 2][:, 0, 1], 0.0, A.mult, A.max), [pk, "RST"], [pk, key("L", n)])
-
-    half = lambda name, n, k: B(name, n)[:, 128 * k:128 * k + 128]
-    hkey = lambda name, n, k: key(name, n) + str(k)
+    def pick(n):
+        if 4 <= n < 36:
+            V("scan", (st(n, 0, 64, 1), T.RST[:], bank(n), 0.0, A.mult, A.max), ["A%d" % (n % 4), "RST"], ["A%d" % (n % 4), key("S", n)])
 
     def block(n):
-        if n >= 2:
-            V("ts", (B("OA", n)[:], B("S", n)[:, 3:64:4], 1.0 / 64, -0.5 + 0.5 / 64, A.mult, A.add), [key("S", n)], [key("OA", n)])
-        for k in range(2):
-            S("act", (half("Z", n, k), T.X[:, 0:16385].indirect(B("OA", n)[:, 8 * k:8 * k + 8]), AF.Copy), [key("OA", n)] + XK, [hkey("Z", n, k)])
-        for k in range(2):
-            S("act", (half("ZL", n, k), half("Z", n, k), AF.Copy), [hkey("Z", n, k)], [hkey("ZL", n, k)], bias=24512.5)
+        if 32 <= n < 36:
+            V("ts", (T.RES[:, 8 * (n % 4):8 * (n % 4) + 8], st(n, 3, 32, 4), 0.25, None, A.mult), [key("S", n)], ["RES%d" % (n % 4)])
+        if 4 <= n < 32:
+            V("ts", (T.O[:, n % 4, :], st(n, 3, 64, 4), 1.0 / 64, -0.5 + 0.5 / 64, A.mult, A.add), [key("S", n)], [key("O", n)])
+        if n < 32:
+            S("act", (tile("Z", n), T.X[:, 0:16385].indirect(T.O[:, n % 4, 0:8]), AF.Copy), [key("O", n)] + XK, [key("Z", n)])
+            mms([(bank(n), T.ONE1[0:96, :], T.CON[0:96, :], True, False)], ["ONE1", "CON"], ["A%d" % (n % 4)])
 
-    def count(n, k):
-        t, pk = n // 2, "P%d" % (n % 2)
-        if k == 0:
-            mms([(PS[n % 2][:, 0], T.ONE1[:], T.CON[:], True, False)], ["ONE1", "CON"], [pk])
-        nxt = (T.ID[:], T.QTB[:, t // 2, :, 8 * k:8 * k + 8, :]) if t % 2 else (T.LTR[:, 128 * (t + k):128 * (t + k) + 128], T.SELQ[:])
-        mms([(out(n, k),) + x + (False, False) for x in ((half("ZL", n, k), T.SELZ[:]), nxt, (half("Z", n, k), T.SELY[:]))],
-            [hkey("Z", n, k), hkey("ZL", n, k), "ID", "SELY0", "SELY1", "SELZ", "SELQ0", "SELQ1", "LTR%d" % (t // 4), "QTB0", "QTB1"], [pk])
-        V("tt", (half("E", n, k), T.W[:, 0:1088].indirect(B("OB", n)[:, 8 * k:8 * k + 8]), half("Z", n, k), A.is_gt),
-          [key("OB", n), "W", hkey("Z", n, k)], [hkey("E", n, k)])
-        mms([(out(n, k), half("E", n, k), T.GB[:], False, k == 1)], [hkey("E", n, k), "GB"], [pk])
+    def letters(n):
+        if 0 <= n < 32:
+            V("ts", (tile("ZL", n), tile("Z", n), 24512.5, None, A.add), [key("Z", n)], [key("ZL", n)])
 
-    for n in range(18):
-        if n >= 2:
-            state(n)
-        if 0 < n < 17:
-            count(n - 1, 0)
-        if n < 16:
-            block(n)
-        else:
-            V("ts", (T.RES[:, 16 * (n % 2):16 * (n % 2) + 16], B("S", n)[:, 3:64:4], 0.25, None, A.mult), [key("S", n)], ["RES%d" % (n % 2)])
-        if 0 < n < 17:
-            count(n - 1, 1)
-        if 2 <= n < 16:
-            low(n)
-            V("copy", (B("OB", n)[:], B("L", n)[:, 3:64:4]), [key("L", n)], [key("OB", n)])
-    dma("s", T.RD[:], T.RES[:], "rd", ["RES0", "RES1"], ["RD"])
+    def compare(n):
+        if 0 <= n < 32:
+            V("tt", (tile("E", n), T.W[:, 0:1088].indirect(T.O[:, n % 4, 8:16]), tile("Z", n), A.is_gt), [key("O", n), "W", key("Z", n)], [key("E", n)])
+
+    def sums(n):
+        if 0 <= n < 32:
+            t, k, pk = n // 4, n % 2, "A%d" % (n % 4)
+            nxt = (T.ID[:], T.QTB[:, t // 2, :, 8 * k:8 * k + 8, :]) if t % 2 else (T.LTR[:, 128 * (t + k):128 * (t + k) + 128], T.SELQ[:])
+            mms([(bank(n),) + x + (False, False) for x in ((tile("ZL", n), T.SELZ[:]), nxt, (tile("Z", n), T.SELY[:]))],
+                [key("Z", n), key("ZL", n), "ID", "SELY0", "SELY1", "SELZ", "SELQ0", "SELQ1", "LTR%d" % (t // 4), "QTB0", "QTB1"], [pk])
+            mms([(bank(n), tile("E", n), T.GB[:], False, True)], [key("E", n), "GB"], [pk])
+
+    for n in range(36):
+        pick(n)
+        compare(n - 2)
+        block(n)
+        letters(n - 2)
+        sums(n - 2)
+    dma("s", T.RD[:], T.RES[:], "rd", ["RES0", "RES1", "RES2", "RES3"], ["RD"])
     send(plan(T, topo, rank, "F")[0], lambda d: T.RD[d], T.FL[rank], "arrF", "locF", ["RD"])
     r0, r1 = 16 * rank, 16 * rank + 16
-    dma("s", T.y[r0:r1, :], T.RES[r0:r1, :], "yself", ["RES0", "RES1"], ["y0"])
+    dma("s", T.y[r0:r1, :], T.RES[r0:r1, :], "yself", ["RES0", "RES1", "RES2", "RES3"], ["y0"])
     if rank > 0:
         dma("s", T.y[0:r0, :], T.FL[0:rank], "yout", ["FL"], ["y1"])
     if rank < 7:

@@ -1,51 +1,66 @@
 import math
 from concourse.bass import DstId, RemoteDMATransfer
-from concourse.mybir import AluOpType as A, AxisListType, ActivationFunctionType as AF
+from concourse.mybir import AluOpType as A, ActivationFunctionType as AF
 
 NON = 4
-CPE = 9216
-NPE = -(-CPE // 2048)
-XQ = "av"
+XH = 0
+XQ = "aavavavavavavava"
+NDMA = (13, 4)
+PLAST = 0
+SMALL = {"early": "p0 p1 p2", "last": "x0 x1 s0 k0 k1 s1 s2 s3 k2 k3", 13: "s4 q0 s5 q1", "l3": "q2 q3 q4 q5 q6 q7 q8 q9"}
+MS = 4
+NPRE = 20
+NSP = 2
+MFIN = 0
+NB = 4
+C7 = 0
+PIECE = "r2 c4 u3 f2 m1 k0 t3 n1 x0"
+SWAP = False
 RW = 120
 LQ = "asssssss"
-SENDS = (1, 3, 5, 6)
 BIG = 2097152.0
 TOFF = (0.0, -1.5, -7.5, -31.5)
-PLANES = "aA0 vB0 vU0 aA2 vB2 aA1 vB1 vA3"
-TURNS = "B3 B0 A0 A2 B2 A1 D0 B1 A3 D1"
-XCQ = "avav"
+TURNS = "B3 B0 A0 A2 B2 A1 B1 A3 D0 D1"
+EARLY = "aA0 aA2 aA1 aA3 vB0 vU0 vU2 vB2 d0 vU1 vB1 d1 d2 d3 b0 vU3 d4 b1 b2 b3 b4 b5"
+LATE = "vX1 aX0 aA0 aA2 aA1 aA3 vB0 vU0 vU2 vB2 d0 b0 vU1 vB1 d1 d2 d3 b1 vU3 d4 b2 b3 b4 b5"
+STEP = "z1 o3 a1 v1 e1 c0 z2 b1 a3 s4 a4 z3 e2 o4 l2 l3 e3 c1 b2 c2 s5 z4 s6 o5 b3 c3 x4 v4 o6 s7 a6 e4 b4"
 
 SCRATCH = {
     "PP": ("dram", [8, 128, 16], "int32"), "SS": ("dram", [8, 128, 4], "int32"),
     "PL": ("dram", [8, 128, 16], "int32"), "SL": ("dram", [8, 128, 4], "int32"),
     "RD": ("dram", [8, 128, 4], "float32"), "FL": ("dram", [8, 128, 4], "float32"),
-    "PV": ("psum", [128, 2048], "bfloat16"), "PSA": ("psum", [128, 2048], "float32"),
-    "PS0": ("psum", [128, 4, 2, 64], "float32"), "PS1": ("psum", [128, 4, 2, 64], "float32"),
+    "PV": ("psum", [128, 8, 2, 2, 64], "bfloat16"), "PSA": ("psum", [128, 2048], "float32"),
+    "PS0": ("psum", [128, 512], "float32"), "PS1": ("psum", [128, 512], "float32"),
 }
 for _n, _w, _d in (
         ("D32", 2048, "int32"), ("D", 2048, "bfloat16"), ("G1", 2048, "bfloat16"), ("G2", 2048, "bfloat16"), ("G3", 2048, "bfloat16"),
-        ("SEND", [8, RW], "bfloat16"), ("LR", [8, RW], "bfloat16"), ("M", 180, "bfloat16"), ("MC", RW, "bfloat16"),
+        ("SEND", [8, RW // 4, 2, 2], "bfloat16"), ("LR", [8, RW // 4, 2, 2], "bfloat16"), ("M", 180, "bfloat16"), ("MC", 66, "bfloat16"),
         ("DPI", 16, "bfloat16"), ("DP", 16, "bfloat16"),
-        ("TA", [32, 4, 16], "bfloat16"), ("TB", [32, 4, 16], "bfloat16"), ("AD", [32, 4, 2], "bfloat16"),
-        ("NI", 64, "int32"), ("DI", [32, 3, 2], "int32"), ("UI", 64, "float32"), ("MASK", 128, "float32"), ("MS", 128, "float32"),
-        ("BX", 8, "float32"), ("BI", 4, "int32"), ("XC", 2048, "bfloat16"), ("X", 16400, "bfloat16"),
-        ("ONE1", 128, "bfloat16"), ("ONE2", 128 * NPE, "bfloat16"), ("FOUR", 64, "bfloat16"), ("GA", 64, "bfloat16"), ("GB", 64, "bfloat16"),
-        ("ID", [8, 4, 4], "bfloat16"), ("CON", 64, "bfloat16"), ("TRI", 128, "bfloat16"), ("SEL", 128 * NPE, "bfloat16"),
+        ("TA", [4, 32, 4, 4], "bfloat16"), ("TB", [4, 32, 4, 4], "bfloat16"), ("AD", [32, 4, 2], "bfloat16"),
+        ("NI", 64, "int32"), ("DI", [32, 3, 2], "int32"), ("UI", 64, "float32"), ("MASK", 80, "float32"), ("MS", 80, "float32"), ("MT", 80, "float32"),
+        ("RS", 80, "bfloat16"), ("BX", 12, "float32"), ("BI", 12, "int32"), ("UC", 32, "float32"), ("MID", 64, "bfloat16"), ("XC", 2048, "bfloat16"), ("XE", 8, "bfloat16"), ("X", 16400, "bfloat16"),
+        ("ONE1", 128, "bfloat16"), ("ONE2", 256, "bfloat16"), ("FOUR", 64, "bfloat16"), ("GA", 64, "bfloat16"), ("GB", 64, "bfloat16"),
+        ("ID", [8, 4, 4], "bfloat16"), ("CON", 64, "bfloat16"), ("TRI", 128, "bfloat16"), ("PERM", 128, "bfloat16"), ("SEL", [2, 4, 128], "bfloat16"),
         ("SELY", 64, "bfloat16"), ("SELZ", 64, "bfloat16"), ("SELQ", 64, "bfloat16"), ("EQ", 32, "bfloat16"), ("CQ", 32, "float32"),
-        ("KI", 8, "int32"), ("KF", 16, "float32"), ("KB", 8, "bfloat16"), ("UC", 64, "float32"), ("RI", 64, "float32"), ("CI", 64, "float32"), ("W0", 64, "float32"),
+        ("KI", 8, "int32"), ("KF", 16, "float32"), ("KB", 8, "bfloat16"), ("RI", 64, "float32"), ("CI", 64, "bfloat16"), ("W0", 64, "bfloat16"),
         ("VA", 16, "float32"), ("VB", 16, "float32"), ("L0", 16, "float32"),
-        ("W", 1088, "bfloat16"), ("LW", 16, "bfloat16"), ("PT", [4, 2, 16], "int32"), ("ST", 32, "int32"), ("ST4", 32, "int32"),
-        ("P4", 64, "int32"), ("PI", 64, "int32"), ("OFP", 64, "uint16"), ("LTR", 1024, "bfloat16"), ("AM", 256, "float32"), ("NX", 64, "float32"),
+        ("W", 1344, "bfloat16"), ("LW", 16, "bfloat16"), ("PT", [4, 2, 16], "int32"), ("ST", 32, "int32"), ("ST4", 32, "int32"),
+        ("P4", 64, "int32"), ("PI", 64, "int32"), ("OFP", 64, "uint16"), ("LTR", 1024, "bfloat16"), ("NID", 128, "bfloat16"), ("NX", 64, "float32"),
         ("QTB", [4, 2, 16, 4], "bfloat16"), ("RST", 64, "float32"), ("RES", 32, "float32"), ("I", 32, "int32"), ("J", 32, "int32"),
         ("O", [4, 16], "uint16"), ("SC", 256, "float32"), ("Z", 512, "bfloat16"), ("ZL", 512, "bfloat16"), ("E", 512, "bfloat16")):
     SCRATCH[_n] = ("sbuf", [128] + (_w if isinstance(_w, list) else [_w]), _d)
 SEMAPHORES = (["vq", "aq", "pq", "gq", "dp", "ds", "dsp", "dss", "lpt", "lst", "rep", "yself", "yout", "rd",
-               "arrP", "arrS", "arrX", "arrF", "locP", "locS", "locX", "locF"] + ["b%d" % _i for _i in range(8)])
+               "arrP", "arrS", "arrE", "arrL", "arrF", "locP", "locS", "locX", "locF"] + ["b%d" % _i for _i in range(8)])
 
 
 def far_first(T, topo, rank):
     chip = lambda d: topo.chip(T.cores[d])
     return sorted((d for d in range(8) if d != rank), key=lambda d: (chip(d) == chip(rank), topo.same_plane(chip(rank), chip(d)), (d - rank) % 8))
+
+
+def halves(T, topo, rank):
+    far = far_first(T, topo, rank)
+    return sorted(far, key=lambda d: (d // 4 == rank // 4) == SWAP)
 
 
 def plan(T, topo, rank, kind):
@@ -55,11 +70,8 @@ def plan(T, topo, rank, kind):
     eo = topo.engines(core, T.cores[off[0]])
     en = [e for e in topo.engines(core, T.cores[on]) if e not in eo][:NON]
     if kind == "X":
-        calls = []
-        for a, b in zip((0,) + tuple(n + 1 for n in SENDS), SENDS):
-            w = len(eo) // max(len(off[a:b + 1]), 1)
-            calls.append([(d, eo[w * i:w * i + w]) for i, d in enumerate(off[a:b + 1])] + [(on, en)] * (b == 6))
-        return calls
+        h, w = halves(T, topo, rank), len(eo) // 2
+        return [[(d, en if d == on else eo[w * i:w * i + w]) for i, d in enumerate(h[a:b])] for a, b in (((0, 2), (2, 4), (4, 6), (6, 7)) if SWAP else ((0, 2), (2, 3), (3, 5), (5, 7)))]
     if kind == "P":
         return [[(off[0], eo[0:2]), (off[1], eo[2:4])] + [(d, [eo[4 + i]]) for i, d in enumerate(off[2:])] + [(on, en[:1])]]
     return [[(d, [eo[i]]) for i, d in enumerate(off)] + [(on, en[:1])]]
@@ -107,7 +119,7 @@ def rank_program(g, core, T, topo):
         deps(q, rd, wr)
         o = Q[q]
         fn = {"copy": lambda: o.tensor_copy(*args), "tt": lambda: o.tensor_tensor(*args), "ts": lambda: o.tensor_scalar(*args),
-              "memset": lambda: o.memset(*args), "red": lambda: o.tensor_reduce(*args), "scan": lambda: o.tensor_tensor_scan(*args),
+              "memset": lambda: o.memset(*args), "scan": lambda: o.tensor_tensor_scan(*args),
               "act": lambda: o.activation(*args, **kw), "iota": lambda: o.iota(*args, **kw), "asel": lambda: o.affine_select(*args)}[name]
         s = QS[q]
         fn().then_inc(T.sem[s], 1)
@@ -138,12 +150,12 @@ def rank_program(g, core, T, topo):
                                         remote_sem=T.sem[arr], srcs=[src(d)], dsts=[dst]))
             total[loc] = total.get(loc, 0) + len(es)
         g.remote_dma_fused(tr, local_sem=T.sem[loc])
-        total[arr] = arrive[arr]
 
-    arrive = {}
-    for kind, k, arr in (("P", "PL", "arrP"), ("S", "SL", "arrS"), ("X", "LR", "arrX"), ("F", "FL", "arrF")):
-        arrive[arr] = sum(len(es) for r in range(8) if r != rank for call in plan(T, topo, r, kind) for d, es in call if d == rank)
-        last[k] = (arr, arrive[arr], {})
+    e0, e1 = (1 - rank // 4, rank // 4) if SWAP else (rank // 4, 1 - rank // 4)
+    for kind, k, arr, src in (("P", "PL", "arrP", range(8)), ("S", "SL", "arrS", range(8)), ("F", "FL", "arrF", range(8)),
+                              ("X", "LR%d" % e0, "arrE", range(4 * e0, 4 * e0 + 4)), ("X", "LR%d" % e1, "arrL", range(4 * e1, 4 * e1 + 4))):
+        total[arr] = sum(len(es) for r in src if r != rank for call in plan(T, topo, r, kind) for d, es in call if d == rank)
+        last[k] = (arr, total[arr], {})
     V = lambda name, args, rd, wr: op("v", name, args, rd, wr)
     S = lambda name, args, rd, wr, **kw: op("a", name, args, rd, wr, **kw)
     G = lambda name, args, rd, wr, **kw: op("g", name, args, rd, wr, **kw)
@@ -156,11 +168,15 @@ def rank_program(g, core, T, topo):
         else:
             S("act", (out, in_, AF.Copy), rd, wr)
 
-    order = far_first(T, topo, rank) + [rank]
-    dma("s", T.PP[:], T.pats[:], "dp", [], ["PP"])
+    def fill(out, n, x, wr):
+        S("act", (out, T.ONE1[:, 0:n], AF.Copy), ["ONE1"], wr, scale=float(x))
+
+    order = halves(T, topo, rank) + [rank]
+    stage = [lambda: dma("s", T.PP[:], T.pats[:], "dp", [], ["PP"]), lambda: dma("s", T.SS[:], T.starts[:], "ds", [], ["SS"])]
+    stage[0]()
+    stage[1]()
     for n, s in enumerate(order):
         dma(LQ[n], T.D32[:, 256 * n:256 * n + 256], T.bwt[s:s + 1, :], "b%d" % n, [], ["D32%d" % n])
-    dma("s", T.SS[:], T.starts[:], "ds", [], ["SS"])
     dma("s", T.PL[rank], T.pats[16 * rank:16 * rank + 16, :], "dsp", [], ["PLs"])
     dma("s", T.SL[rank], T.starts[16 * rank:16 * rank + 16, :], "dss", [], ["SLs"])
 
@@ -172,107 +188,165 @@ def rank_program(g, core, T, topo):
     G("asel", (T.ID[:], T.ONE1[:], [[-1, 128]], A.is_equal, 0.0, 0, 1), ["ONE1"], ["ID"])
     G("asel", (T.DP[:], T.DPI[:], [[15, 2], [16, 8]], A.is_ge, 0.0, -1, -1), ["DPI0", "DPI1"], ["DP"])
     G("iota", (T.MC[:, 0:16], [[16, 8], [0, 2]], -241, 0), [], ["MC0"], **fl)
+    V("memset", (T.M[:, 0:60], 0.0), [], ["M"])
     V("memset", (T.MC[:, 16:64], -256.0), [], ["MC1"])
-    V("memset", (T.MC[:, 64:RW], 0.0), [], ["MC2"])
-    V("ts", (T.KI[:, 1:2], T.KI[:, 0:1], 3, None, A.bitwise_and), ["KI0"], ["KI1"])
-    V("memset", (T.M[:], 0.0), [], ["M"])
-    V("memset", (T.FOUR[:, 0:32], 4.0), [], ["FOUR"])
-    V("memset", (T.FOUR[:, 32:64], 256.0), [], ["FOUR"])
-    V("copy", (col(1), T.KI[:, 1:2]), ["KI1"], ["K1"])
-    S("act", (col(0), col(1), AF.Relu), ["K1"], ["K0"], bias=-1.0)
-    S("act", (T.KB[:, 0:1], col(1), AF.Exp), ["K1"], ["KB0"], scale=-math.log(64.0), bias=math.log(64.0))
-    S("act", (col(10), col(0), AF.Exp), ["K0"], ["K10"], scale=math.log(64.0), bias=math.log(4.0))
-    V("memset", (T.MC[:, 112:114], 128.0), ["MC2"], ["MC2"])
-    V("memset", (T.M[:, 56:180:61], -1.0), ["M"], ["Mt"])
-    V("memset", (T.M[:, 57:180:61], 1.0), [], ["Mt"])
+    V("memset", (T.MC[:, 64:66], 128.0), [], ["MC1"])
+    for i in range(1, 4):
+        fill(T.TB[:, 3, :, i, :], 128, -102400, ["TB3"])
+    for d, n, sh in ((1, 3, 0), (2, 15, 0), (3, 31, 2), (4, 3, 1), (5, 3, 3), (6, 3, 5)):
+        V("ts", (T.KI[:, d:d + 1], T.KI[:, 0:1], sh, n, A.arith_shift_right, A.bitwise_and), ["KI0"], ["KI"])
+    V("copy", (T.KF[:, 1:7], T.KI[:, 1:7]), ["KI"], ["KF"])
     for c in range(4):
-        V("ts", (T.M[:, 8 * c:8 * c + 8], T.ID[:, :, c, 0], 128.0, None, A.mult), ["ID"], ["M0"])
+        V("ts", (T.M[:, 8 * c:8 * c + 8], T.ID[:, :, c, 0], 128.0, None, A.mult), ["ID", "M"], ["M0"])
     for j in range(4):
         for h in range(2):
-            V("ts", (T.M[32 * j:32 * j + 32, 32 + h:56:2], T.ID[32 * j:32 * j + 32, 2 * j + h, :, 1:4], float(4 ** j), None, A.mult), ["ID"], ["M0"])
+            args = (T.M[32 * j:32 * j + 32, 36 + h:60:2], T.ID[32 * j:32 * j + 32, 2 * j + h, :, 1:4])
+            if 2 * j + h < MS:
+                S("act", args + (AF.Copy,), ["ID", "M"], ["MS"], scale=float(4 ** j))
+            else:
+                V("ts", args + (float(4 ** j), None, A.mult), ["ID"], ["M0"])
+    S("act", (T.KB[:, 0:1], col(4), AF.Exp), ["KF"], ["KB0"], scale=-math.log(64.0), bias=math.log(64.0))
     for t in (1, 2):
-        V("copy", (T.M[:, 60 * t:60 * t + 56], T.M[:, 0:56]), ["M0"], ["M%d" % t])
-    for t in (2, 1, 0):
-        o = 68 * t
-        V("tt", (T.M[:, o:o + 16], T.M[:, o:o + 16], T.DP[:], A.add), ["M%d" % t, "DP"], ["M%d" % t])
-    G("iota", (T.UI[:], [[1, 8], [8, 4], [0, 2]], 0, 0), [], ["UI"], **fl)
-    G("iota", (T.UC[:], [[0, 8], [1, 4], [0, 2]], 0, 0), [], ["UC"], **fl)
+        V("copy", (T.M[:, 60 * t:60 * t + 60], T.M[:, 0:60]), ["M0", "MS"], ["M%d" % t])
+
+    def matrices():
+        V("memset", (T.M[:, 32:180:61], -1.0), ["M1", "M2"], ["Mt"])
+        V("memset", (T.M[:, 33:180:61], 1.0), [], ["Mt"])
+        for t in (2, 1, 0):
+            o = 68 * t
+            V("tt", (T.M[:, o:o + 16], T.M[:, o:o + 16], T.DP[:], A.add), ["M%d" % t, "DP"], ["M%d" % t])
+
+    if MFIN < 0:
+        matrices()
     G("iota", (T.RI[:], [[1, 16], [0, 4]], 0, 0), [], ["RI"], **fl)
     G("iota", (T.CI[:], [[0, 16], [128, 4]], -256, 0), [], ["CI"], **fl)
     G("iota", (T.CQ[:], [[4, 8], [1, 4]], 0, 0), [], ["CQ"], **fl)
+    queries = [lambda: send(plan(T, topo, rank, "P")[0], lambda d: T.PP[d], T.PL[rank], "arrP", "locP", ["PP"]),
+               lambda: send(plan(T, topo, rank, "S")[0], lambda d: T.SS[d], T.SL[rank], "arrS", "locS", ["SS"])]
+    queries[0]()
+    queries[1]()
     G("iota", (T.VA[:], [[1, 4], [0, 4]], 0, 0), [], ["VA"], **fl)
     G("iota", (T.VB[:], [[0, 4], [1, 4]], -60, 0), [], ["VB"], **fl)
-    send(plan(T, topo, rank, "P")[0], lambda d: T.PP[d], T.PL[rank], "arrP", "locP", ["PP"])
+    for y in range(2):
+        G("iota", (T.UI[:, 32 * y:32 * y + 32], [[4 - 4 * y, 2], [1, 4], [4, 4]], 4 * y - 4, 0), [], ["UI"], **fl)
+    G("asel", (T.PERM[:], T.ONE1[:], [[-1, 64], [-64, 2]], A.is_equal, 0.0, 0, 1), ["ONE1"], ["PERM"])
+    tri = lambda t: G("asel", (T.TRI[64 * t:64 * t + 64, :], T.ONE1[64 * t:64 * t + 64, :], [[1, 2], [2, 64]], A.is_ge, 0.0, -1 - t, -2), ["PERM", "ONE2"], ["TRI"])
+    tri(0)
 
-    def turn(n):
-        c0, b = 256 * n, n % 2
-        V("copy", (T.D[:, c0:c0 + 256], T.D32[:, c0:c0 + 256]), ["D32%d" % n], ["D%d" % n])
-        tile = lambda h: T.D[:, c0 + 128 * h:c0 + 128 * h + 128]
-        mms([(PS[b][:, h], tile(h), T.ID[:], True, True) for h in range(2)], ["D%d" % n, "ID"], ["P%d" % b])
-        mms([(T.PV[:, 1024 * b + 128 * h:1024 * b + 128 * h + 128], tile(h), T.ID[:]) for h in range(2)], ["D%d" % n, "ID"], ["PV%d" % b])
-        S("act", (T.G3[:, c0:c0 + 256], PS[b][:, 0:2], AF.Relu), ["P%d" % b], ["P%d" % b, "G3%d" % n], bias=-2.0)
+    half = lambda n, t: T.D[:, 256 * n + 128 * t:256 * n + 128 * t + 128]
+    mb = lambda n: 2 + n % 2 if NB == 2 else (2 + n) % 4
+    mixed = lambda n, t, F: [(T.PSA[:, 512 * mb(n) + h:512 * mb(n) + RW:2], F[:, 256 * n + 128 * h:256 * n + 128 * h + 128], T.M[:, 60 * t:60 * t + 60],
+                              t == 2 and h == 0, t == 1 and h == 1) for h in range(2)]
+    sends = plan(T, topo, rank, "X")
 
-    def mix(n):
-        c0, b, d, o, pk = 256 * n, n % 2, order[n], 512 * (n % 4), "A%d" % (n % 4)
+    def convert(n):
+        V("copy", (T.D[:, 256 * n:256 * n + 256], T.D32[:, 256 * n:256 * n + 256]), ["D32%d" % n], ["D%d" % n])
+        if n == MFIN:
+            matrices()
+
+    def turn_v(n):
+        mms([(T.PV[:, 4 * (n % 2), :, t, :], half(n, t), T.ID[:]) for t in range(2)], ["D%d" % n, "ID"], ["PV%d" % (n % 2)])
+
+    def turn_a(n):
+        mms([(PS[n % 2][:, 128 * h + 64 * t:128 * h + 64 * t + 64], half(n, t), T.ID[:, 4 * h:4 * h + 4], True, True) for t in range(2) for h in range(2)], ["D%d" % n, "ID"], ["P%d" % (n % 2)])
+
+    def feature_a(n):
+        S("act", (T.G3[:, 256 * n:256 * n + 256], PS[n % 2][:, 0:256], AF.Relu), ["P%d" % (n % 2)], ["P%d" % (n % 2), "G3%d" % n], bias=-2.0)
+
+    def feature_v(n):
         for t, F in ((1, T.G1), (2, T.G2)):
-            V("ts", (F[:, c0:c0 + 256], T.PV[:, 1024 * b:1024 * b + 256], float(t), None, A.is_ge), ["PV%d" % b] * (t == 1), ["PV%d" % b, "G%d%d" % (t, n)])
-        mms([(T.PSA[:, o:o + RW], T.ONE1[0:1, :], T.MC[0:1, :], True, False)], ["MC0", "MC1", "MC2", "ONE1"], [pk])
-        mms([(T.PSA[:, o + h:o + 120:2], F[:, c0 + 128 * h:c0 + 128 * h + 128], T.M[:, 60 * t:60 * t + 60], False, t == 1 and h == 1)
-             for t, F in ((2, T.G3), (0, T.G1), (1, T.G2)) for h in range(2)], ["G1%d" % n, "G2%d" % n, "G3%d" % n, "M0", "M1", "M2", "Mt"], [pk])
-        out, k = (T.SEND[:, d, :], "SX%d" % d) if d != rank else (T.LR[:, rank, :], "LRs")
-        cp("a", out, T.PSA[:, o:o + RW], [pk], [pk, k])
-        if n in SENDS:
-            call = plan(T, topo, rank, "X")[SENDS.index(n)]
-            send(call, lambda d: T.SEND[:, d, :], T.LR[:, rank, :], "arrX", "locX", ["SX%d" % d for d, _ in call])
+            V("ts", (F[:, 256 * n:256 * n + 256], T.PV[:, 4 * (n % 2)], float(t), None, A.is_ge), ["PV%d" % (n % 2)] * (t == 1), ["PV%d" % (n % 2), "G%d%d" % (t, n)])
 
-    for n in range(9):
-        if n < 8:
-            turn(n)
-        if n > 0:
-            mix(n - 1)
+    def mix_a(n):
+        mms(mixed(n, 2, T.G3) + [(T.PSA[:, 512 * mb(n):512 * mb(n) + 66], T.ONE1[0:1, :], T.MC[0:1, :], False, False)],
+            ["G3%d" % n, "M2", "Mt", "MC0", "MC1", "ONE1"], ["A%d" % mb(n)])
 
-    def fill(out, n, x, wr, p0=0, p1=128):
-        S("act", (out, T.G3[p0:p1, 0:n], AF.Copy), ["G30", "G31", "G32"], wr, scale=0.0, bias=float(x))
+    def mix_v(n):
+        mms(mixed(n, 0, T.G1) + mixed(n, 1, T.G2), ["G1%d" % n, "G2%d" % n, "M0", "M1"], ["A%d" % mb(n)])
 
-    fill(T.TB[:, :, 0, :], 512, -81920, ["TBU"])
-    fill(T.TB[:, :, 1:4, 12:16], 384, -102400, ["TB3"])
-    fill(T.AD[:, :, 0, :], 64, 224, ["AD0"])
-    V("memset", (T.ONE2[:], 1.0), [], ["ONE2"])
-    G("asel", (T.TRI[:], T.ONE1[:], [[1, 128]], A.is_ge, 0.0, -1, -1), ["ONE1"], ["TRI"])
-    send(plan(T, topo, rank, "S")[0], lambda d: T.SS[d], T.SL[rank], "arrS", "locS", ["SS"])
-    G("asel", (T.SEL[:], T.ONE2[:], [[-16, NPE], [0, 8], [-1, 16]], A.is_equal, 0.0, 0, 1), ["ONE2"], ["SEL"])
+    def leave(n):
+        d, o, pk = order[n], 512 * mb(n), "A%d" % mb(n)
+        out, k = (T.SEND, "SX%d" % d) if d != rank else (T.LR, "LRs")
+        for h in range(2):
+            cp("a", out[:, d, :, h, :], T.PSA[:, o + h:o + RW:2], [pk] * (h == 0), [pk, k])
+        for call in sends:
+            if call[-1][0] == d:
+                send(call, lambda d: T.SEND[:, d], T.LR[:, rank], "arrE" if d // 4 == e0 else "arrL", "locX", ["SX%d" % d for d, _ in call])
+        if n == 2:
+            G("iota", (T.ONE2[:], [[0, 256]], 1, 0), [], ["ONE2"], **fl)
+        if n == 4:
+            tri(1)
+
+    def filler(n):
+        if 2 <= n < 6:
+            fill(T.TB[:, n - 2, :, 0, :], 128, -81920, ["TBU"])
+        if n == 6:
+            fill(T.AD[:, :, 0, :], 64, 224, ["AD0"])
+
+    calls = {"c": convert, "t": turn_v, "u": turn_a, "r": feature_a, "f": feature_v, "m": mix_a, "n": mix_v, "k": leave, "x": filler}
+    todo = [(x[0], n + int(x[1])) for n in range(-4, 8) for x in PIECE.split() if 0 <= n + int(x[1]) < 8]
+    if C7:
+        todo.remove(("c", 7))
+        todo.insert(todo.index(("f", C7)) + 1, ("c", 7))
+        for x in "urt":
+            if todo.index((x, 7)) < todo.index(("c", 7)):
+                todo.remove((x, 7))
+                todo.insert(todo.index(("f", C7 + 1)), (x, 7))
+    for x, n in todo:
+        calls[x](n)
+
+    for a, b, w in ((32, 80, 16), (0, 32, 32)):
+        G("asel", (T.RS[:, a:b], T.ONE1[:, a:b], [[0, (b - a) // w], [1, w]], A.is_gt, 0.0, 0, 0), ["TRI"], ["RS"])
+    G("iota", (T.UC[:], [[0, 8], [1, 4]], 0, 0), [], ["UC"], **fl)
+    for h in range(2):
+        for k in (2, 0):
+            G("asel", (T.SEL[:, h, k:k + 2], T.ONE2[:], [[-32, 2], [0, 8], [-2, 16]], A.is_equal, 0.0, -h - 32 * k, 1), ["ONE2"], ["SEL%d" % h])
+    G("iota", (T.FOUR[:], [[252, 2], [0, 32]], 4, 0), [], ["FOUR"], **fl)
     G("asel", (T.GA[:], T.FOUR[:], [[0, 2], [-16, 8], [0, 4]], A.is_ge, 0.0, 0, 1), ["FOUR"], ["GA"])
     G("asel", (T.GB[:], T.GA[:], [[0, 2], [16, 8], [0, 4]], A.is_ge, 0.0, 14, -1), ["GA"], ["GB"])
-    for d, n, sh in ((2, 15, 0), (3, 3, 2), (4, 7, 4), (5, 31, 2)):
-        V("ts", (T.KI[:, d:d + 1], T.KI[:, 0:1], sh, n, A.arith_shift_right, A.bitwise_and), ["KI0"], ["KI"])
-    V("ts", (col(6), col(1), 3.0, -64.0, A.not_equal, A.mult), ["K1"], ["K6"])
-    V("copy", (T.KF[:, 2:6], T.KI[:, 2:6]), ["KI"], ["KF"])
-    V("ts", (col(7), col(1), 2.0, 256.0, A.is_lt, A.mult), ["K1"], ["K7"])
-    V("ts", (col(8), col(1), 0.0, -17.0, A.is_equal, A.mult), ["K1"], ["K8"])
-    V("ts", (col(9), col(3), 8.0, col(4), A.mult, A.add), ["KF"], ["K9"])
-    V("ts", (T.MASK[:, 64:128], T.UC[:], col(3), None, A.is_le), ["UC", "KF"], ["MASK1"])
-    V("ts", (T.L0[:], T.VA[:], col(2), -BIG, A.not_equal, A.mult), ["VA", "KF"], ["L0"])
-    V("ts", (T.MASK[:, 0:64], T.UI[:], col(9), None, A.is_lt), ["UI", "K9"], ["MASK0"])
-    V("ts", (T.W0[:], T.RI[:], col(2), 128.0, A.is_gt, A.mult), ["RI", "KF"], ["W0"])
-    V("tt", (T.LW[:], T.L0[:], T.VB[:], A.add), ["L0", "VB"], ["LW"])
-    V("tt", (T.W[:, 0:64], T.W0[:], T.CI[:], A.add), ["W0", "CI"], ["W"])
-    V("ts", (T.EQ[:], T.CQ[:], col(5), None, A.is_equal), ["CQ", "KF"], ["EQ"])
     G("asel", (T.RST[:], T.ONE1[:, 0:64], [[0, 16], [1, 4]], A.is_gt, 0.0, 0, 0), ["ONE1"], ["RST"])
-    for p0, x, y in ((0, 0xC20000, 0x60000), (32, 0xD600, 0x80), (64, 0xFC, 0)):
+    for p0, x, y in ((0, 0xC20000, 0x60000), (32, 0xD600, 0x80), (64, 0xFC, 0x100)):
         for o, z in ((0, x), (32, y)):
             G("iota", (T.CON[p0:p0 + 32, o:o + 32], [[0, 32]], z, 0), ["RST", "CON"], ["CON"], **fl)
-    V("memset", (T.NX[:, 48:64], -60.0), [], ["NX1"])
+    S("act", (col(0), col(1), AF.Relu), ["KF"], ["K0"], bias=-1.0)
+    S("act", (T.NID[:], T.ID[:], AF.Copy), ["ID"], ["NID"], scale=-1.0)
+    vc = [lambda: V("ts", (T.W0[:], T.RI[:], col(2), 128.0, A.is_gt, A.mult), ["RI", "KF"], ["W0"]),
+          lambda: V("ts", (col(9), col(5), 4.0, col(6), A.mult, A.add), ["KF"], ["K9"]),
+          lambda: V("ts", (col(12), col(5), 4.0, None, A.mult), ["KF"], ["K12"]),
+          lambda: V("ts", (T.KB[:, 2:3], col(4), 1.0, 32.0, A.is_equal, A.mult), ["KF"], ["KB2"]),
+          lambda: V("ts", (T.EQ[:], T.CQ[:], col(3), None, A.is_equal), ["CQ", "KF"], ["EQ"]),
+          lambda: V("tt", (T.W[:, 0:64], T.W0[:], T.CI[:], A.add), ["W0", "CI"], ["W"]),
+          lambda: V("ts", (col(7), col(1), 2.0, 256.0, A.is_lt, A.mult), ["KF"], ["K7"]),
+          lambda: V("ts", (T.MASK[:, 0:32], T.UI[:, 0:32], col(12), None, A.is_lt), ["UI", "K12"], ["PN"]),
+          lambda: V("ts", (T.MS[:, 0:32], T.UI[:, 32:64], col(9), None, A.is_lt), ["UI", "K9"], ["MS"]),
+          lambda: V("ts", (col(11), col(4), 3.0, -64.0, A.not_equal, A.mult), ["KF"], ["K11"]),
+          lambda: V("ts", (T.L0[:], T.VA[:], col(2), -BIG, A.not_equal, A.mult), ["VA", "KF"], ["L0"]),
+          lambda: V("tt", (T.MASK[:, 64:80], T.MASK[:, 0:16], T.MASK[:, 16:32], A.subtract), ["PN"], ["MASK"]),
+          lambda: V("tt", (T.MASK[:, 32:64], T.MS[:, 0:32], T.MASK[:, 0:32], A.subtract), ["PN", "MS"], ["MASK", "MT"]),
+          lambda: V("ts", (col(8), col(4), 0.0, -17.0, A.is_equal, A.mult), ["KF"], ["K8"]),
+          lambda: V("tt", (T.LW[:], T.L0[:], T.VB[:], A.add), ["L0", "VB"], ["LW"])]
+    for f in vc[:NPRE]:
+        f()
+
+    wide = lambda w: cp("a", T.W[:, w:2 * w], T.W[:, 0:w], ["W"], ["W"])
+    S("act", (col(10), col(0), AF.Exp), ["K0"], ["K10"], scale=math.log(64.0), bias=math.log(4.0))
+    S("act", (T.KB[:, 1:2], col(4), AF.Exp), ["KF"], ["KB1"], scale=math.log(64.0), bias=-math.log(128.0))
+    wide(64)
     S("act", (T.SELY[:, 0:32], T.EQ[:], AF.Copy), ["EQ", "K10"], ["SELY0"], scale=col(10))
     S("act", (T.SELY[:, 32:64], T.EQ[:], AF.Copy), ["EQ", "K7"], ["SELY1"], scale=col(7))
+    wide(128)
     for h in range(2):
         S("act", (T.SELQ[:, 32 * h:32 * h + 32], T.ID[:, :, 0, :], AF.Copy), ["ID"], ["SELQ%d" % h], scale=64.0 ** h)
-    S("act", (T.SELZ[:], T.SELY[:], AF.Copy), ["SELY0", "SELY1"], ["SELZ"], scale=-1.0)
-    for w in (64, 128, 256, 512):
-        cp("v", T.W[:, w:2 * w], T.W[:, 0:w], ["W"], ["W"])
-    cp("v", T.W[:, 1024:1088], T.W[:, 0:64], [], ["W"])
 
-    dma("s", T.PT[:], T.PL[:], "lpt", ["PL", "PLs"], ["PT"])
-    dma("s", T.ST[:], T.SL[:], "lst", ["SL", "SLs"], ["ST"])
+    def selectors():
+        wide(256)
+        S("act", (T.SELZ[:], T.SELY[:], AF.Copy), ["SELY0", "SELY1"], ["SELZ"], scale=-1.0)
+        wide(512)
+        cp("a", T.W[:, 1024:1344], T.W[:, 0:320], [], ["W2"])
+
+    fetch = [lambda: dma("s", T.PT[:], T.PL[:], "lpt", ["PL", "PLs"], ["PT"]), lambda: dma("s", T.ST[:], T.SL[:], "lst", ["SL", "SLs"], ["ST"])]
+    fetch[PLAST]()
+    fetch[1 - PLAST]()
 
     def pairs():
         return [lambda: V("ts", (T.P4[:], T.PT[:, :, 0, :], 4.0, None, A.mult), ["PT"], ["P4"]),
@@ -280,117 +354,142 @@ def rank_program(g, core, T, topo):
                 lambda: V("copy", (T.OFP[:], T.PI[:]), ["PI"], ["OFP"])]
 
     def spread(u):
-        S("act", (T.LTR[:, 512 * u:512 * u + 512], T.LW[:, 0:16].indirect(T.OFP[:, 32 * u:32 * u + 32]), AF.Copy), ["LW", "OFP"], ["LTR%d" % u])
+        S("act", (T.LTR[:, 128 * u:128 * u + 128], T.LW[:, 0:16].indirect(T.OFP[:, 8 * u:8 * u + 8]), AF.Copy), ["LW", "OFP"], ["LTR%d" % u])
 
     def odd():
-        V("ts", (T.NX[:, 0:48], T.PT[:, 1:4, 0, :], -60.0, None, A.add), ["PT"], ["NX0"])
-        for c in range(4):
-            V("ts", (T.AM[:, 64 * c:64 * c + 64], T.PT[:, :, 1, :], float(c), -BIG, A.not_equal, A.mult), ["PT"], ["AM%d" % c])
-        for c in range(4):
-            V("tt", (T.QTB[:, :, 0, :, c], T.AM[:, 64 * c:64 * c + 64], T.NX[:], A.add), ["AM%d" % c, "NX0", "NX1"], ["QTB0"])
+        return ([lambda: V("ts", (T.NX[:], T.PT[:, :, 1, :], BIG, None, A.mult), ["PT"], ["NX"]),
+                 lambda: V("tt", (T.NX[:, 0:48], T.NX[:, 0:48], T.PT[:, 1:4, 0, :], A.subtract), ["NX", "PT"], ["NX"])] +
+                [lambda h=h, c=c: S("act", (T.QTB[:, :, h, :, c], T.NX[:], AF.Abs), ["NX"], ["QTB"], scale=64.0 ** h, bias=64.0 ** h * (60 - BIG * c))
+                 for h in range(2) for c in range(4)])
 
     def starts():
         OK = ["O:%d" % u for u in range(4)]
-        return [[lambda: V("ts", (T.QTB[:, :, 1], T.QTB[:, :, 0], 64.0, None, A.mult), ["QTB0"], ["QTB1"]),
-                 lambda: V("ts", (T.X[:, 16384:16385], T.BX[:, 5:6], col(8), -81536.0, A.add, A.add), ["BX2", "K8"], ["XE"])],
-                [lambda: V("ts", (T.ST4[:], T.ST[:], 4.0, None, A.mult), ["ST"], ["ST4"]),
-                 lambda: V("ts", (T.O[:, :, 0:8], T.ST[:], 1.0 / 16, -0.5 + 0.5 / 16, A.mult, A.add), ["ST"], OK)],
-                [lambda h=h: V("tt", (T.I[:, 16 * h:16 * h + 16], T.ST4[:, 16 * h:16 * h + 16], T.PT[:, 0, 0, :], A.add), ["ST4", "PT"], ["I"]) for h in range(2)],
-                [lambda: V("ts", (T.J[:], T.I[:], 63, None, A.bitwise_and), ["I"], ["J"])],
-                [lambda: V("copy", (T.O[:, :, 8:16], T.J[:]), ["J"], OK)]]
+        return ([lambda: V("ts", (T.ST4[:], T.ST[:], 4.0, None, A.mult), ["ST"], ["ST4"]),
+                 lambda: V("ts", (T.O[:, :, 0:8], T.ST[:], 1.0 / 16, -0.5 + 0.5 / 16, A.mult, A.add), ["ST"], OK)] +
+                [lambda h=h: V("tt", (T.I[:, 16 * h:16 * h + 16], T.ST4[:, 16 * h:16 * h + 16], T.PT[:, 0, 0, :], A.add), ["ST4", "PT"], ["I"]) for h in range(2)] +
+                [lambda: V("ts", (T.J[:], T.I[:], 63, None, A.bitwise_and), ["I"], ["J"]),
+                 lambda: V("copy", (T.O[:, :, 8:16], T.J[:]), ["J"], ["OW"])])
 
-    PO = lambda b, m: T.PSA[:, 512 * b + m:512 * b + 512:4]
-    slot = lambda b, m: 2 * (b + 4 * (m % 2)) + m // 2
+    small = {"p": pairs(), "q": odd(), "s": starts(), "x": [lambda u=u: spread(u) for u in range(NSP)]}
+
+    def smalls(at):
+        for x in SMALL.get(at, "").split():
+            small[x[0]][int(x[1])]()
+
     turns = TURNS.split()
+    bk = lambda e, b: 2 * (e != e0) + b
+    LK = lambda e: ["LR%d" % e] + ["LRs"] * (e == rank // 4)
 
-    def turned(n):
+    def turned(e, n):
         x, j = turns[n], int(turns[n][1])
-        first, final = (all(int(y[1]) % 2 != j % 2 for y in part) for part in (turns[:n], turns[n + 1:]))
-        for b in (2 * (j % 2), 2 * (j % 2) + 1):
-            ms = range(4) if x[0] == "D" else (j // 2, j // 2 + 2)
-            mms([(PO(b, m), T.AD[:, :, :, m // 2] if x[0] == "D" else T["T" + x[0]][:, :, :, slot(b, m)], T.ID[:], first and m == ms[0], final and m == ms[-1]) for m in ms],
-                {"A": ["TAU", "T" + x], "B": ["TBU", "T" + x], "D": ["AD0", "AD"]}[x[0]] + ["ID"], ["A%d" % b])
+        for b in range(2):
+            js = (2 * j, 2 * j + 1) if x[0] == "D" else (j,)
+            src = lambda y: T.AD[:, 16 * e:16 * e + 16] if x[0] == "D" else T["T" + x[0]][:, y, 16 * e:16 * e + 16, :, b:4:2]
+            mms([(T.PSA[:, 512 * bk(e, b) + y:512 * bk(e, b) + 512:4], src(y), T.PERM[:], n == 0, n == len(turns) - 1 and y == js[-1]) for y in js],
+                {"A": ["TU%d%d" % (j, e), "T%s%d" % (x, e)], "B": ["TBU", "TB3" if j == 3 else "T%s%d" % (x, e)], "D": ["AD0", "AD%d" % (e + 1)]}[x[0]] + ["PERM"], ["A%d" % bk(e, b)])
 
-    turned(0)
-    LK = ["LR", "LRs"]
-    tot = lambda h: T.LR[:, :, 112 + h:120:2]
-    before = lambda h: T.PS0[:, 0, 0, h:64:2]
-    mms([(before(0), T.TRI[:], tot(0), True, False), (before(0), T.TRI[:], tot(1), False, True),
-         (before(1), T.TRI[:], tot(0), True, False), (before(1), T.TRI[:], tot(1), False, False),
-         (before(1), T.ID[:], tot(0), False, True)], LK + ["TRI", "ID"], ["P0"])
-    mms([(T.PS1[:, 0, h], T.ONE1[:], T.LR[:, :, 112:120], True, True) for h in range(2)], LK + ["ONE1"], ["P1"])
+    def before(e):
+        tot = lambda h: T.LR[:, 4 * e:4 * e + 4, 16:18, h, :]
+        out = lambda h: T.PS0[:, h:32:2]
+        mms([(out(0), T.TRI[:], tot(0), True, False), (out(1), T.ONE1[:], tot(0), False, False), (out(1), T.TRI[:], tot(1), False, True)],
+            LK(e) + ["TRI", "ONE1"], ["P0"])
 
-    def plane(x):
+    def plane(e, x):
         j = int(x[2])
         if x[1] == "U":
-            cp(x[0], T.TA[:, :, 0, :], T.LR[:, :, 0:64], LK, ["TAU"])
+            cp(x[0], T.TA[:, j, 16 * e:16 * e + 16, 0, :], T.LR[:, 4 * e:4 * e + 4, j:16:4], LK(e), ["TU%d%d" % (j, e)])
             return
         k = j + (x[1] == "B")
         add = TOFF[k] + (((160.0 if j else 0.0) if x[1] == "A" else (800.0 if j else 640.0)) * 4 ** j)
         sc = (128.0 if x[1] == "A" else -128.0) / 4 ** j
-        args, wr = (T["T" + x[1]][:, :, 1:4, 4 * j:4 * j + 4], T.LR[:, :, 64:112]), ["T" + x[1:]]
+        args, wr = (T["T" + x[1]][:, j, 16 * e:16 * e + 16, 1:4, :], T.LR[:, 4 * e:4 * e + 4, 18:30]), ["T%s%d" % (x[1:], e)]
         if x[0] == "v":
-            V("ts", args + (add, sc, A.add, A.mult), LK, wr)
+            V("ts", args + (add, sc, A.add, A.mult), LK(e), wr)
         else:
-            S("act", args + (AF.Copy,), LK, wr, scale=sc, bias=sc * add)
+            S("act", args + (AF.Copy,), LK(e), wr, scale=sc, bias=sc * add)
 
-    pl, pr = PLANES.split(), pairs()
-    for x in pl:
-        if x[0] == "a":
-            plane(x)
-    pl = [x for x in pl if x[0] == "v"]
-    plane(pl[0])
-    pr[0]()
-    plane(pl[1])
-    pr[1]()
-    plane(pl[2])
-    V("copy", (T.NI[:], T.PS0[:, 0, 0]), ["P0"], ["P0", "NI"])
-    V("tt", (T.MS[:], T.PS1[:, 0], T.MASK[:], A.mult), ["P1", "MASK0", "MASK1"], ["P1", "MS"])
-    pr[2]()
-    spread(0)
-    for i, (sh, n) in enumerate(((0, 63), (6, 63), (12, 63))):
-        V("ts", (T.DI[:, :, i, :], T.NI[:], sh, n, A.arith_shift_right, A.bitwise_and), ["NI"], ["DI"])
-    for h in range(2):
-        V("red", (T.BX[:, h:h + 1], T.MS[:, 64 * h:64 * h + 64], AxisListType.X, A.add), ["MS"], ["BX0"])
-    V("copy", (T.AD[:, :, 1:4, :], T.DI[:]), ["DI"], ["AD"])
-    V("ts", (T.BI[:, 2:4], T.BX[:, 0:2], T.KB[:, 0:1], 1.0 / 64, A.mult, A.mult), ["BX0", "KB0"], ["BI1"])
-    V("ts", (T.BI[:, 0:2], T.BX[:, 0:2], T.KB[:, 0:1], None, A.mult), ["BX0", "KB0"], ["BI0"])
-    plane(pl[3])
-    V("ts", (T.BX[:, 2:4], T.BI[:, 2:4], col(6), 81696.0, A.mult, A.add), ["BI1", "K6"], ["BX1"])
-    plane(pl[4])
-    V("tt", (T.BX[:, 4:6], T.BI[:, 0:2], T.BX[:, 2:4], A.add), ["BI0", "BX1"], ["BX2"])
+    def digits(e):
+        ni = T.NI[:, 32 * e:32 * e + 32]
+        return ([lambda: V("copy", (ni, T.PS0[:, 0:32]), ["P0"], ["P0", "NI%d" % e])] +
+                [lambda i=i: V("ts", (T.DI[:, 16 * e:16 * e + 16, i, :], ni, 6 * i, 63, A.arith_shift_right, A.bitwise_and), ["NI%d" % e], ["DI%d" % e]) for i in range(3)] +
+                [lambda: V("copy", (T.AD[:, 16 * e:16 * e + 16, 1:4, :], T.DI[:, 16 * e:16 * e + 16]), ["DI%d" % e], ["AD%d" % (e + 1)])])
+
+    def out_of(e, b, q):
+        k, bias = "A%d" % bk(e, b), T.BX[:, 9:10] if e == e0 else T.BX[:, 5 + e:6 + e]
+        args, rd, wr = (T.XC[:, 1024 * e + b:1024 * e + 1024:2], T.PSA[:, 512 * bk(e, b):512 * bk(e, b) + 512]), [k, "BX2%d" % e], [k, "XC%d%d" % (e, b)]
+        if q == "v":
+            V("ts", args + (bias, None, A.add), rd, wr)
+        else:
+            S("act", args + (AF.Identity,), rd, wr, bias=bias)
+
+    def counts(e, parts, m0, i0, o0):
+        w = sum(b - a for a, b in parts) * 4
+        n = 1 if w == 16 else 4
+        mms([(T.PS1[:, 4 * sum(y - x for x, y in parts[:j]):4 * sum(y - x for x, y in parts[:j + 1])], T.ONE1[:], T.LR[:, a:b, 16:18, h, :], j + h == 0, j + h == len(parts))
+             for j, (a, b) in enumerate(parts) for h in range(2)], LK(e0) + LK(e) + ["ONE1"], ["P1"])
+        mt, k = T.MT[:, w + 15 - 16 * n:w:16], lambda x: x + str(e)
+        return [lambda: V("tt", (T.MS[:, 0:w], T.PS1[:, 0:w], T.MASK[:, m0:m0 + w], A.mult), ["P1", "MASK", "MT"], ["P1", "MS"]),
+                lambda: V("scan", (T.MT[:, 0:w], T.RS[:, 80 - w:80], T.MS[:, 0:w], 0.0, A.mult, A.add), ["MS", "RS", "BI"], ["MT"]),
+                lambda: V("ts", (T.BI[:, i0 + n:i0 + 2 * n], mt, T.KB[:, 0:1], 1.0 / 64, A.mult, A.mult), ["MT", "KB0"], [k("BI1")]),
+                lambda: V("ts", (T.BI[:, i0:i0 + n], mt, T.KB[:, 0:1], None, A.mult), ["MT", "KB0"], [k("BI0"), "BI"]),
+                lambda: V("ts", (T.BX[:, o0:o0 + n], T.BI[:, i0 + n:i0 + 2 * n], col(11), 81696.0, A.mult, A.add), [k("BI1"), "K11"], [k("BX1")]),
+                lambda: V("tt", (T.BX[:, o0 + n:o0 + 2 * n], T.BI[:, i0:i0 + n], T.BX[:, o0:o0 + n], A.add), [k("BI0"), k("BX1")], [k("BX2")])]
+
+    def build(e, order, bias):
+        dg = digits(e)
+        for f in order.split():
+            if f[1] == "X":
+                out_of(e0, int(f[2]), f[0])
+            else:
+                plane(e, f) if len(f) == 3 else {"b": bias, "d": dg}[f[0]][int(f[1])]()
+
+    turned(e0, 0)
+    before(e0)
+    build(e0, EARLY, counts(e0, [(4 * e0, 4 * e0 + 4)], 32 + 16 * e0, 8, 8))
     for n in range(1, len(turns)):
-        turned(n)
-    odd()
-    small = starts()
-    for b in range(4):
-        args, rd, wr = (T.XC[:, b:2048:4], T.PSA[:, 512 * b:512 * b + 512]), ["A%d" % b, "BX2"], ["A%d" % b, "XC%d" % b]
-        if XCQ[b] == "v":
-            V("ts", args + (T.BX[:, 4:5], None, A.add), rd, wr)
-        else:
-            S("act", args + (AF.Identity,), rd, wr, bias=T.BX[:, 4:5])
-        if b == 1:
-            spread(1)
-        if XCQ[b] == "v":
-            for f in small.pop(0):
-                f()
+        turned(e0, n)
+    turned(e1, 0)
+    for f in vc[NPRE:]:
+        f()
+    selectors()
+    smalls("early")
+    before(e1)
+    build(e1, LATE, counts(e1, [(0, 8), (0, 8), (4, 8)], 0, 0, 0))
+    XK = []
 
-    XK, XCK = ["XE"], ["XC%d" % b for b in range(4)]
-    share = [min(max(CPE - 2048 * k, 0), 2048) for k in range(8)]
-    for k in range(7, -1, -1):
-        for y in range(8 if share[k] < 2048 else 0):
-            dma("s", T.X[16 * y:16 * y + 16, 2048 * k + share[k]:2048 * k + 2048], T.XC[16 * k:16 * k + 16, share[k]:2048], "rep", XCK, ["XD%d%d" % (k, y)])
-            XK.append("XD%d%d" % (k, y))
-    ring = [(lambda w, b=b: PS[b][:, 0:w // 128], "P%d" % b) for b in range(2)] + [(lambda w, b=b: T.PSA[:, 512 * b:512 * b + w], "A%d" % b) for b in range(4)]
-    for n, (b, k) in enumerate((b, k) for b in range(4) for k in range(NPE)):
-        ps, pk = ring[n % 6]
-        ps = ps(share[k] // 4)
-        mms([(ps, T.SEL[:, 128 * k:128 * k + 128], T.XC[:, b:share[k]:4], True, True)], ["XC%d" % b, "SEL"], [pk])
-        cp(XQ[n % len(XQ)], T.X[:, 2048 * k + b:2048 * k + share[k]:4], ps, [pk], [pk, "X%d" % n])
+    def copies(e, quarters):
+        for k in range(-(-quarters // 4)):
+            for y in range(8):
+                c0, w = 2048 * (4 * e + k), min(512 * (quarters - 4 * k), 2048)
+                dma("s", T.X[16 * y:16 * y + 16, c0:c0 + w], T.XC[32 * k:32 * k + 32:1 + (w < 2048), 1024 * e:1024 * e + min(w, 1024)], "rep", ["XC%d0" % e, "XC%d1" % e], ["XD%d%d%d" % (e, k, y)])
+                XK.append("XD%d%d%d" % (e, k, y))
+
+    copies(e0, NDMA[0])
+    for n in range(1, len(turns)):
+        turned(e1, n)
+    V("ts", (T.XE[:, 0:1], T.BX[:, 7:8], col(8), -81536.0, A.add, A.add), ["BX2%d" % e1, "K8"], ["XE"])
+    small["k"] = ([lambda h=h: V("ts", (T.BX[:, 10 + h:11 + h], T.BX[:, 4:5], -81696.0, T.KB[:, 1 + h:2 + h], A.add, A.mult), ["BX2%d" % e1, "KB1", "KB2"], ["DW%d" % h]) for h in range(2)] +
+                  [lambda h=h: V("ts", (T.MID[:, 32 * h:32 * h + 32], T.UC[:], col(5), T.BX[:, 10 + h:11 + h], A.is_equal, A.mult), ["DW%d" % h, "UC"], ["MID"]) for h in range(2)])
+    smalls("last")
+    for b in range(2):
+        out_of(e1, b, "av"[b])
+    copies(e1, NDMA[1])
+
+    ring = [(PS[b], 0, "P%d" % b) for b in range(2)] + [(T.PSA, 512 * b, "A%d" % b) for b in range(4)]
+    mine = [(e, n // 4, n // 2 % 2, 512 * (n % 2), 512) for e, a in zip((e0, e1), NDMA) for n in range(a, 16)]
+    if XH:
+        x = mine.pop()
+        mine += [x[:3] + (512, XH), x[:3] + (512 + XH, 512 - XH)]
+    for n in range(-1, len(mine)):
+        ps, o, pk = ring[(n + 1) % 6]
+        e, k, h, c0, w = mine[n] if n >= 0 else (0, 0, 0, 0, 1)
+        src, rd = (T.XC[:, 1024 * e + c0:1024 * e + c0 + w], ["XC%d0" % e, "XC%d1" % e]) if n >= 0 else (T.XE[:, 0:1], ["XE"])
+        x0 = 2048 * (4 * e + k) + 1024 * h + c0 if n >= 0 else 16384
+        q = XQ[n + 1]
+        mms([(ps[:, o:o + w], T.SEL[:, h, k], src, True, True)], rd + ["SEL%d" % h], [pk])
+        cp(q, T.X[:, x0:x0 + w], ps[:, o:o + w], [pk], [pk, "X%d" % n])
         XK.append("X%d" % n)
-        if XQ[n % len(XQ)] == "v" and small:
-            for f in small.pop(0):
-                f()
+        smalls(n)
 
     key = lambda name, n: "%s:%d" % (name, n % 4)
     tile = lambda name, n: T[name][:, 128 * (n % 4):128 * (n % 4) + 128]
@@ -398,40 +497,46 @@ def rank_program(g, core, T, topo):
     st = lambda n, a, b, s: T.SC[:, 64 * (n % 4) + a:64 * (n % 4) + b:s]
 
     def pick(n):
-        if 4 <= n < 36:
-            V("scan", (st(n, 0, 64, 1), T.RST[:], bank(n), 0.0, A.mult, A.max), ["A%d" % (n % 4), "RST"], ["A%d" % (n % 4), key("S", n)])
+        V("scan", (st(n, 0, 64, 1), T.RST[:], bank(n), 0.0, A.mult, A.max), ["A%d" % (n % 4), "RST"], ["A%d" % (n % 4), key("S", n)])
+
+    def offsets(n):
+        if n >= 32:
+            V("ts", (T.RES[:, 8 * (n % 4):8 * (n % 4) + 8], st(n, 3, 32, 4), 0.25, None, A.mult), [key("S", n)], ["RES%d" % (n % 4)])
+        else:
+            V("ts", (T.O[:, n % 4, :], st(n, 3, 64, 4), 1.0 / 64, -0.5 + 0.5 / 64, A.mult, A.add), [key("S", n)], [key("O", n)])
 
     def block(n):
-        if 32 <= n < 36:
-            V("ts", (T.RES[:, 8 * (n % 4):8 * (n % 4) + 8], st(n, 3, 32, 4), 0.25, None, A.mult), [key("S", n)], ["RES%d" % (n % 4)])
-        if 4 <= n < 32:
-            V("ts", (T.O[:, n % 4, :], st(n, 3, 64, 4), 1.0 / 64, -0.5 + 0.5 / 64, A.mult, A.add), [key("S", n)], [key("O", n)])
-        if n < 32:
-            S("act", (tile("Z", n), T.X[:, 0:16385].indirect(T.O[:, n % 4, 0:8]), AF.Copy), [key("O", n)] + XK, [key("Z", n)])
-            mms([(bank(n), T.ONE1[0:96, :], T.CON[0:96, :], True, False)], ["ONE1", "CON"], ["A%d" % (n % 4)])
+        S("act", (tile("Z", n), T.X[:, 0:16385].indirect(T.O[:, n % 4, 0:8]), AF.Copy), [key("O", n)] + XK, [key("Z", n)])
 
-    def letters(n):
-        if 0 <= n < 32:
+    def opened(n):
+        mms([(bank(n), T.ONE1[0:96, :], T.CON[0:96, :], True, False)], ["ONE1", "CON"], ["A%d" % (n % 4)])
+
+    def letters(n, q):
+        if q == "v":
             V("ts", (tile("ZL", n), tile("Z", n), 24512.5, None, A.add), [key("Z", n)], [key("ZL", n)])
+        else:
+            S("act", (tile("ZL", n), tile("Z", n), AF.Copy), [key("Z", n)], [key("ZL", n)], bias=24512.5)
 
     def compare(n):
-        if 0 <= n < 32:
-            V("tt", (tile("E", n), T.W[:, 0:1088].indirect(T.O[:, n % 4, 8:16]), tile("Z", n), A.is_gt), [key("O", n), "W", key("Z", n)], [key("E", n)])
+        V("tt", (tile("E", n), T.W[:, 0:1344].indirect(T.O[:, n % 4, 8:16]), tile("Z", n), A.is_gt), [key("O", n), "OW", "W", "W2", key("Z", n)], [key("E", n)])
 
     def sums(n):
-        if 0 <= n < 32:
-            t, k, pk = n // 4, n % 2, "A%d" % (n % 4)
-            nxt = (T.ID[:], T.QTB[:, t // 2, :, 8 * k:8 * k + 8, :]) if t % 2 else (T.LTR[:, 128 * (t + k):128 * (t + k) + 128], T.SELQ[:])
-            mms([(bank(n),) + x + (False, False) for x in ((tile("ZL", n), T.SELZ[:]), nxt, (tile("Z", n), T.SELY[:]))],
-                [key("Z", n), key("ZL", n), "ID", "SELY0", "SELY1", "SELZ", "SELQ0", "SELQ1", "LTR%d" % (t // 4), "QTB0", "QTB1"], [pk])
-            mms([(bank(n), tile("E", n), T.GB[:], False, True)], [key("E", n), "GB"], [pk])
+        t, k = n // 4, n % 2
+        nxt = (T.NID[:], T.QTB[:, t // 2, :, 8 * k:8 * k + 8, :]) if t % 2 else (T.LTR[:, 128 * (t + k):128 * (t + k) + 128], T.SELQ[:])
+        mms([(bank(n),) + x + (False, False) for x in ((tile("ZL", n), T.SELZ[:]), nxt, (T.ONE1[:], T.MID[:]), (tile("Z", n), T.SELY[:]))],
+            [key("Z", n), key("ZL", n), "MID", "NID", "SELY0", "SELY1", "SELZ", "SELQ0", "SELQ1", "QTB" if t % 2 else "LTR%d" % (t + k)], ["A%d" % (n % 4)])
 
-    for n in range(36):
-        pick(n)
-        compare(n - 2)
-        block(n)
-        letters(n - 2)
-        sums(n - 2)
+    def closed(n):
+        mms([(bank(n), tile("E", n), T.GB[:], False, True)], [key("E", n), "GB"], ["A%d" % (n % 4)])
+
+    calls = {"s": pick, "o": offsets, "z": block, "a": opened, "v": lambda n: letters(n, "v"), "l": lambda n: letters(n, "a"), "e": compare,
+             "b": sums, "c": closed, "x": lambda n: spread(NSP - 1 + n // 4)}
+    for t in range(-2, 9):
+        for x in STEP.split():
+            n = 4 * t + int(x[1])
+            if (4 <= n < 36 if x[0] in "so" else 4 <= n < 36 - 4 * NSP if x[0] == "x" else 0 <= n < 32):
+                calls[x[0]](n)
+                smalls(x[0] + str(n))
     dma("s", T.RD[:], T.RES[:], "rd", ["RES0", "RES1", "RES2", "RES3"], ["RD"])
     send(plan(T, topo, rank, "F")[0], lambda d: T.RD[d], T.FL[rank], "arrF", "locF", ["RD"])
     r0, r1 = 16 * rank, 16 * rank + 16

import math
from concourse.bass import DstId, RemoteDMATransfer
from concourse.mybir import AluOpType as A, ActivationFunctionType as AF

NON = 4
XH = 0
XQ = "aavavavavavavava"
NDMA = (13, 4)
PLAST = 0
SMALL = {"early": "p0 p1 p2", "last": "x0 x1 s0 k0 k1 s1 s2 s3 k2 k3", 13: "s4 q0 s5 q1", "l3": "q2 q3 q4 q5 q6 q7 q8 q9"}
MS = 4
NPRE = 20
NSP = 2
MFIN = 0
NB = 4
C7 = 0
PIECE = "r2 c4 u3 f2 m1 k0 t3 n1 x0"
SWAP = False
RW = 120
LQ = "asssssss"
BIG = 2097152.0
TOFF = (0.0, -1.5, -7.5, -31.5)
TURNS = "B3 B0 A0 A2 B2 A1 B1 A3 D0 D1"
EARLY = "aA0 aA2 aA1 aA3 vB0 vU0 vU2 vB2 d0 vU1 vB1 d1 d2 d3 b0 vU3 d4 b1 b2 b3 b4 b5"
LATE = "vX1 aX0 aA0 aA2 aA1 aA3 vB0 vU0 vU2 vB2 d0 b0 vU1 vB1 d1 d2 d3 b1 vU3 d4 b2 b3 b4 b5"
STEP = "z1 o3 a1 v1 e1 c0 z2 b1 a3 s4 a4 z3 e2 o4 l2 l3 e3 c1 b2 c2 s5 z4 s6 o5 b3 c3 x4 v4 o6 s7 a6 e4 b4"

SCRATCH = {
    "PP": ("dram", [8, 128, 16], "int32"), "SS": ("dram", [8, 128, 4], "int32"),
    "PL": ("dram", [8, 128, 16], "int32"), "SL": ("dram", [8, 128, 4], "int32"),
    "RD": ("dram", [8, 128, 4], "float32"), "FL": ("dram", [8, 128, 4], "float32"),
    "PV": ("psum", [128, 8, 2, 2, 64], "bfloat16"), "PSA": ("psum", [128, 2048], "float32"),
    "PS0": ("psum", [128, 512], "float32"), "PS1": ("psum", [128, 512], "float32"),
}
for _n, _w, _d in (
        ("D32", 2048, "int32"), ("D", 2048, "bfloat16"), ("G1", 2048, "bfloat16"), ("G2", 2048, "bfloat16"), ("G3", 2048, "bfloat16"),
        ("SEND", [8, RW // 4, 2, 2], "bfloat16"), ("LR", [8, RW // 4, 2, 2], "bfloat16"), ("M", 180, "bfloat16"), ("MC", 66, "bfloat16"),
        ("DPI", 16, "bfloat16"), ("DP", 16, "bfloat16"),
        ("TA", [4, 32, 4, 4], "bfloat16"), ("TB", [4, 32, 4, 4], "bfloat16"), ("AD", [32, 4, 2], "bfloat16"),
        ("NI", 64, "int32"), ("DI", [32, 3, 2], "int32"), ("UI", 64, "float32"), ("MASK", 80, "float32"), ("MS", 80, "float32"), ("MT", 80, "float32"),
        ("RS", 80, "bfloat16"), ("BX", 12, "float32"), ("BI", 12, "int32"), ("UC", 32, "float32"), ("MID", 64, "bfloat16"), ("XC", 2048, "bfloat16"), ("XE", 8, "bfloat16"), ("X", 16400, "bfloat16"),
        ("ONE1", 128, "bfloat16"), ("ONE2", 256, "bfloat16"), ("FOUR", 64, "bfloat16"), ("GA", 64, "bfloat16"), ("GB", 64, "bfloat16"),
        ("ID", [8, 4, 4], "bfloat16"), ("CON", 64, "bfloat16"), ("TRI", 128, "bfloat16"), ("PERM", 128, "bfloat16"), ("SEL", [2, 4, 128], "bfloat16"),
        ("SELY", 64, "bfloat16"), ("SELZ", 64, "bfloat16"), ("SELQ", 64, "bfloat16"), ("EQ", 32, "bfloat16"), ("CQ", 32, "float32"),
        ("KI", 8, "int32"), ("KF", 16, "float32"), ("KB", 8, "bfloat16"), ("RI", 64, "float32"), ("CI", 64, "bfloat16"), ("W0", 64, "bfloat16"),
        ("VA", 16, "float32"), ("VB", 16, "float32"), ("L0", 16, "float32"),
        ("W", 1344, "bfloat16"), ("LW", 16, "bfloat16"), ("PT", [4, 2, 16], "int32"), ("ST", 32, "int32"), ("ST4", 32, "int32"),
        ("P4", 64, "int32"), ("PI", 64, "int32"), ("OFP", 64, "uint16"), ("LTR", 1024, "bfloat16"), ("NID", 128, "bfloat16"), ("NX", 64, "float32"),
        ("QTB", [4, 2, 16, 4], "bfloat16"), ("RST", 64, "float32"), ("RES", 32, "float32"), ("I", 32, "int32"), ("J", 32, "int32"),
        ("O", [4, 16], "uint16"), ("SC", 256, "float32"), ("Z", 512, "bfloat16"), ("ZL", 512, "bfloat16"), ("E", 512, "bfloat16")):
    SCRATCH[_n] = ("sbuf", [128] + (_w if isinstance(_w, list) else [_w]), _d)
SEMAPHORES = (["vq", "aq", "pq", "gq", "dp", "ds", "dsp", "dss", "lpt", "lst", "rep", "yself", "yout", "rd",
               "arrP", "arrS", "arrE", "arrL", "arrF", "locP", "locS", "locX", "locF"] + ["b%d" % _i for _i in range(8)])


def far_first(T, topo, rank):
    chip = lambda d: topo.chip(T.cores[d])
    return sorted((d for d in range(8) if d != rank), key=lambda d: (chip(d) == chip(rank), topo.same_plane(chip(rank), chip(d)), (d - rank) % 8))


def halves(T, topo, rank):
    far = far_first(T, topo, rank)
    return sorted(far, key=lambda d: (d // 4 == rank // 4) == SWAP)


def plan(T, topo, rank, kind):
    core = T.cores[rank]
    order = far_first(T, topo, rank)
    off, on = order[:6], order[6]
    eo = topo.engines(core, T.cores[off[0]])
    en = [e for e in topo.engines(core, T.cores[on]) if e not in eo][:NON]
    if kind == "X":
        h, w = halves(T, topo, rank), len(eo) // 2
        return [[(d, en if d == on else eo[w * i:w * i + w]) for i, d in enumerate(h[a:b])] for a, b in (((0, 2), (2, 4), (4, 6), (6, 7)) if SWAP else ((0, 2), (2, 3), (3, 5), (5, 7)))]
    if kind == "P":
        return [[(off[0], eo[0:2]), (off[1], eo[2:4])] + [(d, [eo[4 + i]]) for i, d in enumerate(off[2:])] + [(on, en[:1])]]
    return [[(d, [eo[i]]) for i, d in enumerate(off)] + [(on, en[:1])]]


def rank_program(g, core, T, topo):
    rank = T.rank_of(core)
    if rank is None:
        return
    Q = {"v": g.vector, "a": g.scalar, "p": g.tensor, "g": g, "s": g.sync}
    QS = {"v": "vq", "a": "aq", "p": "pq", "g": "gq"}
    total, last, readers = {}, {}, {}
    known = {q: {} for q in Q}

    def wait(q, tok):
        sem, val, know = tok
        if val is None:
            val = total[sem]
        if known[q].get(sem, 0) >= val:
            return
        Q[q].wait_ge(T.sem[sem], int(val))
        known[q][sem] = val
        for s, v in know.items():
            if known[q].get(s, 0) < v:
                known[q][s] = v

    def deps(q, rd, wr):
        own = QS.get(q)
        for k in rd:
            if k in last:
                wait(q, last[k])
        for k in wr:
            for tok in readers.get(k, []) + ([last[k]] if k in last else []):
                if tok[0] != own:
                    wait(q, tok)

    def mark(tok, rd, wr):
        for k in rd:
            readers.setdefault(k, []).append(tok)
        for k in wr:
            last[k] = tok
            readers[k] = []

    def op(q, name, args, rd, wr, **kw):
        deps(q, rd, wr)
        o = Q[q]
        fn = {"copy": lambda: o.tensor_copy(*args), "tt": lambda: o.tensor_tensor(*args), "ts": lambda: o.tensor_scalar(*args),
              "memset": lambda: o.memset(*args), "scan": lambda: o.tensor_tensor_scan(*args),
              "act": lambda: o.activation(*args, **kw), "iota": lambda: o.iota(*args, **kw), "asel": lambda: o.affine_select(*args)}[name]
        s = QS[q]
        fn().then_inc(T.sem[s], 1)
        total[s] = total.get(s, 0) + 1
        mark((s, total[s], dict(known[q])), rd, wr)

    def mms(calls, rd, wr):
        deps("p", rd, wr)
        for i, a in enumerate(calls):
            ins = g.tensor.matmul(*a) if len(a) == 5 else g.tensor.transpose(*a)
            if i == len(calls) - 1:
                ins.then_inc(T.sem.pq, 1)
        total["pq"] = total.get("pq", 0) + 1
        mark(("pq", total["pq"], dict(known["p"])), rd, wr)

    def dma(q, out, in_, sem, rd, wr):
        deps(q, rd, wr)
        Q[q].dma_start(out, in_).then_inc(T.sem[sem], 16)
        total[sem] = total.get(sem, 0) + 16
        mark((sem, None, dict(known[q])), rd, wr)

    def send(call, src, dst, arr, loc, rd):
        deps("g", rd, [])
        tr = []
        for d, es in call:
            rid, pid, _ = topo.addr(T.cores[d])
            tr.append(RemoteDMATransfer(dst_ids=[DstId(rid=rid, pnc=pid)], dma_engine_mask=sum(1 << e for e in es),
                                        remote_sem=T.sem[arr], srcs=[src(d)], dsts=[dst]))
            total[loc] = total.get(loc, 0) + len(es)
        g.remote_dma_fused(tr, local_sem=T.sem[loc])

    e0, e1 = (1 - rank // 4, rank // 4) if SWAP else (rank // 4, 1 - rank // 4)
    for kind, k, arr, src in (("P", "PL", "arrP", range(8)), ("S", "SL", "arrS", range(8)), ("F", "FL", "arrF", range(8)),
                              ("X", "LR%d" % e0, "arrE", range(4 * e0, 4 * e0 + 4)), ("X", "LR%d" % e1, "arrL", range(4 * e1, 4 * e1 + 4))):
        total[arr] = sum(len(es) for r in src if r != rank for call in plan(T, topo, r, kind) for d, es in call if d == rank)
        last[k] = (arr, total[arr], {})
    V = lambda name, args, rd, wr: op("v", name, args, rd, wr)
    S = lambda name, args, rd, wr, **kw: op("a", name, args, rd, wr, **kw)
    G = lambda name, args, rd, wr, **kw: op("g", name, args, rd, wr, **kw)
    PS = (T.PS0, T.PS1)
    col = lambda j: T.KF[:, j:j + 1]

    def cp(q, out, in_, rd, wr):
        if q == "v":
            V("copy", (out, in_), rd, wr)
        else:
            S("act", (out, in_, AF.Copy), rd, wr)

    def fill(out, n, x, wr):
        S("act", (out, T.ONE1[:, 0:n], AF.Copy), ["ONE1"], wr, scale=float(x))

    order = halves(T, topo, rank) + [rank]
    stage = [lambda: dma("s", T.PP[:], T.pats[:], "dp", [], ["PP"]), lambda: dma("s", T.SS[:], T.starts[:], "ds", [], ["SS"])]
    stage[0]()
    stage[1]()
    for n, s in enumerate(order):
        dma(LQ[n], T.D32[:, 256 * n:256 * n + 256], T.bwt[s:s + 1, :], "b%d" % n, [], ["D32%d" % n])
    dma("s", T.PL[rank], T.pats[16 * rank:16 * rank + 16, :], "dsp", [], ["PLs"])
    dma("s", T.SL[rank], T.starts[16 * rank:16 * rank + 16, :], "dss", [], ["SLs"])

    fl = dict(allow_small_or_imprecise_dtypes=True)
    V("memset", (T.ONE1[:], 1.0), [], ["ONE1"])
    V("memset", (T.DPI[:, 0:8], -1.0), [], ["DPI0"])
    V("memset", (T.DPI[:, 8:16], 1.0), [], ["DPI1"])
    G("iota", (T.KI[:, 0:1], [[0, 1]], 0, 1), [], ["KI0"])
    G("asel", (T.ID[:], T.ONE1[:], [[-1, 128]], A.is_equal, 0.0, 0, 1), ["ONE1"], ["ID"])
    G("asel", (T.DP[:], T.DPI[:], [[15, 2], [16, 8]], A.is_ge, 0.0, -1, -1), ["DPI0", "DPI1"], ["DP"])
    G("iota", (T.MC[:, 0:16], [[16, 8], [0, 2]], -241, 0), [], ["MC0"], **fl)
    V("memset", (T.M[:, 0:60], 0.0), [], ["M"])
    V("memset", (T.MC[:, 16:64], -256.0), [], ["MC1"])
    V("memset", (T.MC[:, 64:66], 128.0), [], ["MC1"])
    for i in range(1, 4):
        fill(T.TB[:, 3, :, i, :], 128, -102400, ["TB3"])
    for d, n, sh in ((1, 3, 0), (2, 15, 0), (3, 31, 2), (4, 3, 1), (5, 3, 3), (6, 3, 5)):
        V("ts", (T.KI[:, d:d + 1], T.KI[:, 0:1], sh, n, A.arith_shift_right, A.bitwise_and), ["KI0"], ["KI"])
    V("copy", (T.KF[:, 1:7], T.KI[:, 1:7]), ["KI"], ["KF"])
    for c in range(4):
        V("ts", (T.M[:, 8 * c:8 * c + 8], T.ID[:, :, c, 0], 128.0, None, A.mult), ["ID", "M"], ["M0"])
    for j in range(4):
        for h in range(2):
            args = (T.M[32 * j:32 * j + 32, 36 + h:60:2], T.ID[32 * j:32 * j + 32, 2 * j + h, :, 1:4])
            if 2 * j + h < MS:
                S("act", args + (AF.Copy,), ["ID", "M"], ["MS"], scale=float(4 ** j))
            else:
                V("ts", args + (float(4 ** j), None, A.mult), ["ID"], ["M0"])
    S("act", (T.KB[:, 0:1], col(4), AF.Exp), ["KF"], ["KB0"], scale=-math.log(64.0), bias=math.log(64.0))
    for t in (1, 2):
        V("copy", (T.M[:, 60 * t:60 * t + 60], T.M[:, 0:60]), ["M0", "MS"], ["M%d" % t])

    def matrices():
        V("memset", (T.M[:, 32:180:61], -1.0), ["M1", "M2"], ["Mt"])
        V("memset", (T.M[:, 33:180:61], 1.0), [], ["Mt"])
        for t in (2, 1, 0):
            o = 68 * t
            V("tt", (T.M[:, o:o + 16], T.M[:, o:o + 16], T.DP[:], A.add), ["M%d" % t, "DP"], ["M%d" % t])

    if MFIN < 0:
        matrices()
    G("iota", (T.RI[:], [[1, 16], [0, 4]], 0, 0), [], ["RI"], **fl)
    G("iota", (T.CI[:], [[0, 16], [128, 4]], -256, 0), [], ["CI"], **fl)
    G("iota", (T.CQ[:], [[4, 8], [1, 4]], 0, 0), [], ["CQ"], **fl)
    queries = [lambda: send(plan(T, topo, rank, "P")[0], lambda d: T.PP[d], T.PL[rank], "arrP", "locP", ["PP"]),
               lambda: send(plan(T, topo, rank, "S")[0], lambda d: T.SS[d], T.SL[rank], "arrS", "locS", ["SS"])]
    queries[0]()
    queries[1]()
    G("iota", (T.VA[:], [[1, 4], [0, 4]], 0, 0), [], ["VA"], **fl)
    G("iota", (T.VB[:], [[0, 4], [1, 4]], -60, 0), [], ["VB"], **fl)
    for y in range(2):
        G("iota", (T.UI[:, 32 * y:32 * y + 32], [[4 - 4 * y, 2], [1, 4], [4, 4]], 4 * y - 4, 0), [], ["UI"], **fl)
    G("asel", (T.PERM[:], T.ONE1[:], [[-1, 64], [-64, 2]], A.is_equal, 0.0, 0, 1), ["ONE1"], ["PERM"])
    tri = lambda t: G("asel", (T.TRI[64 * t:64 * t + 64, :], T.ONE1[64 * t:64 * t + 64, :], [[1, 2], [2, 64]], A.is_ge, 0.0, -1 - t, -2), ["PERM", "ONE2"], ["TRI"])
    tri(0)

    half = lambda n, t: T.D[:, 256 * n + 128 * t:256 * n + 128 * t + 128]
    mb = lambda n: 2 + n % 2 if NB == 2 else (2 + n) % 4
    mixed = lambda n, t, F: [(T.PSA[:, 512 * mb(n) + h:512 * mb(n) + RW:2], F[:, 256 * n + 128 * h:256 * n + 128 * h + 128], T.M[:, 60 * t:60 * t + 60],
                              t == 2 and h == 0, t == 1 and h == 1) for h in range(2)]
    sends = plan(T, topo, rank, "X")

    def convert(n):
        V("copy", (T.D[:, 256 * n:256 * n + 256], T.D32[:, 256 * n:256 * n + 256]), ["D32%d" % n], ["D%d" % n])
        if n == MFIN:
            matrices()

    def turn_v(n):
        mms([(T.PV[:, 4 * (n % 2), :, t, :], half(n, t), T.ID[:]) for t in range(2)], ["D%d" % n, "ID"], ["PV%d" % (n % 2)])

    def turn_a(n):
        mms([(PS[n % 2][:, 128 * h + 64 * t:128 * h + 64 * t + 64], half(n, t), T.ID[:, 4 * h:4 * h + 4], True, True) for t in range(2) for h in range(2)], ["D%d" % n, "ID"], ["P%d" % (n % 2)])

    def feature_a(n):
        S("act", (T.G3[:, 256 * n:256 * n + 256], PS[n % 2][:, 0:256], AF.Relu), ["P%d" % (n % 2)], ["P%d" % (n % 2), "G3%d" % n], bias=-2.0)

    def feature_v(n):
        for t, F in ((1, T.G1), (2, T.G2)):
            V("ts", (F[:, 256 * n:256 * n + 256], T.PV[:, 4 * (n % 2)], float(t), None, A.is_ge), ["PV%d" % (n % 2)] * (t == 1), ["PV%d" % (n % 2), "G%d%d" % (t, n)])

    def mix_a(n):
        mms(mixed(n, 2, T.G3) + [(T.PSA[:, 512 * mb(n):512 * mb(n) + 66], T.ONE1[0:1, :], T.MC[0:1, :], False, False)],
            ["G3%d" % n, "M2", "Mt", "MC0", "MC1", "ONE1"], ["A%d" % mb(n)])

    def mix_v(n):
        mms(mixed(n, 0, T.G1) + mixed(n, 1, T.G2), ["G1%d" % n, "G2%d" % n, "M0", "M1"], ["A%d" % mb(n)])

    def leave(n):
        d, o, pk = order[n], 512 * mb(n), "A%d" % mb(n)
        out, k = (T.SEND, "SX%d" % d) if d != rank else (T.LR, "LRs")
        for h in range(2):
            cp("a", out[:, d, :, h, :], T.PSA[:, o + h:o + RW:2], [pk] * (h == 0), [pk, k])
        for call in sends:
            if call[-1][0] == d:
                send(call, lambda d: T.SEND[:, d], T.LR[:, rank], "arrE" if d // 4 == e0 else "arrL", "locX", ["SX%d" % d for d, _ in call])
        if n == 2:
            G("iota", (T.ONE2[:], [[0, 256]], 1, 0), [], ["ONE2"], **fl)
        if n == 4:
            tri(1)

    def filler(n):
        if 2 <= n < 6:
            fill(T.TB[:, n - 2, :, 0, :], 128, -81920, ["TBU"])
        if n == 6:
            fill(T.AD[:, :, 0, :], 64, 224, ["AD0"])

    calls = {"c": convert, "t": turn_v, "u": turn_a, "r": feature_a, "f": feature_v, "m": mix_a, "n": mix_v, "k": leave, "x": filler}
    todo = [(x[0], n + int(x[1])) for n in range(-4, 8) for x in PIECE.split() if 0 <= n + int(x[1]) < 8]
    if C7:
        todo.remove(("c", 7))
        todo.insert(todo.index(("f", C7)) + 1, ("c", 7))
        for x in "urt":
            if todo.index((x, 7)) < todo.index(("c", 7)):
                todo.remove((x, 7))
                todo.insert(todo.index(("f", C7 + 1)), (x, 7))
    for x, n in todo:
        calls[x](n)

    for a, b, w in ((32, 80, 16), (0, 32, 32)):
        G("asel", (T.RS[:, a:b], T.ONE1[:, a:b], [[0, (b - a) // w], [1, w]], A.is_gt, 0.0, 0, 0), ["TRI"], ["RS"])
    G("iota", (T.UC[:], [[0, 8], [1, 4]], 0, 0), [], ["UC"], **fl)
    for h in range(2):
        for k in (2, 0):
            G("asel", (T.SEL[:, h, k:k + 2], T.ONE2[:], [[-32, 2], [0, 8], [-2, 16]], A.is_equal, 0.0, -h - 32 * k, 1), ["ONE2"], ["SEL%d" % h])
    G("iota", (T.FOUR[:], [[252, 2], [0, 32]], 4, 0), [], ["FOUR"], **fl)
    G("asel", (T.GA[:], T.FOUR[:], [[0, 2], [-16, 8], [0, 4]], A.is_ge, 0.0, 0, 1), ["FOUR"], ["GA"])
    G("asel", (T.GB[:], T.GA[:], [[0, 2], [16, 8], [0, 4]], A.is_ge, 0.0, 14, -1), ["GA"], ["GB"])
    G("asel", (T.RST[:], T.ONE1[:, 0:64], [[0, 16], [1, 4]], A.is_gt, 0.0, 0, 0), ["ONE1"], ["RST"])
    for p0, x, y in ((0, 0xC20000, 0x60000), (32, 0xD600, 0x80), (64, 0xFC, 0x100)):
        for o, z in ((0, x), (32, y)):
            G("iota", (T.CON[p0:p0 + 32, o:o + 32], [[0, 32]], z, 0), ["RST", "CON"], ["CON"], **fl)
    S("act", (col(0), col(1), AF.Relu), ["KF"], ["K0"], bias=-1.0)
    S("act", (T.NID[:], T.ID[:], AF.Copy), ["ID"], ["NID"], scale=-1.0)
    vc = [lambda: V("ts", (T.W0[:], T.RI[:], col(2), 128.0, A.is_gt, A.mult), ["RI", "KF"], ["W0"]),
          lambda: V("ts", (col(9), col(5), 4.0, col(6), A.mult, A.add), ["KF"], ["K9"]),
          lambda: V("ts", (col(12), col(5), 4.0, None, A.mult), ["KF"], ["K12"]),
          lambda: V("ts", (T.KB[:, 2:3], col(4), 1.0, 32.0, A.is_equal, A.mult), ["KF"], ["KB2"]),
          lambda: V("ts", (T.EQ[:], T.CQ[:], col(3), None, A.is_equal), ["CQ", "KF"], ["EQ"]),
          lambda: V("tt", (T.W[:, 0:64], T.W0[:], T.CI[:], A.add), ["W0", "CI"], ["W"]),
          lambda: V("ts", (col(7), col(1), 2.0, 256.0, A.is_lt, A.mult), ["KF"], ["K7"]),
          lambda: V("ts", (T.MASK[:, 0:32], T.UI[:, 0:32], col(12), None, A.is_lt), ["UI", "K12"], ["PN"]),
          lambda: V("ts", (T.MS[:, 0:32], T.UI[:, 32:64], col(9), None, A.is_lt), ["UI", "K9"], ["MS"]),
          lambda: V("ts", (col(11), col(4), 3.0, -64.0, A.not_equal, A.mult), ["KF"], ["K11"]),
          lambda: V("ts", (T.L0[:], T.VA[:], col(2), -BIG, A.not_equal, A.mult), ["VA", "KF"], ["L0"]),
          lambda: V("tt", (T.MASK[:, 64:80], T.MASK[:, 0:16], T.MASK[:, 16:32], A.subtract), ["PN"], ["MASK"]),
          lambda: V("tt", (T.MASK[:, 32:64], T.MS[:, 0:32], T.MASK[:, 0:32], A.subtract), ["PN", "MS"], ["MASK", "MT"]),
          lambda: V("ts", (col(8), col(4), 0.0, -17.0, A.is_equal, A.mult), ["KF"], ["K8"]),
          lambda: V("tt", (T.LW[:], T.L0[:], T.VB[:], A.add), ["L0", "VB"], ["LW"])]
    for f in vc[:NPRE]:
        f()

    wide = lambda w: cp("a", T.W[:, w:2 * w], T.W[:, 0:w], ["W"], ["W"])
    S("act", (col(10), col(0), AF.Exp), ["K0"], ["K10"], scale=math.log(64.0), bias=math.log(4.0))
    S("act", (T.KB[:, 1:2], col(4), AF.Exp), ["KF"], ["KB1"], scale=math.log(64.0), bias=-math.log(128.0))
    wide(64)
    S("act", (T.SELY[:, 0:32], T.EQ[:], AF.Copy), ["EQ", "K10"], ["SELY0"], scale=col(10))
    S("act", (T.SELY[:, 32:64], T.EQ[:], AF.Copy), ["EQ", "K7"], ["SELY1"], scale=col(7))
    wide(128)
    for h in range(2):
        S("act", (T.SELQ[:, 32 * h:32 * h + 32], T.ID[:, :, 0, :], AF.Copy), ["ID"], ["SELQ%d" % h], scale=64.0 ** h)

    def selectors():
        wide(256)
        S("act", (T.SELZ[:], T.SELY[:], AF.Copy), ["SELY0", "SELY1"], ["SELZ"], scale=-1.0)
        wide(512)
        cp("a", T.W[:, 1024:1344], T.W[:, 0:320], [], ["W2"])

    fetch = [lambda: dma("s", T.PT[:], T.PL[:], "lpt", ["PL", "PLs"], ["PT"]), lambda: dma("s", T.ST[:], T.SL[:], "lst", ["SL", "SLs"], ["ST"])]
    fetch[PLAST]()
    fetch[1 - PLAST]()

    def pairs():
        return [lambda: V("ts", (T.P4[:], T.PT[:, :, 0, :], 4.0, None, A.mult), ["PT"], ["P4"]),
                lambda: V("tt", (T.PI[:], T.P4[:], T.PT[:, :, 1, :], A.add), ["P4", "PT"], ["PI"]),
                lambda: V("copy", (T.OFP[:], T.PI[:]), ["PI"], ["OFP"])]

    def spread(u):
        S("act", (T.LTR[:, 128 * u:128 * u + 128], T.LW[:, 0:16].indirect(T.OFP[:, 8 * u:8 * u + 8]), AF.Copy), ["LW", "OFP"], ["LTR%d" % u])

    def odd():
        return ([lambda: V("ts", (T.NX[:], T.PT[:, :, 1, :], BIG, None, A.mult), ["PT"], ["NX"]),
                 lambda: V("tt", (T.NX[:, 0:48], T.NX[:, 0:48], T.PT[:, 1:4, 0, :], A.subtract), ["NX", "PT"], ["NX"])] +
                [lambda h=h, c=c: S("act", (T.QTB[:, :, h, :, c], T.NX[:], AF.Abs), ["NX"], ["QTB"], scale=64.0 ** h, bias=64.0 ** h * (60 - BIG * c))
                 for h in range(2) for c in range(4)])

    def starts():
        OK = ["O:%d" % u for u in range(4)]
        return ([lambda: V("ts", (T.ST4[:], T.ST[:], 4.0, None, A.mult), ["ST"], ["ST4"]),
                 lambda: V("ts", (T.O[:, :, 0:8], T.ST[:], 1.0 / 16, -0.5 + 0.5 / 16, A.mult, A.add), ["ST"], OK)] +
                [lambda h=h: V("tt", (T.I[:, 16 * h:16 * h + 16], T.ST4[:, 16 * h:16 * h + 16], T.PT[:, 0, 0, :], A.add), ["ST4", "PT"], ["I"]) for h in range(2)] +
                [lambda: V("ts", (T.J[:], T.I[:], 63, None, A.bitwise_and), ["I"], ["J"]),
                 lambda: V("copy", (T.O[:, :, 8:16], T.J[:]), ["J"], ["OW"])])

    small = {"p": pairs(), "q": odd(), "s": starts(), "x": [lambda u=u: spread(u) for u in range(NSP)]}

    def smalls(at):
        for x in SMALL.get(at, "").split():
            small[x[0]][int(x[1])]()

    turns = TURNS.split()
    bk = lambda e, b: 2 * (e != e0) + b
    LK = lambda e: ["LR%d" % e] + ["LRs"] * (e == rank // 4)

    def turned(e, n):
        x, j = turns[n], int(turns[n][1])
        for b in range(2):
            js = (2 * j, 2 * j + 1) if x[0] == "D" else (j,)
            src = lambda y: T.AD[:, 16 * e:16 * e + 16] if x[0] == "D" else T["T" + x[0]][:, y, 16 * e:16 * e + 16, :, b:4:2]
            mms([(T.PSA[:, 512 * bk(e, b) + y:512 * bk(e, b) + 512:4], src(y), T.PERM[:], n == 0, n == len(turns) - 1 and y == js[-1]) for y in js],
                {"A": ["TU%d%d" % (j, e), "T%s%d" % (x, e)], "B": ["TBU", "TB3" if j == 3 else "T%s%d" % (x, e)], "D": ["AD0", "AD%d" % (e + 1)]}[x[0]] + ["PERM"], ["A%d" % bk(e, b)])

    def before(e):
        tot = lambda h: T.LR[:, 4 * e:4 * e + 4, 16:18, h, :]
        out = lambda h: T.PS0[:, h:32:2]
        mms([(out(0), T.TRI[:], tot(0), True, False), (out(1), T.ONE1[:], tot(0), False, False), (out(1), T.TRI[:], tot(1), False, True)],
            LK(e) + ["TRI", "ONE1"], ["P0"])

    def plane(e, x):
        j = int(x[2])
        if x[1] == "U":
            cp(x[0], T.TA[:, j, 16 * e:16 * e + 16, 0, :], T.LR[:, 4 * e:4 * e + 4, j:16:4], LK(e), ["TU%d%d" % (j, e)])
            return
        k = j + (x[1] == "B")
        add = TOFF[k] + (((160.0 if j else 0.0) if x[1] == "A" else (800.0 if j else 640.0)) * 4 ** j)
        sc = (128.0 if x[1] == "A" else -128.0) / 4 ** j
        args, wr = (T["T" + x[1]][:, j, 16 * e:16 * e + 16, 1:4, :], T.LR[:, 4 * e:4 * e + 4, 18:30]), ["T%s%d" % (x[1:], e)]
        if x[0] == "v":
            V("ts", args + (add, sc, A.add, A.mult), LK(e), wr)
        else:
            S("act", args + (AF.Copy,), LK(e), wr, scale=sc, bias=sc * add)

    def digits(e):
        ni = T.NI[:, 32 * e:32 * e + 32]
        return ([lambda: V("copy", (ni, T.PS0[:, 0:32]), ["P0"], ["P0", "NI%d" % e])] +
                [lambda i=i: V("ts", (T.DI[:, 16 * e:16 * e + 16, i, :], ni, 6 * i, 63, A.arith_shift_right, A.bitwise_and), ["NI%d" % e], ["DI%d" % e]) for i in range(3)] +
                [lambda: V("copy", (T.AD[:, 16 * e:16 * e + 16, 1:4, :], T.DI[:, 16 * e:16 * e + 16]), ["DI%d" % e], ["AD%d" % (e + 1)])])

    def out_of(e, b, q):
        k, bias = "A%d" % bk(e, b), T.BX[:, 9:10] if e == e0 else T.BX[:, 5 + e:6 + e]
        args, rd, wr = (T.XC[:, 1024 * e + b:1024 * e + 1024:2], T.PSA[:, 512 * bk(e, b):512 * bk(e, b) + 512]), [k, "BX2%d" % e], [k, "XC%d%d" % (e, b)]
        if q == "v":
            V("ts", args + (bias, None, A.add), rd, wr)
        else:
            S("act", args + (AF.Identity,), rd, wr, bias=bias)

    def counts(e, parts, m0, i0, o0):
        w = sum(b - a for a, b in parts) * 4
        n = 1 if w == 16 else 4
        mms([(T.PS1[:, 4 * sum(y - x for x, y in parts[:j]):4 * sum(y - x for x, y in parts[:j + 1])], T.ONE1[:], T.LR[:, a:b, 16:18, h, :], j + h == 0, j + h == len(parts))
             for j, (a, b) in enumerate(parts) for h in range(2)], LK(e0) + LK(e) + ["ONE1"], ["P1"])
        mt, k = T.MT[:, w + 15 - 16 * n:w:16], lambda x: x + str(e)
        return [lambda: V("tt", (T.MS[:, 0:w], T.PS1[:, 0:w], T.MASK[:, m0:m0 + w], A.mult), ["P1", "MASK", "MT"], ["P1", "MS"]),
                lambda: V("scan", (T.MT[:, 0:w], T.RS[:, 80 - w:80], T.MS[:, 0:w], 0.0, A.mult, A.add), ["MS", "RS", "BI"], ["MT"]),
                lambda: V("ts", (T.BI[:, i0 + n:i0 + 2 * n], mt, T.KB[:, 0:1], 1.0 / 64, A.mult, A.mult), ["MT", "KB0"], [k("BI1")]),
                lambda: V("ts", (T.BI[:, i0:i0 + n], mt, T.KB[:, 0:1], None, A.mult), ["MT", "KB0"], [k("BI0"), "BI"]),
                lambda: V("ts", (T.BX[:, o0:o0 + n], T.BI[:, i0 + n:i0 + 2 * n], col(11), 81696.0, A.mult, A.add), [k("BI1"), "K11"], [k("BX1")]),
                lambda: V("tt", (T.BX[:, o0 + n:o0 + 2 * n], T.BI[:, i0:i0 + n], T.BX[:, o0:o0 + n], A.add), [k("BI0"), k("BX1")], [k("BX2")])]

    def build(e, order, bias):
        dg = digits(e)
        for f in order.split():
            if f[1] == "X":
                out_of(e0, int(f[2]), f[0])
            else:
                plane(e, f) if len(f) == 3 else {"b": bias, "d": dg}[f[0]][int(f[1])]()

    turned(e0, 0)
    before(e0)
    build(e0, EARLY, counts(e0, [(4 * e0, 4 * e0 + 4)], 32 + 16 * e0, 8, 8))
    for n in range(1, len(turns)):
        turned(e0, n)
    turned(e1, 0)
    for f in vc[NPRE:]:
        f()
    selectors()
    smalls("early")
    before(e1)
    build(e1, LATE, counts(e1, [(0, 8), (0, 8), (4, 8)], 0, 0, 0))
    XK = []

    def copies(e, quarters):
        for k in range(-(-quarters // 4)):
            for y in range(8):
                c0, w = 2048 * (4 * e + k), min(512 * (quarters - 4 * k), 2048)
                dma("s", T.X[16 * y:16 * y + 16, c0:c0 + w], T.XC[32 * k:32 * k + 32:1 + (w < 2048), 1024 * e:1024 * e + min(w, 1024)], "rep", ["XC%d0" % e, "XC%d1" % e], ["XD%d%d%d" % (e, k, y)])
                XK.append("XD%d%d%d" % (e, k, y))

    copies(e0, NDMA[0])
    for n in range(1, len(turns)):
        turned(e1, n)
    V("ts", (T.XE[:, 0:1], T.BX[:, 7:8], col(8), -81536.0, A.add, A.add), ["BX2%d" % e1, "K8"], ["XE"])
    small["k"] = ([lambda h=h: V("ts", (T.BX[:, 10 + h:11 + h], T.BX[:, 4:5], -81696.0, T.KB[:, 1 + h:2 + h], A.add, A.mult), ["BX2%d" % e1, "KB1", "KB2"], ["DW%d" % h]) for h in range(2)] +
                  [lambda h=h: V("ts", (T.MID[:, 32 * h:32 * h + 32], T.UC[:], col(5), T.BX[:, 10 + h:11 + h], A.is_equal, A.mult), ["DW%d" % h, "UC"], ["MID"]) for h in range(2)])
    smalls("last")
    for b in range(2):
        out_of(e1, b, "av"[b])
    copies(e1, NDMA[1])

    ring = [(PS[b], 0, "P%d" % b) for b in range(2)] + [(T.PSA, 512 * b, "A%d" % b) for b in range(4)]
    mine = [(e, n // 4, n // 2 % 2, 512 * (n % 2), 512) for e, a in zip((e0, e1), NDMA) for n in range(a, 16)]
    if XH:
        x = mine.pop()
        mine += [x[:3] + (512, XH), x[:3] + (512 + XH, 512 - XH)]
    for n in range(-1, len(mine)):
        ps, o, pk = ring[(n + 1) % 6]
        e, k, h, c0, w = mine[n] if n >= 0 else (0, 0, 0, 0, 1)
        src, rd = (T.XC[:, 1024 * e + c0:1024 * e + c0 + w], ["XC%d0" % e, "XC%d1" % e]) if n >= 0 else (T.XE[:, 0:1], ["XE"])
        x0 = 2048 * (4 * e + k) + 1024 * h + c0 if n >= 0 else 16384
        q = XQ[n + 1]
        mms([(ps[:, o:o + w], T.SEL[:, h, k], src, True, True)], rd + ["SEL%d" % h], [pk])
        cp(q, T.X[:, x0:x0 + w], ps[:, o:o + w], [pk], [pk, "X%d" % n])
        XK.append("X%d" % n)
        smalls(n)

    key = lambda name, n: "%s:%d" % (name, n % 4)
    tile = lambda name, n: T[name][:, 128 * (n % 4):128 * (n % 4) + 128]
    bank = lambda n: T.PSA[:, 512 * (n % 4):512 * (n % 4) + 64]
    st = lambda n, a, b, s: T.SC[:, 64 * (n % 4) + a:64 * (n % 4) + b:s]

    def pick(n):
        V("scan", (st(n, 0, 64, 1), T.RST[:], bank(n), 0.0, A.mult, A.max), ["A%d" % (n % 4), "RST"], ["A%d" % (n % 4), key("S", n)])

    def offsets(n):
        if n >= 32:
            V("ts", (T.RES[:, 8 * (n % 4):8 * (n % 4) + 8], st(n, 3, 32, 4), 0.25, None, A.mult), [key("S", n)], ["RES%d" % (n % 4)])
        else:
            V("ts", (T.O[:, n % 4, :], st(n, 3, 64, 4), 1.0 / 64, -0.5 + 0.5 / 64, A.mult, A.add), [key("S", n)], [key("O", n)])

    def block(n):
        S("act", (tile("Z", n), T.X[:, 0:16385].indirect(T.O[:, n % 4, 0:8]), AF.Copy), [key("O", n)] + XK, [key("Z", n)])

    def opened(n):
        mms([(bank(n), T.ONE1[0:96, :], T.CON[0:96, :], True, False)], ["ONE1", "CON"], ["A%d" % (n % 4)])

    def letters(n, q):
        if q == "v":
            V("ts", (tile("ZL", n), tile("Z", n), 24512.5, None, A.add), [key("Z", n)], [key("ZL", n)])
        else:
            S("act", (tile("ZL", n), tile("Z", n), AF.Copy), [key("Z", n)], [key("ZL", n)], bias=24512.5)

    def compare(n):
        V("tt", (tile("E", n), T.W[:, 0:1344].indirect(T.O[:, n % 4, 8:16]), tile("Z", n), A.is_gt), [key("O", n), "OW", "W", "W2", key("Z", n)], [key("E", n)])

    def sums(n):
        t, k = n // 4, n % 2
        nxt = (T.NID[:], T.QTB[:, t // 2, :, 8 * k:8 * k + 8, :]) if t % 2 else (T.LTR[:, 128 * (t + k):128 * (t + k) + 128], T.SELQ[:])
        mms([(bank(n),) + x + (False, False) for x in ((tile("ZL", n), T.SELZ[:]), nxt, (T.ONE1[:], T.MID[:]), (tile("Z", n), T.SELY[:]))],
            [key("Z", n), key("ZL", n), "MID", "NID", "SELY0", "SELY1", "SELZ", "SELQ0", "SELQ1", "QTB" if t % 2 else "LTR%d" % (t + k)], ["A%d" % (n % 4)])

    def closed(n):
        mms([(bank(n), tile("E", n), T.GB[:], False, True)], [key("E", n), "GB"], ["A%d" % (n % 4)])

    calls = {"s": pick, "o": offsets, "z": block, "a": opened, "v": lambda n: letters(n, "v"), "l": lambda n: letters(n, "a"), "e": compare,
             "b": sums, "c": closed, "x": lambda n: spread(NSP - 1 + n // 4)}
    for t in range(-2, 9):
        for x in STEP.split():
            n = 4 * t + int(x[1])
            if (4 <= n < 36 if x[0] in "so" else 4 <= n < 36 - 4 * NSP if x[0] == "x" else 0 <= n < 32):
                calls[x[0]](n)
                smalls(x[0] + str(n))
    dma("s", T.RD[:], T.RES[:], "rd", ["RES0", "RES1", "RES2", "RES3"], ["RD"])
    send(plan(T, topo, rank, "F")[0], lambda d: T.RD[d], T.FL[rank], "arrF", "locF", ["RD"])
    r0, r1 = 16 * rank, 16 * rank + 16
    dma("s", T.y[r0:r1, :], T.RES[r0:r1, :], "yself", ["RES0", "RES1", "RES2", "RES3"], ["y0"])
    if rank > 0:
        dma("s", T.y[0:r0, :], T.FL[0:rank], "yout", ["FL"], ["y1"])
    if rank < 7:
        dma("s", T.y[r1:128, :], T.FL[rank + 1:8], "yout", ["FL"], ["y2"])
    for sem in sorted(total):
        wait("g", (sem, total[sem], {}))
